import numpy as np, ml_dtypes
CORES = [2,3,42,43,82,83,122,123]
N = 8
BF = ml_dtypes.bfloat16
def gentries(a):
    return np.ascontiguousarray(a.reshape(8, 16, -1).transpose(0, 2, 1)).reshape(8, -1)
def gtable(e):
    e = np.asarray(e); return np.ascontiguousarray(e.reshape(8, -1, 16).transpose(0, 2, 1)).reshape(128, -1).astype(np.int32)
W, K, E, X, S, RO = 8192, 3072, 128, 3, 3, 2
ANY = np.arange(256); LEN = np.arange(1, 13)
def place(u1, u2, m):
    return ((((u1 & 4095) * (u2 & 4095)) >> 5) + u2 + 97 * m) & (W - 1)
def hashes(st, m, wt):
    u = np.where(np.arange(12) < m[:, None], st, 0) @ wt
    return place(u[:, 0], u[:, 1], m)
def ropes(rng, shape, lens):
    n = np.minimum(rng.integers(0, 8, shape), 4)
    return np.where(np.arange(4) < n[..., None], lens[rng.integers(0, len(lens), shape + (4,))], 0)
def fill(rng):
    return np.concatenate([rng.integers(0, 256, (N, 8, 12, W)), np.moveaxis(ropes(rng, (N, 8, W), LEN), 3, 2)], axis=2)
def pool(rng, M, vals):
    st = vals[rng.integers(0, len(vals), (M, 12))]; h = max(M // 8, 1); keep = rng.integers(0, 13, M); keep[:h] = 0
    return np.where(np.arange(12) < keep[:, None], st[rng.integers(0, h, M)], st)
def plant(T, st, m, ro, wt):
    h = hashes(st, m, wt); T[:, h] = np.concatenate([st.T, ro.T])
def asks(rng, st, vals, lens):
    x = st[rng.integers(0, len(st), K)]; cut = np.where(rng.random(K) < 0.3, rng.integers(0, 13, K), 12)
    x = np.where(np.arange(12) < cut[:, None], x, vals[rng.integers(0, len(vals), (K, 12))])
    return np.concatenate([x.T, ropes(rng, (K,), lens).T])
def parts(rng, wt, M, n, vals, lens):
    P = fill(rng); q = np.zeros((N, 8, 16, K), np.int64)
    for g in range(8):
        st = pool(rng, int(M[g]), vals)
        for a in range(N):
            plant(P[a, g], st[rng.integers(0, len(st), n)], lens[rng.integers(0, len(lens), n)], ropes(rng, (n,), lens), wt[a, g])
            q[a, g] = asks(rng, st, vals, lens)
    return P, q
def alike_ropes(n, l):
    return np.tile(np.array((tuple(l) + (0, 0, 0, 0))[:4]), (n, 1))
def steer(rng, c):
    v = ((np.diff(c, axis=1, prepend=0) - 194) & (W - 1)) + W * rng.integers(0, 65280 // W, c.shape)
    return np.stack([v % 255, v // 255], axis=2).reshape(len(c), 12)
def meetings(rng, ends):
    n = 6; F = 2 + 2 * S; cut = 2 + n * np.arange(7); four = (6, 8, 10, 12)
    c = 1 + rng.permutation(W - 2)[:(2 + 7 * n) * 6].reshape(-1, 6)
    d, s1, e1, q2, s3, o3, q4, s5 = np.split(c, cut)
    for i in range(2): d[i, ends[i][0]] = ends[i][1]
    s1[:, 1] = s1[:, 0]; e1[:, 0] = s1[:, 0]
    q2[:, S] = q2[:, 1]
    s3[:, S - 1] = s3[:, S]; o3[:, :2] = s3[:, :2]
    q4[:, 3] = q4[:, 1]
    s5[:, 5] = s5[:, 2]
    x = steer(rng, c); d, s1, e1, q2, s3, o3, q4, s5 = np.split(x, cut)
    e1[:, :2] = s1[:, :2]; o3[:, :4] = s3[:, :4]
    r2 = q2.copy(); r2[:, 4:] = (r2[:, 4:] + rng.integers(1, 256, (n, 8))) & 255
    r4 = q4.copy(); r4[:, 4:] = (r4[:, 4:] + rng.integers(1, 256, (n, 8))) & 255
    marks = [(d, 4, four), (d, F + 2, ()), (s1, 4, four), (s1, F + 2, ()), (r2, 4, four), (q2, F + 2, ()), (s3, 4, four), (s3, F + 2, ()), (o3, F, ()), (r4, 4, ()), (s5, 4, (6,))]
    ask = [(d, (4,)), (s1, (4,)), (q2, (F,)), (s3, (4,)), (o3, (4,)), (q4, (8,)), (s5, (4,)), (s5, (12,)), (e1, (12, 2)), (q2, (4,)), (q4, (8, 4))]
    return marks, np.concatenate([y for y, l in ask]), np.concatenate([alike_ropes(len(y), l) for y, l in ask]), 2 + 7 * n
def pack(P, q, wt):
    w = np.concatenate([wt, np.zeros((N, 8, 4, 2), np.int64)], axis=2)
    return {"mk": P.reshape(N, 128, W).astype(np.float32).astype(BF), "qs": q.reshape(N, 128, K).astype(np.float32).astype(BF), "wt": w.reshape(N, 128, 2).astype(np.float32).astype(BF)}
def setup_inputs(rng):
    wt = rng.integers(0, 256, (N, 8, 12, 2)); P, q = parts(rng, wt, [512] * 8, 3 * W // 4, ANY, LEN)
    return pack(P, q, wt)
def setup_inputs_alike(rng):
    wt = rng.integers(0, 256, (N, 8, 12, 2)); P, q = parts(rng, wt, rng.integers(16, 33, 8), 160, ANY, LEN)
    return pack(P, q, wt)
def setup_inputs_ends(rng):
    wt = rng.choice(np.array([0, 1, 255]), (N, 8, 12, 2)); wt[:, 3] = 0; wt[:, 5] = 255
    for g in (0, 1, 6):
        wt[:, g] = 0; wt[:, g, 0::2, 1] = 1; wt[:, g, 1::2, 1] = 255
    P, q = parts(rng, wt, [64] * 8, W // 4, np.array([0, 255, 0, 1, 254]), np.array([1, 12, 1, 12, 2, 11]))
    for g, ends in ((0, ((S, 0), (1, W - 1))), (1, ((S + 1, 0), (S + 1, W - 1))), (6, ((S, W - 1), (1, 0)))):
        marks, st, ro, look = meetings(rng, ends)
        for a in range(N):
            for y, m, l in marks: plant(P[a, g], y, np.full(len(y), m), alike_ropes(len(y), l), wt[a, g])
            j = np.concatenate([rng.permutation(len(st)), rng.integers(0, look, K - len(st))])
            q[a, g] = np.concatenate([st[j].T, ro[j].T])
    x = rng.integers(225, 256, (2048, 12)); x = x[np.unique(np.sum(x, axis=1), return_index=True)[1]]
    u = 255 * np.sum(x, axis=1); x = x[np.argsort(-((((u & 4095) ** 2) >> 5) + u))[:24]]
    for a in range(N):
        plant(P[a, 5], x, np.full(len(x), 12), np.zeros((len(x), 4), np.int64), wt[a, 5])
        t = rng.permutation(K)[:96]; q[a, 5][:12, t] = x[np.arange(96) % len(x)].T; q[a, 5][12:, t] = np.array([12, 0, 0, 0])[:, None]
    return pack(P, q, wt)
def setup_inputs_full(rng):
    w = rng.integers(0, 256, (8, 12, 2)); wt = np.stack([w] * N); P = fill(rng); q = np.zeros((N, 8, 16, K), np.int64)
    for g in range(8):
        st = rng.integers(0, 256, (2048, 12)); hs = np.stack([hashes(st, np.full(2048, m), w[g]) for m in [5] + [9 + i for i in range(S)]])
        used = set(); keep = []
        for i in range(2048):
            c = set(hs[:, i].tolist())
            if len(keep) < E and len(c) == S + 1 and not (c & used):
                used |= c; keep.append(i)
        x = st[np.array(keep)]; n = len(keep)
        for a in range(N):
            plant(P[a, g], x, np.full(n, 5), np.stack([np.array([9, 10, 11, 12])] * n), w[g])
            plant(P[a, g], x, np.full(n, 8 + S), np.zeros((n, 4), np.int64), w[g])
            j = np.concatenate([rng.permutation(n), rng.integers(0, n, K - n)])
            first = (rng.random(K) < 0.5) | (np.arange(K) < n)
            ro = np.where(first[:, None], np.array([5, 8, 0, 0]), np.array([7 + S, 5, 12, 0]))
            q[a, g] = np.concatenate([x[j].T, ro.T])
    return pack(P, q, wt)
def setup_inputs_still(rng):
    wt = rng.integers(0, 256, (N, 8, 12, 2)); P, q = parts(rng, wt, [256] * 8, W // 2, ANY, LEN); e = rng.permutation(8)
    q[:, :, 12:] = np.where(rng.random((N, 8, 1, K)) < 0.5, 0, q[:, :, 12:])
    q[:, e[0], 12:] = 0; P[:, e[1], 12:] = 0; q[:, e[2], :12] = rng.integers(0, 256, (N, 12, K))
    q[:, e[2], 12:] = np.where(q[:, e[2], 12:] > 0, np.maximum(q[:, e[2], 12:], 4), 0)
    return pack(P, q, wt)
def setup_inputs_spread(rng):
    vals = np.minimum(np.exp2(8.01 * rng.random(512)).astype(np.int64), 256) - 1
    wt = vals[rng.integers(0, 512, (N, 8, 12, 2))]; P, q = parts(rng, wt, 2 ** rng.integers(3, 12, 8), W // 2, vals, LEN)
    return pack(P, q, wt)
def check_inputs(d):
    bad = []
    for k, n in (("mk", W), ("qs", K), ("wt", 2)):
        v = np.asarray(d[k]).astype(np.float32).reshape(N, 8, 16, n)
        if not np.all(v == np.floor(v)): bad.append("whole numbers of " + k)
        if not (np.min(v) >= 0 and np.max(v[:, :, :12]) <= 255): bad.append("range of " + k)
        if not np.max(v[:, :, 12:]) <= (0 if k == "wt" else 12): bad.append("last four rows of " + k)
        if k != "wt" and np.any((v[:, :, 12:15] == 0) & (v[:, :, 13:] > 0)): bad.append("ropes of " + k)
    return bad
def reference(mk, qs, wt):
    P = mk.astype(np.float32).astype(np.int32).reshape(N, 8, 16, W); q = qs.astype(np.float32).astype(np.int32).reshape(N, 8, 16, K)
    w = np.ascontiguousarray(wt.astype(np.float32).astype(np.int32).reshape(N, 8, 16, 2)[:, :, :12].transpose(0, 1, 3, 2))
    p = np.arange(12, dtype=np.int32)[:, None]
    for rnd in range(RO):
        sy = q[:, :, :12]; ro = q[:, :, 12:]
        b = np.full((N, 8, K), -1, np.int32); f = np.full((N, 8, K), -1, np.int32); mb = np.zeros((N, 8, K), np.int32); mf = np.zeros((N, 8, K), np.int32)
        for step in range(S):
            m = ro[:, :, 0]
            u = np.matmul(w, np.where(p < m[:, :, None], sy, 0))
            h = place(u[:, :, 0], u[:, :, 1], m)
            v = np.take_along_axis(P, h[:, :, None], axis=3)
            same = np.all((v[:, :, :12] == sy) | (p >= m[:, :, None]), axis=2)
            hit = (m > 0) & same; miss = (m > 0) & ~same
            b = np.where(hit, h, b); mb = np.where(hit, m, mb)
            f = np.where(miss, h, np.where(hit, -1, f)); mf = np.where(miss, m, mf)
            less = np.concatenate([ro[:, :, 1:], np.zeros((N, 8, 1, K), np.int32)], axis=2)
            ro = np.where(hit[:, :, None], v[:, :, 12:], np.where(miss[:, :, None], less, ro))
        old = np.take_along_axis(P, np.maximum(b, 0)[:, :, None], axis=3)[:, :, :12]
        new = q.copy(); new[:, :, :12] = np.where((b >= 0)[:, :, None] & (p < mb[:, :, None] + X), old, sy)
        if rnd < RO - 1:
            for a in range(N):
                for g in range(8):
                    T = P[a, g]; c = np.nonzero((b[a, g, :E] >= 0) & (f[a, g, :E] >= 0))[0]
                    t = c[np.unique(f[a, g, c], return_index=True)[1]]
                    T[:, f[a, g, t]] = np.concatenate([sy[a, g][:, t], ro[a, g][:, t]])
                    t = c[np.unique(b[a, g, c], return_index=True)[1]]
                    have = T[12:15, b[a, g, t]]
                    T[12:, b[a, g, t]] = np.concatenate([mf[a, g, t][None], have])
            q = np.ascontiguousarray(new.reshape(N, 8, 16, N, K // N).transpose(3, 1, 2, 0, 4)).reshape(N, 8, 16, K)
    return {"yq": new.reshape(N, 128, K).astype(np.float32).astype(BF), "yb": np.stack([gtable(x) for x in b]).astype(np.float32)}

@@ -1,0 +1,536 @@
+from concourse.bass import DstId, RemoteDMATransfer
+from concourse.mybir import AluOpType, AxisListType, ActivationFunctionType
+
+A = AluOpType
+F = ActivationFunctionType
+W, NC, CH, NN, S = 8192, 3, 1024, 64, 3
+BIG, SL = 2.0 ** 60, 7.6
+
+SCRATCH, BANKS = {}, []
+
+
+def _b(dtype, where, spec, k=1):
+    for x in spec.split():
+        n, w = x.split(":")
+        SCRATCH[n] = (where, [128, k * int(w)], dtype)
+        if where == "psum":
+            BANKS.append(n)
+
+
+_b("bfloat16", "sbuf", "mk0:8192 mk1:8320 wts:2 ones:132 idw:132 ident:128 nident:128 isym:128 sh1:128 sh2:128 spl:128 spa:128 "
+   "z8a:8 z8:8 bm:143 WX:143 WY:143 WE:143 WR0:143 WR1:143 WR2:143 thv:64 ths:64 tha:64 thb:64 th3:64 sel1:16 sel2:16 "
+   "mt:16 g0:128 ga1:128 ga2:128 wnew:128 g1:128 mfw:128 snew:128")
+_b("int32", "sbuf", "ip:1 i16:1 kai:8 fi:8 mfi:8 sbi:8")
+_b("uint16", "sbuf", "flu:16 tgu:16 sbl:8 mfl:8")
+_b("float32", "sbuf", "icol:1 m12:1 sil:1 wc:1 c12:1 c13:1 c14:1 ge13:1 ge14:1 mid:1 wcm:1 wtf:2 mrow:64 iot:8208 trow:256 "
+   "t16a:16 t16:16 dump16:16 act:24 ka:24 kam:8 ed1:8 ed0:8 ed:16 fbm:16 fbe:16 nb:16 krow:256 dk:2048 first:16 win:16 "
+   "gg:16 tgt:16")
+SCRATCH["yby"] = ("sbuf", [128, 8, 24], "float32")
+_b("bfloat16", "sbuf", "qa:1024 qb:1024 rr:1024 zz:1024 dd:1024 ld:1024 lm:1024 nwa:1024 nwb:1024", NC)
+_b("float32", "sbuf", "rq:192 xx:128 x2:64 n2:64 m2:64 m3:64 thr0:64 thr:64 w97:64 hit:64 kb:64 ybx:64", NC)
+_b("int32", "sbuf", "ui:128 ac:128 pp:64 kk:64 ss:64 hi:64 ki:64 bi:64 mbi:64", NC)
+_b("uint16", "sbuf", "ml:64 hl:64 bl:64 mbl:64", NC)
+_b("float32", "psum", "pn0:512 pn1:512 pn2:512 pw0:512 pw1:512 pw2:512 vp:512 pe:512")
+
+SEMAPHORES = ["sT", "sV", "sS", "sG", "lw", "lm0", "lm1", "lyb"]
+for _c in range(NC):
+    SEMAPHORES += ["lq%d" % _c, "slf%d" % _c, "arr%d" % _c, "snt%d" % _c, "out%d" % _c]
+
+VC, PC, VG, VGS, OV, WAKE = 0.9545, 0.575, 1.5, 1.5, 20.0, 110.0
+BIAS = {"k": -1058e3, "e": 354e3}
+for _k, _v in (("00", (184, -129, -1279, 631)), ("01", (-1, 1099, 683, 606)), ("02", (615, 632, -124, 711)),
+               ("10", (1096, -254, 1530, -251)), ("11", (-293, 381, -1481, -1093)), ("12", (-816, -872, -293, 4))):
+    for _i in range(4):
+        BIAS[_k + str(_i)] = _v[_i] * 1e3
+Z_V = {(0, 0, 0), (0, 0, 1), (0, 0, 2), (0, 1, 0), (0, 1, 2), (0, 2, 0), (0, 2, 1), (0, 2, 2), (1, 0, 0), (1, 0, 1), (1, 0, 2),
+       (1, 1, 0), (1, 1, 1), (1, 1, 2), (1, 2, 0), (1, 2, 1)}
+D_S = {(0, 0, 1), (0, 0, 2), (1, 0, 2), (1, 1, 2)}
+L_S = {(0, 0), (1, 0)}
+
+
+def graph():
+    ops, acc, cur = [], {}, [""]
+
+    def add(q, dur, fn, R, Wr, sem=None, inc=1, lat=0.0, deps=(), pr=0.0):
+        i = len(ops)
+        d = set(deps)
+        for lst, isw in ((R, False), (Wr, True)):
+            for (b, lo, hi) in lst:
+                for (k, kq, klo, khi, kw) in acc.get(b, []):
+                    if lo < khi and klo < hi and (isw or kw):
+                        d.add(k)
+                    elif b in BANKS and kq != q:
+                        d.add(k)
+        for lst, isw in ((R, False), (Wr, True)):
+            for (b, lo, hi) in lst:
+                old = acc.setdefault(b, [])
+                if isw and b not in BANKS:
+                    old[:] = [x for x in old if x[0] == i or not (lo <= x[2] and x[3] <= hi)]
+                old.append((i, q, lo, hi, isw))
+        ops.append({"q": q, "dur": dur, "fn": fn, "deps": d, "sem": sem, "inc": inc, "lat": lat, "pr": pr, "tag": cur[0]})
+        return i
+
+    def ap(T, x):
+        return T[x[0]][:, x[1]:x[2]]
+
+    def vdur(n, k=1.0):
+        return max(64.0, n * k) * VC + OV
+
+    def insb(x):
+        return x[0] not in BANKS
+
+    def tt(out, a, b, op, ind=None):
+        n = out[2] - out[1]
+        if ind is None:
+            f = lambda g, T, e: g.vector.tensor_tensor(ap(T, out), ap(T, a), ap(T, b), op)
+            return add("V", vdur(n, 2.0 if insb(a) and insb(b) else 1.0), f, [a, b], [out])
+        f = lambda g, T, e: g.vector.tensor_tensor(ap(T, out), ap(T, a).indirect(ap(T, ind)), ap(T, b), op)
+        return add("V", 50 + n * VG * VC, f, [a, b, ind], [out])
+
+    def ts(out, a, s1, op0, s2=None, op1=None):
+        R = [a] + [s for s in (s1, s2) if isinstance(s, tuple)]
+
+        def f(g, T, e):
+            v1 = ap(T, s1) if isinstance(s1, tuple) else s1
+            v2 = ap(T, s2) if isinstance(s2, tuple) else s2
+            if op1 is None:
+                return g.vector.tensor_scalar(ap(T, out), ap(T, a), v1, None, op0)
+            return g.vector.tensor_scalar(ap(T, out), ap(T, a), v1, v2, op0, op1)
+        return add("V", vdur(out[2] - out[1]), f, R, [out])
+
+    def cp(out, a):
+        return add("V", vdur(out[2] - out[1]), lambda g, T, e: g.vector.tensor_copy(ap(T, out), ap(T, a)), [a], [out])
+
+    def scat(win, ind, src):
+        return add("V", 50 + (src[2] - src[1]) * 3 * VC,
+                   lambda g, T, e: g.vector.tensor_copy(ap(T, win).indirect(ap(T, ind)), ap(T, src)), [src, ind], [win])
+
+    def ms(out, v):
+        return add("V", vdur(out[2] - out[1]), lambda g, T, e: g.vector.memset(ap(T, out), v), [], [out])
+
+    def sa(out, a, func, scale=1.0, bias=0.0, ind=None):
+        n = out[2] - out[1]
+        R = [a] + ([ind] if ind else []) + ([bias] if isinstance(bias, tuple) else [])
+
+        def f(g, T, e):
+            src = ap(T, a).indirect(ap(T, ind)) if ind else ap(T, a)
+            if func is F.Copy:
+                return g.scalar.activation(ap(T, out), src, func)
+            return g.scalar.activation(ap(T, out), src, func, bias=ap(T, bias) if isinstance(bias, tuple) else bias, scale=scale)
+        return add("S", (65 + n * VGS * VC) if ind else (max(64.0, n) * VC + 60), f, R, [out])
+
+    def sm(out, a, col):
+        return add("S", max(64.0, out[2] - out[1]) * VC + 60,
+                   lambda g, T, e: g.scalar.activation(ap(T, out), ap(T, a), F.Copy, scale=ap(T, col)), [a, col], [out])
+
+    def pas(out, w, src):
+        bank, lo, hi = out
+        name, a, b = src
+
+        def f(g, T, e):
+            r = None
+            for j in range(16):
+                r = g.tensor.matmul(T[bank][:, lo:hi], T[w][:, 15 - j:143 - j], T[name][:, a + j:b:16], j == 0, j == 15)
+            return r
+        return add("T", 16 * 64 * PC + 60, f, [(w, 0, 143), src], [out])
+
+    def mm(out, *pairs):
+        def f(g, T, e):
+            r = None
+            for k, (l, x) in enumerate(pairs):
+                r = g.tensor.matmul(ap(T, out), ap(T, l), ap(T, x), k == 0, k == len(pairs) - 1)
+            return r
+        return add("T", len(pairs) * max(out[2] - out[1], 64) * PC + 60, f, [p[0] for p in pairs] + [p[1] for p in pairs], [out])
+
+    def gi(out, pattern, base, cm, flag):
+        def f(g, T, e):
+            if flag:
+                return g.iota(ap(T, out), pattern, base, cm, allow_small_or_imprecise_dtypes=True)
+            return g.iota(ap(T, out), pattern, base, cm)
+        return add("G", 130 + (out[2] - out[1]) * 2 * VC, f, [], [out])
+
+    def gs(out, a, pattern, op, base, cm):
+        return add("G", 170 + 2 * VC * (out[2] - out[1]),
+                   lambda g, T, e: g.affine_select(ap(T, out), ap(T, a), pattern, op, 0.0, base, cm), [a], [out])
+
+    def full(n):
+        return (n, 0, SCRATCH[n][1][1])
+
+    def c_(n, c, lo=0, hi=None):
+        w = SCRATCH[n][1][1] // NC
+        return (n, c * w + lo, c * w + (w if hi is None else hi))
+
+    def ldq(c, s, q):
+        a = c * CH + 128 * s
+
+        def f(g, T, e):
+            return (g.sync if q == "Y" else g.scalar).dma_start(T.qa[:, a:a + 128], T.qs[:, 384 * s + 128 * c:384 * s + 128 * c + 128])
+        add(q, 60, f, [], [("qa", a, a + 128)], sem="lq%d" % c, inc=16, lat=2500, pr=1e7 - c * 1e4)
+
+    add("Y", 60, lambda g, T, e: g.sync.dma_start(T.wts[:, :], T.wt[:, :]), [], [full("wts")], sem="lw", inc=16, lat=2000, pr=5e7)
+    for c in range(NC):
+        for s in range(8):
+            ldq(c, s, "S" if c == 0 and s >= 4 else "Y")
+        if c == 0:
+            add("S", 60, lambda g, T, e: g.scalar.dma_start(T.mk0[:, :], T.mk[:, :]), [], [full("mk0")], sem="lm0", inc=16,
+                lat=7000, pr=5e6)
+    add("Y", 60, lambda g, T, e: g.sync.dma_start(T.mk1[:, 0:W], T.mk[:, :]), [], [("mk1", 0, W)], sem="lm1", inc=16, lat=7000)
+
+    gi(full("ip"), [[0, 1]], 0, 1, False)
+    ms(full("ones"), 1.0)
+    gs(full("z8a"), ("ones", 0, 8), [[-16, 8]], A.is_ge, 0, 1)
+    gs(full("z8"), full("z8a"), [[16, 8]], A.is_ge, 15, -1)
+    gs(full("idw"), full("ones"), [[1, 132]], A.is_equal, -2, -1)
+    gi(full("mrow"), [[0, 4], [1, 16]], 0, 0, True)
+    ts(full("i16"), full("ip"), 15, A.bitwise_and)
+    cp(full("icol"), full("i16"))
+    ms(full("bm"), 0.0)
+    add("V", 84, lambda g, T, e: g.vector.tensor_copy(T.bm[:, 15:128:16], T.z8[:, :]), [full("z8")], [full("bm")])
+    for n, op, v in (("m12", A.is_lt, 12.0), ("c12", A.is_equal, 12.0), ("c13", A.is_equal, 13.0), ("c14", A.is_equal, 14.0),
+                     ("ge13", A.is_ge, 13.0), ("ge14", A.is_ge, 14.0)):
+        ts(full(n), full("icol"), v, op)
+    cp(full("wtf"), full("wts"))
+    for k in range(3):
+        sm(full("WR%d" % k), full("bm"), full("c1%d" % (2 + k)))
+    sm(full("WX"), full("bm"), ("wtf", 0, 1))
+    sm(full("WY"), full("bm"), ("wtf", 1, 2))
+    cp(full("ident"), ("idw", 2, 130))
+    ts(full("nident"), ("idw", 2, 130), -1.0, A.mult)
+    ts(full("thv"), full("mrow"), full("icol"), A.is_gt, full("m12"), A.mult)
+    ts(full("ths"), full("thv"), 256.0, A.mult, -256.0, A.add)
+    sa(full("sil"), full("icol"), F.Silu, scale=-SL, bias=-SL)
+    ts(full("wc"), full("sil"), -1.5 * BIG, A.mult, full("m12"), A.mult)
+    sm(full("WE"), full("bm"), full("wc"))
+    ts(full("tha"), full("mrow"), 3.0, A.add, full("icol"), A.is_gt)
+    ts(full("thb"), full("mrow"), 0.0, A.is_gt, full("m12"), A.mult)
+    tt(full("th3"), full("tha"), full("thb"), A.mult)
+
+    def edit_constants():
+        gi(full("trow"), [[0, 2], [1, 128]], 0, 0, True)
+        gi(full("t16a"), [[0, 2], [16, 8]], 0, 0, True)
+        gi(full("iot"), [[256, 8208]], 0, 0, True)
+        ts(full("t16"), full("t16a"), full("icol"), A.add)
+        ts(full("dump16"), full("t16"), 8192.0, A.add)
+        sm(full("isym"), ("idw", 2, 130), full("m12"))
+        sm(full("sh1"), ("idw", 3, 131), full("ge13"))
+        sm(full("sh2"), ("idw", 4, 132), full("ge14"))
+        ts(full("sel1"), ("mrow", 0, 16), 2.0, A.is_equal)
+        ts(full("sel2"), ("mrow", 0, 16), 1.0, A.is_equal)
+        sm(full("mt"), ("mrow", 0, 16), full("c12"))
+        ts(full("mid"), full("icol"), 15.0, A.is_lt)
+        tt(full("wcm"), full("mid"), full("m12"), A.subtract)
+        sm(full("spa"), ("idw", 1, 129), full("wcm"))
+        tt(full("spl"), full("spa"), full("isym"), A.add)
+
+    def under(rd, c, st, q):
+        ml = c_("ml", c)
+        if (rd, c, st) in Z_V:
+            tt(c_("zz", c), full("thv"), c_(q, c), A.mult, ind=ml)
+            return
+        for h in (0, 512):
+            sa(c_("rr", c, h, h + 512), full("ths"), F.Copy, ind=c_("ml", c, h // 16, h // 16 + 32))
+            mm(("pw%d" % c, 0, 512), (full("ident"), c_(q, c, h, h + 512)), (full("ident"), c_("rr", c, h, h + 512)))
+            sa(c_("zz", c, h, h + 512), ("pw%d" % c, 0, 512), F.Relu)
+
+    def diff(c, out, mk, q, ind, byS):
+        if not byS:
+            tt(out, mk, c_(q, c), A.subtract, ind=ind)
+            return
+        for h in (0, 512):
+            sa(c_("rr", c, h, h + 512), mk, F.Copy, ind=(ind[0], ind[1] + h // 16, ind[1] + h // 16 + 32))
+            mm(("pw%d" % c, 0, 512), (full("ident"), c_("rr", c, h, h + 512)), (full("nident"), c_(q, c, h, h + 512)))
+            sa((out[0], out[1] + h, out[1] + h + 512), ("pw%d" % c, 0, 512), F.Copy)
+
+    def search(rd, c):
+        q = "qa" if rd == 0 else "qb"
+        mk = ("mk0" if rd == 0 else "mk1", 0, W)
+        pn, pw = "pn%d" % c, "pw%d" % c
+        u2, R0, R1, ky = (pn, 64, 128), (pn, 128, 192), (pn, 192, 256), (pn, 448, 512)
+        tA, tB = ("vp", c * 128, c * 128 + 64), ("vp", c * 128 + 64, c * 128 + 128)
+        hit = c_("hit", c)
+        rq = lambda k: c_("rq", c, NN * k, NN * k + NN)
+        cur[0] = "%d%d0" % (rd, c)
+        pas((pn, 256, 320), "WR0", c_(q, c))
+        cp(c_("ml", c), (pn, 256, 320))
+        sa(rq(0), (pn, 256, 320), F.Copy)
+        for st in range(S):
+            cur[0] = "%d%d%d" % (rd, c, st)
+            m = rq(0) if st == 0 else c_("m%d" % (st + 1), c)
+            under(rd, c, st, q)
+            sa(c_("w97", c), m, F.Identity, scale=97.0)
+            sa(ky, m, F.Identity, scale=8192.0, bias=float((st + 1) << 17))
+            sa(c_("thr0", c), m, F.Silu, scale=-SL)
+            sa(c_("thr", c), c_("thr0", c), F.Abs, scale=BIG)
+            pas((pn, 0, 64), "WX", c_("zz", c))
+            pas(u2, "WY", c_("zz", c))
+            cp(c_("ui", c), (pn, 0, 128))
+            ts(c_("ac", c), c_("ui", c), 4095, A.bitwise_and)
+            tt(tA, u2, c_("w97", c), A.add)
+            tt(c_("pp", c), c_("ac", c, 0, NN), c_("ac", c, NN, 2 * NN), A.mult)
+            ts(c_("kk", c), c_("pp", c), 5, A.arith_shift_right)
+            tt(c_("ss", c), tA, c_("kk", c), A.add)
+            ts(c_("hi", c), c_("ss", c), W - 1, A.bitwise_and)
+            cp(c_("hl", c), c_("hi", c))
+            tt(ky, ky, c_("hi", c), A.add)
+            if rd == 0 and c == 0:
+                x8 = ("act", 8 * st, 8 * st + 8)
+                ts(x8, (m[0], m[1], m[1] + 8), 0.0, A.is_gt)
+                tt(("ka", 8 * st, 8 * st + 8), (pn, 448, 456), x8, A.mult)
+            diff(c, c_("dd", c), mk, q, c_("hl", c), (rd, c, st) in D_S)
+            if st == 0:
+                for k in (1, 2):
+                    pas((pn, 256 + 64 * k, 320 + 64 * k), "WR%d" % k, c_(q, c))
+                sa(c_("rq", c, NN, 3 * NN), (pn, 320, 448), F.Copy)
+                tt(c_("xx", c), (pn, 256, 384), c_("rq", c, NN, 3 * NN), A.subtract)
+            pas((pw, 0, 64), "WE", c_("dd", c))
+            if st < 2:
+                pas(R0, "WR0", c_("dd", c))
+            if st < 1:
+                pas(R1, "WR1", c_("dd", c))
+            sa((pw, 64, 128), (pw, 0, 64), F.Abs)
+            tt(hit, (pw, 64, 128), c_("thr", c), A.is_lt)
+            if st < 2:
+                nx = c_("m%d" % (st + 2), c)
+                if st == 0:
+                    x, old = c_("xx", c, 0, NN), rq(1)
+                else:
+                    x, old = c_("x2", c), c_("n2", c)
+                    tt(x, rq(0), old, A.subtract)
+                tt(tB, R0, x, A.add)
+                tt(tB, tB, hit, A.mult)
+                tt(nx, tB, old, A.add)
+                cp(c_("ml", c), nx)
+            if st == 0:
+                tt(c_("kb", c), ky, hit, A.mult)
+                tt(tA, R1, c_("xx", c, NN, 2 * NN), A.add)
+                tt(tA, tA, hit, A.mult)
+                tt(c_("n2", c), tA, rq(2), A.add)
+            else:
+                tt(tA, ky, hit, A.mult)
+                tt(c_("kb", c), tA, c_("kb", c), A.max)
+
+    def learn(rd, c):
+        q = "qa" if rd == 0 else "qb"
+        nw = "nwa" if rd == 0 else "nwb"
+        mk = ("mk0" if rd == 0 else "mk1", 0, W)
+        cur[0] = "%d%d3" % (rd, c)
+        cp(c_("ki", c), c_("kb", c))
+        ts(c_("bi", c), c_("ki", c), W - 1, A.bitwise_and)
+        cp(c_("bl", c), c_("bi", c))
+        diff(c, c_("ld", c), mk, q, c_("bl", c), (rd, c) in L_S)
+        ts(c_("mbi", c), c_("ki", c), 13, A.arith_shift_right)
+        cp(c_("mbl", c), c_("mbi", c))
+        for h in (0, 512):
+            tt(c_("lm", c, h, h + 512), full("th3"), c_("ld", c, h, h + 512), A.mult, ind=c_("mbl", c, h // 16, h // 16 + 32))
+            mm(("pw%d" % c, 0, 512), (full("ident"), c_(q, c, h, h + 512)), (full("ident"), c_("lm", c, h, h + 512)))
+            sa(c_(nw, c, h, h + 512), ("pw%d" % c, 0, 512), F.Copy)
+
+    def move(c):
+        def f(g, T, e):
+            core, rank, topo = e
+            moves, k = [], 0
+            for d in range(1, 8):
+                s = (rank + d) % 8
+                dst = T.cores[s]
+                en = topo.engines(core, dst)
+                if topo.chip(dst) == topo.chip(core):
+                    eng = en[-1]
+                else:
+                    eng = (en[0::2] + en[1::2])[k]
+                    k += 1
+                ad = topo.addr(dst)
+                moves.append(RemoteDMATransfer(
+                    dst_ids=[DstId(rid=ad[0], pnc=ad[1])], dma_engine_mask=1 << eng, remote_sem=T.sem["arr%d" % c],
+                    src=T.nwa[:, c * CH + 128 * s:c * CH + 128 * s + 128],
+                    dst=T.qb[:, c * CH + 128 * rank:c * CH + 128 * rank + 128]))
+            return g.remote_dma_fused(moves, local_sem=T.sem["snt%d" % c])
+        i = add("G", 1500, f, [c_("nwa", c)], [], sem="none%d" % c, inc=0)
+        add("arr%d" % c, 0, None, [], [c_("qb", c)], sem="arr%d" % c, inc=7, lat=7000, deps=(i,))
+
+        def f2(g, T, e):
+            a = c * CH + 128 * e[1]
+            return g.sync.dma_start(T.qb[:, a:a + 128], T.nwa[:, a:a + 128])
+        k = add("Y", 60, f2, [c_("nwa", c)], [], sem="slf%d" % c, inc=16, lat=2500)
+        acc["qb"].append((k, "Y", c * CH, c * CH + CH, True))
+
+    def edits():
+        e8 = lambda n: c_(n, 0, 0, 8)
+        a8 = lambda n, k: (n, 8 * k, 8 * k + 8)
+        tt(full("kam"), a8("ka", 0), a8("ka", 1), A.max)
+        tt(full("kam"), full("kam"), a8("ka", 2), A.max)
+        cp(full("kai"), full("kam"))
+        ts(full("fi"), full("kai"), W - 1, A.bitwise_and)
+        ts(full("mfi"), full("kai"), 13, A.arith_shift_right, 15, A.bitwise_and)
+        ts(full("sbi"), e8("ki"), 17, A.arith_shift_right)
+        cp(full("sbl"), full("sbi"))
+        cp(full("mfl"), full("mfi"))
+        tt(full("ed1"), full("kam"), e8("kb"), A.is_gt)
+        ts(full("ed0"), e8("kb"), 0.0, A.is_gt)
+        for k in (0, 1):
+            tt(a8("ed", k), full("ed1"), full("ed0"), A.mult)
+        ts(a8("fbm", 0), full("fi"), -8192.0, A.add)
+        ts(a8("fbm", 1), e8("bi"), -8192.0, A.add)
+        tt(full("fbe"), full("fbm"), full("ed"), A.mult)
+        ts(full("flu"), full("fbe"), 8192.0, A.add)
+        ts(full("nb"), full("fbe"), -256.0, A.mult, -2097152.0, A.add)
+        tt(full("krow"), full("iot"), full("trow"), A.add, ind=full("flu"))
+        for k in range(16):
+            h, n = 128 * (k // 8), 16 * (k % 8 + 1)
+            sa(("dk", 128 * k, 128 * k + n), ("krow", h, h + n), F.Identity, bias=("nb", k, k + 1))
+            add("V", vdur(n), lambda g, T, e, k=k, n=n: g.vector.tensor_reduce(
+                T.first[:, k:k + 1], T.dk[:, 128 * k:128 * k + n], AxisListType.X, A.min, apply_absolute_value=True),
+                [("dk", 128 * k, 128 * k + n)], [("first", k, k + 1)])
+        tt(full("win"), full("first"), full("t16"), A.is_equal)
+        tt(full("win"), full("win"), full("ed"), A.mult)
+        tt(full("gg"), full("fbm"), full("t16"), A.subtract)
+        tt(full("gg"), full("gg"), full("win"), A.mult)
+        tt(full("tgt"), full("gg"), full("dump16"), A.add)
+        cp(full("tgu"), full("tgt"))
+        sa(full("g0"), ("mk0", 0, W), F.Copy, ind=e8("bl"))
+        tt(full("ga1"), full("sel1"), full("g0"), A.mult, ind=full("sbl"))
+        tt(full("ga2"), full("sel2"), full("g0"), A.mult, ind=full("sbl"))
+        mm(("pe", 0, 128), (full("sh1"), full("ga1")), (full("sh2"), full("ga2")), (full("isym"), ("qa", 0, 128)))
+        sa(full("wnew"), ("pe", 0, 128), F.Copy)
+        scat(full("mk1"), ("tgu", 0, 8), full("wnew"))
+        sa(full("g1"), ("mk1", 0, W), F.Copy, ind=e8("bl"))
+        sa(full("mfw"), full("mt"), F.Copy, ind=full("mfl"))
+        mm(("pe", 0, 128), (full("spl"), full("g1")), (full("ident"), full("mfw")))
+        sa(full("snew"), ("pe", 0, 128), F.Copy)
+        scat(full("mk1"), ("tgu", 8, 16), full("snew"))
+
+    def blocks(c):
+        ts(c_("ybx", c), c_("kb", c), 0.0, A.is_equal, -1.0, A.mult)
+        add("V", vdur(64, 2), lambda g, T, e: g.vector.tensor_tensor(T.yby[:, :, 8 * c:8 * c + 8], ap(T, c_("ybx", c)),
+            ap(T, c_("bi", c)), A.add), [c_("ybx", c), c_("bi", c)], [("yby", 64 * c, 64 * c + 64)])
+        if c == NC - 1:
+            add("Y", 60, lambda g, T, e: g.sync.dma_start(T.yb[:, :], T.yby[:, :, :]),
+                [("yby", 0, 192)], [], sem="lyb", inc=16, lat=2500)
+
+    def store(c):
+        for s in range(8):
+            q = "S" if c == NC - 1 and s >= 6 else "Y"
+            a = c * CH + 128 * s
+
+            def f(g, T, e, a=a, s=s, q=q):
+                return (g.sync if q == "Y" else g.scalar).dma_start(
+                    T.yq[:, 384 * s + 128 * c:384 * s + 128 * c + 128], T.nwb[:, a:a + 128])
+            add(q, 60, f, [("nwb", a, a + 128)], [], sem="out%d" % c, inc=16, lat=2500)
+
+    for c in range(NC):
+        search(0, c)
+        learn(0, c)
+        move(c)
+    cur[0] = "k"
+    edit_constants()
+    cur[0] = "e"
+    edits()
+    for c in range(NC):
+        search(1, c)
+        learn(1, c)
+        blocks(c)
+        store(c)
+    return ops
+
+
+QSEM = {"T": "sT", "V": "sV", "S": "sS", "G": "sG"}
+
+
+def schedule(ops):
+    n = len(ops)
+    kids = [[] for _ in range(n)]
+    need = [len(o["deps"]) for o in ops]
+    for i, o in enumerate(ops):
+        for d in o["deps"]:
+            kids[d].append(i)
+    tail = [0.0] * n
+    for i in range(n - 1, -1, -1):
+        tail[i] = ops[i]["dur"] + ops[i]["lat"] + max([tail[k] + WAKE for k in kids[i]] or [0.0])
+    free, ready, est, done = {}, {}, [0.0] * n, [0.0] * n
+    for i in range(n):
+        ready.setdefault(ops[i]["q"], [])
+        free[ops[i]["q"]] = 0.0
+        if need[i] == 0:
+            ready[ops[i]["q"]].append(i)
+    order = []
+    for _ in range(n):
+        best = None
+        for q, lst in ready.items():
+            if lst:
+                t = max(free[q], min(est[i] for i in lst))
+                if best is None or t < best[0]:
+                    best = (t, q)
+        t, q = best
+        i = max((i for i in ready[q] if est[i] <= t), key=lambda i: (tail[i] + ops[i]["pr"] + BIAS.get(ops[i]["tag"], 0.0), -i))
+        ready[q].remove(i)
+        free[q] = t + ops[i]["dur"]
+        done[i] = free[q] + ops[i]["lat"]
+        order.append(i)
+        for k in kids[i]:
+            est[k] = max(est[k], done[i] + WAKE)
+            need[k] -= 1
+            if need[k] == 0:
+                ready[ops[k]["q"]].append(k)
+    return order, max(done), done
+
+
+PLAN = {}
+
+
+def rank_program(g, core, T, topo):
+    rank = T.rank_of(core)
+    if rank is None:
+        return
+    if not PLAN:
+        PLAN["ops"] = graph()
+        PLAN["order"] = schedule(PLAN["ops"])[0]
+    ops, order = PLAN["ops"], PLAN["order"]
+    env = (core, rank, topo)
+    eng = {"T": g.tensor, "V": g.vector, "S": g.scalar, "G": g, "Y": g.sync}
+    total = {}
+    for o in ops:
+        if o["sem"] and o["inc"]:
+            total[o["sem"]] = total.get(o["sem"], 0) + o["inc"]
+    count, stamp, clock, known = {}, {}, {}, {}
+    for i in order:
+        o = ops[i]
+        q = o["q"]
+        kn = known.setdefault(q, {})
+        want = {}
+        for d in o["deps"]:
+            s, v = stamp[d]
+            if kn.get(s, 0) < v:
+                want[s] = max(want.get(s, 0), v)
+        for s in sorted(want, key=lambda s: -len(clock[(s, want[s])])):
+            v = want[s]
+            if kn.get(s, 0) >= v:
+                continue
+            if o["fn"] is not None and not s.startswith("none"):
+                eng[q].wait_ge(T.sem[s], v)
+            kn[s] = max(kn.get(s, 0), v)
+            for s2, v2 in clock[(s, v)].items():
+                kn[s2] = max(kn.get(s2, 0), v2)
+        ins = o["fn"](g, T, env) if o["fn"] is not None else None
+        if o["sem"] is None:
+            s = QSEM[q]
+            count[s] = count.get(s, 0) + 1
+            ins.then_inc(T.sem[s], 1)
+            v = count[s]
+            prev = clock.get((s, v - 1), {})
+        else:
+            s = o["sem"]
+            v = total.get(s, 1)
+            if ins is not None and o["inc"]:
+                ins.then_inc(T.sem[s], o["inc"])
+            prev = clock.get((s, v), {})
+        stamp[i] = (s, v)
+        ck = {}
+        if not s.startswith("arr"):
+            ck = dict(prev)
+            for s2, v2 in kn.items():
+                ck[s2] = max(ck.get(s2, 0), v2)
+        clock[(s, v)] = ck
+    for s in SEMAPHORES:
+        if s in count:
+            g.wait_ge(T.sem[s], count[s])
+        else:
+            g.wait_ge(T.sem[s], total[s] if s in total else 7)

@@ -1,10 +1,13 @@
+import math
 from concourse.bass import DstId, RemoteDMATransfer
 from concourse.mybir import AluOpType, AxisListType, ActivationFunctionType
 
 A = AluOpType
 F = ActivationFunctionType
 W, NC, CH, NN, S = 8192, 3, 1024, 64, 3
-BIG, SL = 2.0 ** 60, 7.6
+LN2 = math.log(2.0)
+M13, M18 = 1.5 * 2.0 ** 36, 1.5 * 2.0 ** 41
+HALF = 4095.5
 
 SCRATCH, BANKS = {}, []
 
@@ -17,61 +20,69 @@ def _b(dtype, where, spec, k=1):
             BANKS.append(n)
 
 
-_b("bfloat16", "sbuf", "mk0:8192 mk1:8320 wts:2 ones:132 idw:132 ident:128 nident:128 isym:128 sh1:128 sh2:128 spl:128 spa:128 "
-   "z8a:8 z8:8 bm:143 WX:143 WY:143 WE:143 WR0:143 WR1:143 WR2:143 thv:64 ths:64 tha:64 thb:64 th3:64 sel1:16 sel2:16 "
+_b("bfloat16", "sbuf", "mk0:8208 mk1:8336 wts:2 ones:132 idw:132 ident:128 nident:128 i97:128 n97:128 i68:128 ik:128 i75:128 "
+   "n75:128 f75:128 bda:128 bd:128 dk1:128 dk3:128 lk:1024 lp:1024 ln:1024 e3:3 wu1:24 wu2:16 wq:40 wd0:24 wd1:16 "
+   "isym:128 sh1:128 sh2:128 spl:128 spa:128 z8a:8 z8:8 sel1:16 sel2:16 "
    "mt:16 g0:128 ga1:128 ga2:128 wnew:128 g1:128 mfw:128 snew:128")
-_b("int32", "sbuf", "ip:1 i16:1 kai:8 fi:8 mfi:8 sbi:8")
+_b("int32", "sbuf", "ip:1 i16:1 k2:16 fb:16 mfi:8 sbi:8")
 _b("uint16", "sbuf", "flu:16 tgu:16 sbl:8 mfl:8")
-_b("float32", "sbuf", "icol:1 m12:1 sil:1 wc:1 c12:1 c13:1 c14:1 ge13:1 ge14:1 mid:1 wcm:1 wtf:2 mrow:64 iot:8208 trow:256 "
-   "t16a:16 t16:16 dump16:16 act:24 ka:24 kam:8 ed1:8 ed0:8 ed:16 fbm:16 fbe:16 nb:16 krow:256 dk:2048 first:16 win:16 "
+_b("float32", "sbuf", "col:32 identf:128 selm:8 wtf:2 mrow:64 iot:8208 trow:256 "
+   "t16a:16 t16:16 t16b:16 dump16:16 act:64 ed1:8 ed0:8 ed:16 fbm:16 fbe:16 nb:16 krow:256 dk:2048 first:16 win:16 "
    "gg:16 tgt:16")
 SCRATCH["yby"] = ("sbuf", [128, 8, 24], "float32")
-_b("bfloat16", "sbuf", "qa:1024 qb:1024 rr:1024 zz:1024 dd:1024 ld:1024 lm:1024 nwa:1024 nwb:1024", NC)
-_b("float32", "sbuf", "rq:192 xx:128 x2:64 n2:64 m2:64 m3:64 thr0:64 thr:64 w97:64 hit:64 kb:64 ybx:64", NC)
-_b("int32", "sbuf", "ui:128 ac:128 pp:64 kk:64 ss:64 hi:64 ki:64 bi:64 mbi:64", NC)
-_b("uint16", "sbuf", "ml:64 hl:64 bl:64 mbl:64", NC)
+for _n, _d in (("xf0", "float32"), ("xf1", "float32"), ("xf2", "float32"), ("xk", "float32"), ("xa", "float32"),
+               ("fx0", "bfloat16"), ("fx1", "bfloat16"), ("fx2", "bfloat16")):
+    SCRATCH[_n] = ("sbuf", [128, 17, 8], _d)
+_b("bfloat16", "sbuf", "qa:1024 qb:1024 zz:1024 dd:1024 ld:1024 nwa:1024 nwb:1024 ra:512 rb:320 fts:128 hit:64", NC)
+_b("float32", "sbuf", "cs:64 tt:64 kb:64 mb8:64 ybx:64", NC)
+_b("int32", "sbuf", "pp:64 kk:64", NC)
+_b("uint16", "sbuf", "hl:64 bl:64", NC)
 _b("float32", "psum", "pn0:512 pn1:512 pn2:512 pw0:512 pw1:512 pw2:512 vp:512 pe:512")
 
 SEMAPHORES = ["sT", "sV", "sS", "sG", "lw", "lm0", "lm1", "lyb"]
 for _c in range(NC):
     SEMAPHORES += ["lq%d" % _c, "slf%d" % _c, "arr%d" % _c, "snt%d" % _c, "out%d" % _c]
 
-VC, PC, VG, VGS, OV, WAKE = 0.9545, 0.575, 1.5, 1.5, 20.0, 110.0
-BIAS = {"k": -1058e3, "e": 354e3}
-for _k, _v in (("00", (184, -129, -1279, 631)), ("01", (-1, 1099, 683, 606)), ("02", (615, 632, -124, 711)),
-               ("10", (1096, -254, 1530, -251)), ("11", (-293, 381, -1481, -1093)), ("12", (-816, -872, -293, 4))):
-    for _i in range(4):
-        BIAS[_k + str(_i)] = _v[_i] * 1e3
-Z_V = {(0, 0, 0), (0, 0, 1), (0, 0, 2), (0, 1, 0), (0, 1, 2), (0, 2, 0), (0, 2, 1), (0, 2, 2), (1, 0, 0), (1, 0, 1), (1, 0, 2),
-       (1, 1, 0), (1, 1, 1), (1, 1, 2), (1, 2, 0), (1, 2, 1)}
-D_S = {(0, 0, 1), (0, 0, 2), (1, 0, 2), (1, 1, 2)}
-L_S = {(0, 0), (1, 0)}
+VC, PC, VG, VGS, OV, OS, WAKE = 0.9545, 0.48, 1.5, 1.5, 20.0, 60.0, 110.0
+BIAS = {'000': 140900, '001': -47100, '002': -127700, '003': 161800, '010': 4000, '011': -51400, '012': -46900, '013': -27700, '020': 1000, '021': 118100, '022': -24400, '023': 105800, '100': 47200, '101': -55800, '102': 87400, '103': -14200, '110': 13000, '111': 97800, '112': 23900, '113': -143600, '120': -41600, '121': 44000, '122': 12100, '123': -68100, 'c': 41800, 'e': -87600, 'k': -24900, 'l': -84200}
+Z_V = {(0, 1, 0, 0), (1, 0, 0, 0), (1, 0, 0, 1), (1, 0, 1, 1), (1, 0, 2, 0), (1, 1, 0, 1), (1, 2, 0, 1)}
+L_V = {(0, 2), (1, 1), (1, 2)}
+COLS = {}
 
 
 def graph():
     ops, acc, cur = [], {}, [""]
 
-    def add(q, dur, fn, R, Wr, sem=None, inc=1, lat=0.0, deps=(), pr=0.0):
+    def add(q, dur, fn, R, Wr, sem=None, inc=1, lat=0.0, deps=(), pr=0.0, cont=None):
         i = len(ops)
         d = set(deps)
         for lst, isw in ((R, False), (Wr, True)):
-            for (b, lo, hi) in lst:
+            for x in lst:
+                b, lo, hi = x[:3]
                 for (k, kq, klo, khi, kw) in acc.get(b, []):
                     if lo < khi and klo < hi and (isw or kw):
                         d.add(k)
                     elif b in BANKS and kq != q:
                         d.add(k)
         for lst, isw in ((R, False), (Wr, True)):
-            for (b, lo, hi) in lst:
+            for x in lst:
+                b, lo, hi = x[:3]
                 old = acc.setdefault(b, [])
                 if isw and b not in BANKS:
-                    old[:] = [x for x in old if x[0] == i or not (lo <= x[2] and x[3] <= hi)]
+                    old[:] = [y for y in old if y[0] == i or not (lo <= y[2] and y[3] <= hi)]
                 old.append((i, q, lo, hi, isw))
-        ops.append({"q": q, "dur": dur, "fn": fn, "deps": d, "sem": sem, "inc": inc, "lat": lat, "pr": pr, "tag": cur[0]})
+        ops.append({"q": q, "dur": dur, "fn": fn, "deps": d, "sem": sem, "inc": inc, "lat": lat, "pr": pr, "tag": cur[0],
+                    "cont": cont})
         return i
 
     def ap(T, x):
-        return T[x[0]][:, x[1]:x[2]]
+        return x[3](T) if len(x) > 3 else T[x[0]][:, x[1]:x[2]]
+
+    def wd(x):
+        return x[4] if len(x) > 3 else x[2] - x[1]
+
+    def two(*xs):
+        return all(SCRATCH[x[0]][2] in ("bfloat16", "uint16") for x in xs)
 
     def vdur(n, k=1.0):
         return max(64.0, n * k) * VC + OV
@@ -80,7 +91,7 @@ def graph():
         return x[0] not in BANKS
 
     def tt(out, a, b, op, ind=None):
-        n = out[2] - out[1]
+        n = wd(out)
         if ind is None:
             f = lambda g, T, e: g.vector.tensor_tensor(ap(T, out), ap(T, a), ap(T, b), op)
             return add("V", vdur(n, 2.0 if insb(a) and insb(b) else 1.0), f, [a, b], [out])
@@ -96,61 +107,84 @@ def graph():
             if op1 is None:
                 return g.vector.tensor_scalar(ap(T, out), ap(T, a), v1, None, op0)
             return g.vector.tensor_scalar(ap(T, out), ap(T, a), v1, v2, op0, op1)
-        return add("V", vdur(out[2] - out[1]), f, R, [out])
+        return add("V", vdur(wd(out), 0.5 if two(out, a) else 1.0), f, R, [out])
 
     def cp(out, a):
-        return add("V", vdur(out[2] - out[1]), lambda g, T, e: g.vector.tensor_copy(ap(T, out), ap(T, a)), [a], [out])
+        return add("V", vdur(wd(out), 0.5 if two(out, a) else 1.0),
+                   lambda g, T, e: g.vector.tensor_copy(ap(T, out), ap(T, a)), [a], [out])
 
     def scat(win, ind, src):
-        return add("V", 50 + (src[2] - src[1]) * 3 * VC,
+        return add("V", 50 + wd(src) * 3 * VC,
                    lambda g, T, e: g.vector.tensor_copy(ap(T, win).indirect(ap(T, ind)), ap(T, src)), [src, ind], [win])
 
     def ms(out, v):
-        return add("V", vdur(out[2] - out[1]), lambda g, T, e: g.vector.memset(ap(T, out), v), [], [out])
+        return add("V", vdur(wd(out), 0.5 if two(out) else 1.0), lambda g, T, e: g.vector.memset(ap(T, out), v), [], [out])
 
-    def sa(out, a, func, scale=1.0, bias=0.0, ind=None):
-        n = out[2] - out[1]
-        R = [a] + ([ind] if ind else []) + ([bias] if isinstance(bias, tuple) else [])
+    def sa(out, a, func, scale=1.0, bias=0.0, ind=None, more=0.0):
+        n = wd(out)
+        R = [a] + ([ind] if ind else []) + [x for x in (bias, scale) if isinstance(x, tuple)]
 
         def f(g, T, e):
             src = ap(T, a).indirect(ap(T, ind)) if ind else ap(T, a)
+            sc = ap(T, scale) if isinstance(scale, tuple) else scale
             if func is F.Copy:
-                return g.scalar.activation(ap(T, out), src, func)
-            return g.scalar.activation(ap(T, out), src, func, bias=ap(T, bias) if isinstance(bias, tuple) else bias, scale=scale)
-        return add("S", (65 + n * VGS * VC) if ind else (max(64.0, n) * VC + 60), f, R, [out])
+                return g.scalar.activation(ap(T, out), src, func, scale=sc)
+            return g.scalar.activation(ap(T, out), src, func, bias=ap(T, bias) if isinstance(bias, tuple) else bias, scale=sc)
+        return add("S", more + ((65 + n * VGS * VC) if ind else (max(64.0, n) * VC + OS)), f, R, [out])
 
-    def sm(out, a, col):
-        return add("S", max(64.0, out[2] - out[1]) * VC + 60,
-                   lambda g, T, e: g.scalar.activation(ap(T, out), ap(T, a), F.Copy, scale=ap(T, col)), [a, col], [out])
-
-    def pas(out, w, src):
-        bank, lo, hi = out
-        name, a, b = src
-
+    def pe(calls, R, Wr, cont=None):
         def f(g, T, e):
             r = None
-            for j in range(16):
-                r = g.tensor.matmul(T[bank][:, lo:hi], T[w][:, 15 - j:143 - j], T[name][:, a + j:b:16], j == 0, j == 15)
+            for cy, o, l, x, st, sp in calls:
+                r = g.tensor.matmul(o(T), l(T), x(T), st, sp)
             return r
-        return add("T", 16 * 64 * PC + 60, f, [(w, 0, 143), src], [out])
+        return add("T", sum(k[0] for k in calls) * PC + 60, f, R, Wr, cont=cont)
+
+    def at(x):
+        return lambda T: ap(T, x)
+
+    def sl(name, lo, hi, step):
+        return lambda T: T[name][:, lo:hi:step]
 
     def mm(out, *pairs):
-        def f(g, T, e):
-            r = None
-            for k, (l, x) in enumerate(pairs):
-                r = g.tensor.matmul(ap(T, out), ap(T, l), ap(T, x), k == 0, k == len(pairs) - 1)
-            return r
-        return add("T", len(pairs) * max(out[2] - out[1], 64) * PC + 60, f, [p[0] for p in pairs] + [p[1] for p in pairs], [out])
+        n = max(wd(out), 64)
+        return pe([(n, at(out), at(l), at(x), k == 0, k == len(pairs) - 1) for k, (l, x) in enumerate(pairs)],
+                  [p[0] for p in pairs] + [p[1] for p in pairs], [out])
+
+    def feats(bank, base, w, src, first, last, tiles=range(8), step=8):
+        nf = wd(w) // 8
+        calls = []
+        for jl in tiles:
+            l = sl(src[0], src[1] + jl, src[2], 8) if step == 8 else sl(src[0], src[1] + 128 * jl, src[1] + 128 * jl + 128, 1)
+            calls.append((64, sl(bank, base + jl, base + 64 * nf, 8), l, at(w), first, last and (first or jl == tiles[-1])))
+        return calls
+
+    def pad(n):
+        return (n, 0, 136, lambda T: T[n][:, 1::2, :], 64)
+
+    def whole(n):
+        return (n, 0, 136, lambda T: T[n][:, :, :], 136)
+
+    def turn(out, x, f=None):
+        n = wd(out)
+        calls = []
+        for src, idn, cy in ((x, "identf", 256), (f, "ik", 64)):
+            if src:
+                calls.append([cy, at(out), lambda T, s=src: T[s][:, 0:16, :], sl(idn, 1, 2 * n, 2), False, False])
+                calls.append([cy, at(out), lambda T, s=src: T[s][:, 1:17, :], sl(idn, 0, 2 * n, 2), False, False])
+        calls[0][4] = True
+        calls[-1][5] = True
+        return pe(calls, [whole(x), full("identf")] + ([whole(f), full("ik")] if f else []), [out])
 
     def gi(out, pattern, base, cm, flag):
         def f(g, T, e):
             if flag:
                 return g.iota(ap(T, out), pattern, base, cm, allow_small_or_imprecise_dtypes=True)
             return g.iota(ap(T, out), pattern, base, cm)
-        return add("G", 130 + (out[2] - out[1]) * 2 * VC, f, [], [out])
+        return add("G", 130 + wd(out) * 2 * VC, f, [], [out])
 
     def gs(out, a, pattern, op, base, cm):
-        return add("G", 170 + 2 * VC * (out[2] - out[1]),
+        return add("G", 170 + 2 * VC * wd(out),
                    lambda g, T, e: g.affine_select(ap(T, out), ap(T, a), pattern, op, 0.0, base, cm), [a], [out])
 
     def full(n):
@@ -159,6 +193,10 @@ def graph():
     def c_(n, c, lo=0, hi=None):
         w = SCRATCH[n][1][1] // NC
         return (n, c * w + lo, c * w + (w if hi is None else hi))
+
+    def col(n):
+        k = COLS.setdefault(n, len(COLS))
+        return ("col", k, k + 1)
 
     def ldq(c, s, q):
         a = c * CH + 128 * s
@@ -172,158 +210,234 @@ def graph():
         for s in range(8):
             ldq(c, s, "S" if c == 0 and s >= 4 else "Y")
         if c == 0:
-            add("S", 60, lambda g, T, e: g.scalar.dma_start(T.mk0[:, :], T.mk[:, :]), [], [full("mk0")], sem="lm0", inc=16,
-                lat=7000, pr=5e6)
-    add("Y", 60, lambda g, T, e: g.sync.dma_start(T.mk1[:, 0:W], T.mk[:, :]), [], [("mk1", 0, W)], sem="lm1", inc=16, lat=7000)
+            lm = add("S", 60, lambda g, T, e: g.scalar.dma_start(T.mk0[:, 0:W], T.mk[:, :]), [], [("mk0", 0, W)], sem="lm0", inc=16,
+                     lat=7000, pr=5e6)
+    add("Y", 60, lambda g, T, e: g.sync.dma_start(T.mk1[:, 0:W], T.mk[:, :]), [], [("mk1", 0, W)], sem="lm1", inc=16, lat=7000,
+        deps=(lm,))
 
+    cur[0] = "c"
+    idn = ("idw", 2, 130)
+    icol, m12 = col("i"), col("m12")
     gi(full("ip"), [[0, 1]], 0, 1, False)
     ms(full("ones"), 1.0)
     gs(full("z8a"), ("ones", 0, 8), [[-16, 8]], A.is_ge, 0, 1)
     gs(full("z8"), full("z8a"), [[16, 8]], A.is_ge, 15, -1)
     gs(full("idw"), full("ones"), [[1, 132]], A.is_equal, -2, -1)
+    gs(full("bda"), ("ones", 0, 128), [[-16, 8], [0, 16]], A.is_ge, 0, 1)
+    gs(full("bd"), full("bda"), [[16, 8], [0, 16]], A.is_ge, 15, -1)
     gi(full("mrow"), [[0, 4], [1, 16]], 0, 0, True)
     ts(full("i16"), full("ip"), 15, A.bitwise_and)
-    cp(full("icol"), full("i16"))
-    ms(full("bm"), 0.0)
-    add("V", 84, lambda g, T, e: g.vector.tensor_copy(T.bm[:, 15:128:16], T.z8[:, :]), [full("z8")], [full("bm")])
-    for n, op, v in (("m12", A.is_lt, 12.0), ("c12", A.is_equal, 12.0), ("c13", A.is_equal, 13.0), ("c14", A.is_equal, 14.0),
-                     ("ge13", A.is_ge, 13.0), ("ge14", A.is_ge, 14.0)):
-        ts(full(n), full("icol"), v, op)
+    cp(icol, full("i16"))
+    ts(col("i11"), icol, 11.0, A.min)
+    sa(("e3", 0, 1), col("i11"), F.Exp, scale=17 * LN2, bias=-100 * LN2, more=1300.0)
+    sa(("e3", 1, 2), col("i11"), F.Exp, scale=-17 * LN2, bias=64 * LN2)
+    for n, op, v in (("m12", A.is_lt, 12.0), ("c12", A.is_equal, 12.0), ("c13", A.is_equal, 13.0), ("c14", A.is_equal, 14.0)):
+        ts(col(n), icol, v, op)
+    z8 = full("z8")
+    ts(col("d0"), col("c12"), col("c13"), A.subtract)
+    ts(col("d1"), col("c13"), col("c14"), A.subtract)
+    for k, n in enumerate(("c12", "c13", "c14", "d0", "d1")):
+        ts(("wq", 8 * k, 8 * k + 8), z8, col(n), A.mult)
+    ts(col("k0"), icol, 0.0, A.is_gt, m12, A.mult)
+    ts(col("k1"), ("e3", 0, 1), col("k0"), A.mult, -255.0 * 2.0 ** -48, A.mult)
+    ts(full("dk1"), idn, col("k1"), A.mult)
+    ts(full("selm"), ("mrow", 0, 8), 8.0, A.add, icol, A.is_equal)
+    mm(("pe", 0, 128), (full("bd"), full("dk1")))
+    for jl in range(8):
+        if jl % 2:
+            ts(("lk", 128 * jl, 128 * jl + 128), ("pe", 0, 128), ("selm", jl, jl + 1), A.mult)
+    for jl in range(8):
+        if jl % 2 == 0:
+            sa(("lk", 128 * jl, 128 * jl + 128), ("pe", 0, 128), F.Copy, scale=("selm", jl, jl + 1))
+    cp(full("ident"), idn)
+    ts(full("i68"), idn, m12, A.mult, 2.0 ** -68, A.mult)
+    ts(col("zb"), col("c12"), col("c13"), A.add, 2.0 ** -68, A.mult)
+    for c in range(NC):
+        ms(whole("fx%d" % c), 0.0)
+        ms(c_("ra", c, 0, 128), 2.0 ** 29)
     cp(full("wtf"), full("wts"))
-    for k in range(3):
-        sm(full("WR%d" % k), full("bm"), full("c1%d" % (2 + k)))
-    sm(full("WX"), full("bm"), ("wtf", 0, 1))
-    sm(full("WY"), full("bm"), ("wtf", 1, 2))
-    cp(full("ident"), ("idw", 2, 130))
-    ts(full("nident"), ("idw", 2, 130), -1.0, A.mult)
-    ts(full("thv"), full("mrow"), full("icol"), A.is_gt, full("m12"), A.mult)
-    ts(full("ths"), full("thv"), 256.0, A.mult, -256.0, A.add)
-    sa(full("sil"), full("icol"), F.Silu, scale=-SL, bias=-SL)
-    ts(full("wc"), full("sil"), -1.5 * BIG, A.mult, full("m12"), A.mult)
-    sm(full("WE"), full("bm"), full("wc"))
-    ts(full("tha"), full("mrow"), 3.0, A.add, full("icol"), A.is_gt)
-    ts(full("thb"), full("mrow"), 0.0, A.is_gt, full("m12"), A.mult)
-    tt(full("th3"), full("tha"), full("thb"), A.mult)
+    ts(col("h13"), col("c13"), 0.5, A.mult)
+    ts(col("ca"), col("c12"), -2048.0, A.mult, col("h13"), A.add)
+    ts(col("cb"), col("c12"), -4096.0, A.mult, col("h13"), A.add)
+    for k, (w, x) in enumerate(((0, "ca"), (1, "ca"), (1, "cb"))):
+        ts(col("u%d" % k), ("wtf", w, w + 1), col(x), A.add, 2.0 ** 68, A.mult)
+        ts(("wu1", 8 * k, 8 * k + 8), z8, col("u%d" % k), A.mult)
+    for k in range(2):
+        ts(("wu2", 8 * k, 8 * k + 8), z8, ("wtf", k, k + 1), A.mult, -2.0 ** 68, A.mult)
+    ts(full("i97"), idn, 97.0, A.mult)
+    ts(full("n97"), idn, -97.0, A.mult)
+    cp(full("identf"), idn)
+    ts(full("ik"), idn, 2.0 ** -66, A.mult)
+    for c in range(NC):
+        ms(whole("xf%d" % c), 0.0)
+        ms(c_("ra", c, 448, 512), 0.0)
+        ms(c_("rb", c, 0, 128), 2.0 ** 29)
+        ms(c_("rb", c, 256, 320), 0.0)
+    ms(("mk0", W, W + 16), 2.0 ** 20)
+    ms(("mk1", W, W + 16), 2.0 ** 20)
+    cp(("wd0", 0, 16), ("wq", 0, 16))
+    cp(("wd1", 0, 8), ("wq", 0, 8))
+    ts(col("we"), ("e3", 1, 2), m12, A.mult)
+    ts(("wd0", 16, 24), z8, col("we"), A.mult)
+    ts(("wd1", 8, 16), z8, col("we"), A.mult)
+    ts(full("nident"), idn, -1.0, A.mult)
+    ms(whole("xk"), 0.0)
+    ms(whole("xa"), 0.0)
+
+    def learn_constants():
+        ts(col("th"), col("i11"), -3.0, A.add, 0.0, A.max)
+        sa(("e3", 2, 3), col("th"), F.Exp, scale=21 * LN2, bias=-102 * LN2)
+        ts(col("k3"), ("e3", 2, 3), m12, A.mult)
+        ts(full("dk3"), idn, col("k3"), A.mult)
+        mm(("pe", 128, 256), (full("bd"), full("dk3")))
+        for jl in range(8):
+            sa(("lp", 128 * jl, 128 * jl + 128), ("pe", 128, 256), F.Copy, scale=("selm", jl, jl + 1))
+        ts(full("ln"), full("lp"), -1.0, A.mult)
+        ts(full("i75"), idn, m12, A.mult, 2.0 ** -75, A.mult)
+        ts(full("n75"), idn, m12, A.mult, -2.0 ** -75, A.mult)
+        ts(full("f75"), idn, 2.0 ** -75, A.mult)
 
     def edit_constants():
         gi(full("trow"), [[0, 2], [1, 128]], 0, 0, True)
         gi(full("t16a"), [[0, 2], [16, 8]], 0, 0, True)
         gi(full("iot"), [[256, 8208]], 0, 0, True)
-        ts(full("t16"), full("t16a"), full("icol"), A.add)
-        ts(full("dump16"), full("t16"), 8192.0, A.add)
-        sm(full("isym"), ("idw", 2, 130), full("m12"))
-        sm(full("sh1"), ("idw", 3, 131), full("ge13"))
-        sm(full("sh2"), ("idw", 4, 132), full("ge14"))
+        ts(full("t16"), full("t16a"), icol, A.add)
+        ts(full("t16b"), full("t16"), 16.0, A.add)
+        ts(full("dump16"), full("t16"), 8208.0, A.add)
+        ts(col("ge13"), icol, 13.0, A.is_ge)
+        ts(col("ge14"), icol, 14.0, A.is_ge)
+        ts(full("isym"), idn, m12, A.mult)
+        ts(full("sh1"), ("idw", 3, 131), col("ge13"), A.mult)
+        ts(full("sh2"), ("idw", 4, 132), col("ge14"), A.mult)
         ts(full("sel1"), ("mrow", 0, 16), 2.0, A.is_equal)
         ts(full("sel2"), ("mrow", 0, 16), 1.0, A.is_equal)
-        sm(full("mt"), ("mrow", 0, 16), full("c12"))
-        ts(full("mid"), full("icol"), 15.0, A.is_lt)
-        tt(full("wcm"), full("mid"), full("m12"), A.subtract)
-        sm(full("spa"), ("idw", 1, 129), full("wcm"))
+        ts(full("mt"), ("mrow", 0, 16), col("c12"), A.mult)
+        ts(col("wcm"), icol, 15.0, A.is_lt, m12, A.subtract)
+        ts(full("spa"), ("idw", 1, 129), col("wcm"), A.mult)
         tt(full("spl"), full("spa"), full("isym"), A.add)
 
-    def under(rd, c, st, q):
-        ml = c_("ml", c)
-        if (rd, c, st) in Z_V:
-            tt(c_("zz", c), full("thv"), c_(q, c), A.mult, ind=ml)
-            return
-        for h in (0, 512):
-            sa(c_("rr", c, h, h + 512), full("ths"), F.Copy, ind=c_("ml", c, h // 16, h // 16 + 32))
-            mm(("pw%d" % c, 0, 512), (full("ident"), c_(q, c, h, h + 512)), (full("ident"), c_("rr", c, h, h + 512)))
-            sa(c_("zz", c, h, h + 512), ("pw%d" % c, 0, 512), F.Relu)
-
-    def diff(c, out, mk, q, ind, byS):
-        if not byS:
-            tt(out, mk, c_(q, c), A.subtract, ind=ind)
-            return
-        for h in (0, 512):
-            sa(c_("rr", c, h, h + 512), mk, F.Copy, ind=(ind[0], ind[1] + h // 16, ind[1] + h // 16 + 32))
-            mm(("pw%d" % c, 0, 512), (full("ident"), c_("rr", c, h, h + 512)), (full("nident"), c_(q, c, h, h + 512)))
-            sa((out[0], out[1] + h, out[1] + h + 512), ("pw%d" % c, 0, 512), F.Copy)
+    def flip(c):
+        fx, pw = "fx%d" % c, "pw%d" % c
+        pe([(128, at((pw, 0, 128)), lambda T: T[fx][:, 0:16, :], at(full("ident")), True, True)],
+           [whole(fx), full("ident")], [(pw, 0, 128)])
+        sa(c_("fts", c), (pw, 0, 128), F.Copy)
 
     def search(rd, c):
-        q = "qa" if rd == 0 else "qb"
-        mk = ("mk0" if rd == 0 else "mk1", 0, W)
-        pn, pw = "pn%d" % c, "pw%d" % c
-        u2, R0, R1, ky = (pn, 64, 128), (pn, 128, 192), (pn, 192, 256), (pn, 448, 512)
-        tA, tB = ("vp", c * 128, c * 128 + 64), ("vp", c * 128 + 64, c * 128 + 128)
-        hit = c_("hit", c)
-        rq = lambda k: c_("rq", c, NN * k, NN * k + NN)
+        q = c_("qa" if rd == 0 else "qb", c)
+        mk = ("mk0" if rd == 0 else "mk1", 0, W + 16)
+        pn, pw, fx, xf = "pn%d" % c, "pw%d" % c, "fx%d" % c, "xf%d" % c
+        ss, key = ("vp", c * 128, c * 128 + 64), ("vp", c * 128 + 64, c * 128 + 128)
+        hit, zz, dd = c_("hit", c), c_("zz", c), c_("dd", c)
+        kb = pad("xk") if c == 0 else c_("kb", c)
+        r = lambda k: c_("ra", c, 128 + 64 * k, 192 + 64 * k)
+        n2 = c_("rb", c, 192, 256)
         cur[0] = "%d%d0" % (rd, c)
-        pas((pn, 256, 320), "WR0", c_(q, c))
-        cp(c_("ml", c), (pn, 256, 320))
-        sa(rq(0), (pn, 256, 320), F.Copy)
+        pe(feats(pn, 0, full("wq"), q, True, True), [q, full("wq")], [(pn, 0, 320)])
+        sa(r(0), (pn, 0, 64), F.Copy)
+        sa(c_("ra", c, 192, 448), (pn, 64, 320), F.Copy)
         for st in range(S):
             cur[0] = "%d%d%d" % (rd, c, st)
-            m = rq(0) if st == 0 else c_("m%d" % (st + 1), c)
-            under(rd, c, st, q)
-            sa(c_("w97", c), m, F.Identity, scale=97.0)
-            sa(ky, m, F.Identity, scale=8192.0, bias=float((st + 1) << 17))
-            sa(c_("thr0", c), m, F.Silu, scale=-SL)
-            sa(c_("thr", c), c_("thr0", c), F.Abs, scale=BIG)
-            pas((pn, 0, 64), "WX", c_("zz", c))
-            pas(u2, "WY", c_("zz", c))
-            cp(c_("ui", c), (pn, 0, 128))
-            ts(c_("ac", c), c_("ui", c), 4095, A.bitwise_and)
-            tt(tA, u2, c_("w97", c), A.add)
-            tt(c_("pp", c), c_("ac", c, 0, NN), c_("ac", c, NN, 2 * NN), A.mult)
-            ts(c_("kk", c), c_("pp", c), 5, A.arith_shift_right)
-            tt(c_("ss", c), tA, c_("kk", c), A.add)
-            ts(c_("hi", c), c_("ss", c), W - 1, A.bitwise_and)
-            cp(c_("hl", c), c_("hi", c))
-            tt(ky, ky, c_("hi", c), A.add)
-            if rd == 0 and c == 0:
-                x8 = ("act", 8 * st, 8 * st + 8)
-                ts(x8, (m[0], m[1], m[1] + 8), 0.0, A.is_gt)
-                tt(("ka", 8 * st, 8 * st + 8), (pn, 448, 456), x8, A.mult)
-            diff(c, c_("dd", c), mk, q, c_("hl", c), (rd, c, st) in D_S)
-            if st == 0:
-                for k in (1, 2):
-                    pas((pn, 256 + 64 * k, 320 + 64 * k), "WR%d" % k, c_(q, c))
-                sa(c_("rq", c, NN, 3 * NN), (pn, 320, 448), F.Copy)
-                tt(c_("xx", c), (pn, 256, 384), c_("rq", c, NN, 3 * NN), A.subtract)
-            pas((pw, 0, 64), "WE", c_("dd", c))
-            if st < 2:
-                pas(R0, "WR0", c_("dd", c))
-            if st < 1:
-                pas(R1, "WR1", c_("dd", c))
-            sa((pw, 64, 128), (pw, 0, 64), F.Abs)
-            tt(hit, (pw, 64, 128), c_("thr", c), A.is_lt)
-            if st < 2:
-                nx = c_("m%d" % (st + 2), c)
-                if st == 0:
-                    x, old = c_("xx", c, 0, NN), rq(1)
+            mx = "ra" if st == 0 else "rb"
+            m = c_(mx, c, 128, 192)
+            sa(pad(fx), m, F.Exp, scale=-17 * LN2, bias=80 * LN2)
+            flip(c)
+            for h, bank in ((0, pn), (1, pw)):
+                calls = []
+                for jl in range(4 * h, 4 * h + 4):
+                    o = (bank, 128 * (jl % 4), 128 * (jl % 4) + 128)
+                    calls.append((128, at(o), at(full("i68")), sl(q[0], q[1] + jl, q[2], 8), True, False))
+                    calls.append((128, at(o), at(("lk", 128 * jl, 128 * jl + 128)), at(c_("fts", c)), False, True))
+                pe(calls, [q, full("i68"), ("lk", 512 * h, 512 * h + 512), c_("fts", c)], [(bank, 0, 512)])
+                if (rd, c, st, h) in Z_V:
+                    ts(c_("zz", c, 512 * h, 512 * h + 512), (bank, 0, 512), col("zb"), A.add, 0.0, A.max)
                 else:
-                    x, old = c_("x2", c), c_("n2", c)
-                    tt(x, rq(0), old, A.subtract)
-                tt(tB, R0, x, A.add)
-                tt(tB, tB, hit, A.mult)
-                tt(nx, tB, old, A.add)
-                cp(c_("ml", c), nx)
+                    sa(c_("zz", c, 512 * h, 512 * h + 512), (bank, 0, 512), F.Relu, bias=col("zb"))
+            ky = (pw, 0, 64)
+            sa(ky, m, F.Identity, scale=8192.0, bias=float((st + 1) << 18))
+            u = (pn, 0, 192)
+            k = pe([(192, at(u), at(full("i97")), at(c_(mx, c, 0, 192)), True, False)]
+                   + feats(pn, 0, full("wu1"), zz, False, False, range(4), 1),
+                   [full("i97"), c_(mx, c, 0, 192), full("wu1"), c_("zz", c, 0, 512)], [u])
+            pe(feats(pn, 0, full("wu1"), zz, False, False, range(4, 8), 1)
+               + [(128, at((pn, 0, 128)), at(full("n97")), at(c_(mx, c, 0, 128)), False, False)]
+               + feats(pn, 0, full("wu2"), zz, False, True, range(8), 1),
+               [full("n97"), full("wu1"), full("wu2"), zz], [u], cont=k)
+            sa(c_("cs", c), (pn, 64, 128), F.Copy)
+            tt(c_("pp", c), (pn, 0, 64), c_("cs", c), A.mult)
+            ts(c_("kk", c), c_("pp", c), 5, A.arith_shift_right)
+            tt(ss, (pn, 128, 192), c_("kk", c), A.add)
+            ts(c_("tt", c), ss, M13, A.add, M13, A.subtract)
+            tt(pad(xf), ss, c_("tt", c), A.subtract)
+            turn((pn, 192, 256), xf, fx)
+            ts(c_("hl", c), (pn, 192, 256), HALF, A.add, float(W), A.min)
+            tt(key, ky, pad(xf), A.add)
+            if rd == 0 and c == 0:
+                ts(full("act"), m, 0.0, A.is_gt)
+                if st == 0:
+                    tt(pad("xa"), key, full("act"), A.mult)
+                else:
+                    tt(("vp", 384, 448), key, full("act"), A.mult)
+                    tt(pad("xa"), ("vp", 384, 448), pad("xa"), A.max)
+            tt(dd, mk, q, A.subtract, ind=c_("hl", c))
             if st == 0:
-                tt(c_("kb", c), ky, hit, A.mult)
-                tt(tA, R1, c_("xx", c, NN, 2 * NN), A.add)
-                tt(tA, tA, hit, A.mult)
-                tt(c_("n2", c), tA, rq(2), A.add)
+                o, x = (pn, 256, 448), c_("ra", c, 320, 512)
+                pe([(192, at(o), at(full("ident")), at(x), True, False)] + feats(pn, 256, full("wd0"), dd, False, True),
+                   [full("ident"), x, full("wd0"), dd], [o])
+            elif st == 1:
+                o, x = (pn, 256, 384), c_("rb", c, 192, 320)
+                pe([(128, at(o), at(full("nident")), at(x), True, False),
+                    (64, at((pn, 256, 320)), at(full("ident")), at(r(0)), False, False)]
+                   + feats(pn, 256, full("wd1"), dd, False, True), [full("ident"), full("nident"), x, r(0), full("wd1"), dd], [o])
             else:
-                tt(tA, ky, hit, A.mult)
-                tt(c_("kb", c), tA, c_("kb", c), A.max)
+                o = (pn, 256, 320)
+                pe(feats(pn, 256, ("wd1", 8, 16), dd, True, True), [full("wd1"), dd], [o])
+            sa((pn, 448, 512), (pn, o[2] - 64, o[2]), F.Abs)
+            tt(hit, (pn, 448, 512), pad(fx), A.is_lt)
+            if st < 2:
+                tt(ss, (pn, 256, 320), hit, A.mult)
+                tt(c_("rb", c, 128, 192), ss, r(1) if st == 0 else n2, A.add)
+            if st == 0:
+                tt(ss, (pn, 320, 384), hit, A.mult)
+                tt(n2, ss, r(2), A.add)
+                tt(kb, key, hit, A.mult)
+            else:
+                tt(key, key, hit, A.mult)
+                tt(kb, key, kb, A.max)
 
     def learn(rd, c):
-        q = "qa" if rd == 0 else "qb"
+        qn = "qa" if rd == 0 else "qb"
         nw = "nwa" if rd == 0 else "nwb"
-        mk = ("mk0" if rd == 0 else "mk1", 0, W)
+        mk = ("mk0" if rd == 0 else "mk1", 0, W + 16)
+        pn, pw, fx, xf = "pn%d" % c, "pw%d" % c, "fx%d" % c, "xf%d" % c
+        kb = pad("xk") if c == 0 else c_("kb", c)
+        ta = ("vp", c * 128, c * 128 + 64)
         cur[0] = "%d%d3" % (rd, c)
-        cp(c_("ki", c), c_("kb", c))
-        ts(c_("bi", c), c_("ki", c), W - 1, A.bitwise_and)
-        cp(c_("bl", c), c_("bi", c))
-        diff(c, c_("ld", c), mk, q, c_("bl", c), (rd, c) in L_S)
-        ts(c_("mbi", c), c_("ki", c), 13, A.arith_shift_right)
-        cp(c_("mbl", c), c_("mbi", c))
-        for h in (0, 512):
-            tt(c_("lm", c, h, h + 512), full("th3"), c_("ld", c, h, h + 512), A.mult, ind=c_("mbl", c, h // 16, h // 16 + 32))
-            mm(("pw%d" % c, 0, 512), (full("ident"), c_(q, c, h, h + 512)), (full("ident"), c_("lm", c, h, h + 512)))
-            sa(c_(nw, c, h, h + 512), ("pw%d" % c, 0, 512), F.Copy)
+        ts(ta, kb, M13, A.add, M13, A.subtract)
+        tt(pad(xf), kb, ta, A.subtract)
+        turn((pn, 192, 256), xf)
+        ts(c_("bl", c), (pn, 192, 256), HALF, A.add, float(W), A.min)
+        if (rd, c) in L_V:
+            tt(c_("ld", c), mk, c_(qn, c), A.subtract, ind=c_("bl", c))
+        else:
+            sa(c_("ld", c), mk, F.Copy, ind=c_("bl", c))
+        ts(c_("tt", c), kb, M18, A.add, M18, A.subtract)
+        tt(c_("mb8", c), ta, c_("tt", c), A.subtract)
+        sa(pad(fx), c_("mb8", c), F.Exp, scale=-21 * LN2 / 8192, bias=60 * LN2)
+        flip(c)
+        if rd == 1:
+            blocks(c)
+        for h, bank in ((0, pn), (1, pw)):
+            o, qh, lh = (bank, 0, 512), c_(qn, c, 512 * h, 512 * h + 512), c_("ld", c, 512 * h, 512 * h + 512)
+            calls = [(512, at(o), at(full("i75")), at(lh), True, False)]
+            if (rd, c) not in L_V:
+                calls.append((512, at(o), at(full("n75")), at(qh), False, False))
+            for l in ("lp", "ln"):
+                for jl in range(8):
+                    calls.append((64, sl(bank, jl, 512, 8), at((l, 128 * jl, 128 * jl + 128)),
+                                  at(c_("fts", c, 64 * h, 64 * h + 64)), False, False))
+            calls.append((512, at(o), at(full("f75")), at(qh), False, True))
+            pe(calls, [qh, lh, full("i75"), full("n75"), full("f75"), full("lp"), full("ln"), c_("fts", c)], [o])
+            sa(c_(nw, c, 512 * h, 512 * h + 512), o, F.Relu, scale=2.0 ** 75, bias=-2.0 ** -10)
 
     def move(c):
         def f(g, T, e):
@@ -354,22 +468,21 @@ def graph():
         acc["qb"].append((k, "Y", c * CH, c * CH + CH, True))
 
     def edits():
-        e8 = lambda n: c_(n, 0, 0, 8)
         a8 = lambda n, k: (n, 8 * k, 8 * k + 8)
-        tt(full("kam"), a8("ka", 0), a8("ka", 1), A.max)
-        tt(full("kam"), full("kam"), a8("ka", 2), A.max)
-        cp(full("kai"), full("kam"))
-        ts(full("fi"), full("kai"), W - 1, A.bitwise_and)
-        ts(full("mfi"), full("kai"), 13, A.arith_shift_right, 15, A.bitwise_and)
-        ts(full("sbi"), e8("ki"), 17, A.arith_shift_right)
+        bl = ("bl", 0, 8)
+        turn(("pe", 256, 264), "xa")
+        turn(("pe", 264, 272), "xk")
+        ts(full("k2"), ("pe", 256, 272), HALF, A.add)
+        ts(full("fb"), full("k2"), W - 1, A.bitwise_and)
+        ts(full("mfi"), a8("k2", 0), 13, A.arith_shift_right, 15, A.bitwise_and)
+        ts(full("sbi"), a8("k2", 1), 18, A.arith_shift_right)
         cp(full("sbl"), full("sbi"))
         cp(full("mfl"), full("mfi"))
-        tt(full("ed1"), full("kam"), e8("kb"), A.is_gt)
-        ts(full("ed0"), e8("kb"), 0.0, A.is_gt)
+        tt(full("ed1"), a8("k2", 0), a8("k2", 1), A.is_gt)
+        ts(full("ed0"), a8("k2", 1), 8192.0, A.is_gt)
         for k in (0, 1):
             tt(a8("ed", k), full("ed1"), full("ed0"), A.mult)
-        ts(a8("fbm", 0), full("fi"), -8192.0, A.add)
-        ts(a8("fbm", 1), e8("bi"), -8192.0, A.add)
+        ts(full("fbm"), full("fb"), -8192.0, A.add)
         tt(full("fbe"), full("fbm"), full("ed"), A.mult)
         ts(full("flu"), full("fbe"), 8192.0, A.add)
         ts(full("nb"), full("fbe"), -256.0, A.mult, -2097152.0, A.add)
@@ -380,28 +493,29 @@ def graph():
             add("V", vdur(n), lambda g, T, e, k=k, n=n: g.vector.tensor_reduce(
                 T.first[:, k:k + 1], T.dk[:, 128 * k:128 * k + n], AxisListType.X, A.min, apply_absolute_value=True),
                 [("dk", 128 * k, 128 * k + n)], [("first", k, k + 1)])
+        tt(full("gg"), full("fbm"), full("t16b"), A.subtract)
+        tt(full("gg"), full("gg"), full("ed"), A.mult)
         tt(full("win"), full("first"), full("t16"), A.is_equal)
-        tt(full("win"), full("win"), full("ed"), A.mult)
-        tt(full("gg"), full("fbm"), full("t16"), A.subtract)
         tt(full("gg"), full("gg"), full("win"), A.mult)
         tt(full("tgt"), full("gg"), full("dump16"), A.add)
         cp(full("tgu"), full("tgt"))
-        sa(full("g0"), ("mk0", 0, W), F.Copy, ind=e8("bl"))
+        sa(full("g0"), ("mk0", 0, W + 16), F.Copy, ind=bl)
         tt(full("ga1"), full("sel1"), full("g0"), A.mult, ind=full("sbl"))
         tt(full("ga2"), full("sel2"), full("g0"), A.mult, ind=full("sbl"))
         mm(("pe", 0, 128), (full("sh1"), full("ga1")), (full("sh2"), full("ga2")), (full("isym"), ("qa", 0, 128)))
         sa(full("wnew"), ("pe", 0, 128), F.Copy)
         scat(full("mk1"), ("tgu", 0, 8), full("wnew"))
-        sa(full("g1"), ("mk1", 0, W), F.Copy, ind=e8("bl"))
+        sa(full("g1"), ("mk1", 0, W + 16), F.Copy, ind=bl)
         sa(full("mfw"), full("mt"), F.Copy, ind=full("mfl"))
         mm(("pe", 0, 128), (full("spl"), full("g1")), (full("ident"), full("mfw")))
         sa(full("snew"), ("pe", 0, 128), F.Copy)
         scat(full("mk1"), ("tgu", 8, 16), full("snew"))
 
     def blocks(c):
-        ts(c_("ybx", c), c_("kb", c), 0.0, A.is_equal, -1.0, A.mult)
-        add("V", vdur(64, 2), lambda g, T, e: g.vector.tensor_tensor(T.yby[:, :, 8 * c:8 * c + 8], ap(T, c_("ybx", c)),
-            ap(T, c_("bi", c)), A.add), [c_("ybx", c), c_("bi", c)], [("yby", 64 * c, 64 * c + 64)])
+        v, x = ("pn%d" % c, 192, 256), ("vp", c * 128 + 64, c * 128 + 128)
+        ts(c_("ybx", c), v, 0.0, A.is_equal, -HALF - 1.0, A.mult)
+        tt(x, v, c_("ybx", c), A.add)
+        ts(("yby", 64 * c, 64 * c + 64, lambda T: T.yby[:, :, 8 * c:8 * c + 8], 64), x, HALF, A.add)
         if c == NC - 1:
             add("Y", 60, lambda g, T, e: g.sync.dma_start(T.yb[:, :], T.yby[:, :, :]),
                 [("yby", 0, 192)], [], sem="lyb", inc=16, lat=2500)
@@ -416,6 +530,8 @@ def graph():
                     T.yq[:, 384 * s + 128 * c:384 * s + 128 * c + 128], T.nwb[:, a:a + 128])
             add(q, 60, f, [("nwb", a, a + 128)], [], sem="out%d" % c, inc=16, lat=2500)
 
+    cur[0] = "l"
+    learn_constants()
     for c in range(NC):
         search(0, c)
         learn(0, c)
@@ -427,7 +543,6 @@ def graph():
     for c in range(NC):
         search(1, c)
         learn(1, c)
-        blocks(c)
         store(c)
     return ops
 
@@ -445,6 +560,7 @@ def schedule(ops):
     tail = [0.0] * n
     for i in range(n - 1, -1, -1):
         tail[i] = ops[i]["dur"] + ops[i]["lat"] + max([tail[k] + WAKE for k in kids[i]] or [0.0])
+    prio = [tail[i] + ops[i]["pr"] + BIAS.get(ops[i]["tag"], 0.0) for i in range(n)]
     free, ready, est, done = {}, {}, [0.0] * n, [0.0] * n
     for i in range(n):
         ready.setdefault(ops[i]["q"], [])
@@ -460,7 +576,7 @@ def schedule(ops):
                 if best is None or t < best[0]:
                     best = (t, q)
         t, q = best
-        i = max((i for i in ready[q] if est[i] <= t), key=lambda i: (tail[i] + ops[i]["pr"] + BIAS.get(ops[i]["tag"], 0.0), -i))
+        i = max((i for i in ready[q] if est[i] <= t), key=lambda i: (prio[i], -i))
         ready[q].remove(i)
         free[q] = t + ops[i]["dur"]
         done[i] = free[q] + ops[i]["lat"]
@@ -497,6 +613,8 @@ def rank_program(g, core, T, topo):
         kn = known.setdefault(q, {})
         want = {}
         for d in o["deps"]:
+            if d == o["cont"]:
+                continue
             s, v = stamp[d]
             if kn.get(s, 0) < v:
                 want[s] = max(want.get(s, 0), v)

@@ -6,7 +6,7 @@ A = AluOpType
 F = ActivationFunctionType
 W, NC, CH, NN, S = 8192, 3, 1024, 64, 3
 LN2 = math.log(2.0)
-M13, M18 = 1.5 * 2.0 ** 36, 1.5 * 2.0 ** 41
+M12, M13, M18 = 1.5 * 2.0 ** 35, 1.5 * 2.0 ** 36, 1.5 * 2.0 ** 41
 HALF = 4095.5
 
 SCRATCH, BANKS = {}, []
@@ -21,33 +21,86 @@ def _b(dtype, where, spec, k=1):
 
 
 _b("bfloat16", "sbuf", "mk0:8208 mk1:8336 wts:2 ones:132 idw:132 ident:128 nident:128 i97:128 n97:128 i68:128 ik:128 i75:128 "
-   "n75:128 f75:128 bda:128 bd:128 dk1:128 dk3:128 lk:1024 lp:1024 ln:1024 e3:3 wu1:24 wu2:16 wq:40 wd0:24 wd1:16 "
+   "n75:128 f75:128 bda:128 bd:128 dk1:128 dk2:128 dk3:128 dk4:128 lk:1024 lp:1024 ln:1024 e3:3 wu1:40 wu2:16 wu3:24 cc:320 two:128 thv:16 th3:16 wq:40 wd0:24 wg:184 "
    "isym:128 sh1:128 sh2:128 spl:128 spa:128 z8a:8 z8:8 sel1:16 sel2:16 "
    "mt:16 g0:128 ga1:128 ga2:128 wnew:128 g1:128 mfw:128 snew:128")
-_b("int32", "sbuf", "ip:1 i16:1 k2:16 fb:16 mfi:8 sbi:8")
+_b("int32", "sbuf", "ip:1 i16:3 k2:16 fb:16 mfi:8 sbi:8")
 _b("uint16", "sbuf", "flu:16 tgu:16 sbl:8 mfl:8")
-_b("float32", "sbuf", "col:32 identf:128 selm:8 wtf:2 mrow:64 iot:8208 trow:256 "
+_b("float32", "sbuf", "col:40 identf:128 selm:16 wtf:2 mrow:64 iot:8208 trow:256 "
    "t16a:16 t16:16 t16b:16 dump16:16 act:64 ed1:8 ed0:8 ed:16 fbm:16 fbe:16 nb:16 krow:256 dk:2048 first:16 win:16 "
    "gg:16 tgt:16")
 SCRATCH["yby"] = ("sbuf", [128, 8, 24], "float32")
-for _n, _d in (("xf0", "float32"), ("xf1", "float32"), ("xf2", "float32"), ("xk", "float32"), ("xa", "float32"),
-               ("fx0", "bfloat16"), ("fx1", "bfloat16"), ("fx2", "bfloat16")):
-    SCRATCH[_n] = ("sbuf", [128, 17, 8], _d)
-_b("bfloat16", "sbuf", "qa:1024 qb:1024 zz:1024 dd:1024 ld:1024 nwa:1024 nwb:1024 ra:512 rb:320 fts:128 hit:64", NC)
-_b("float32", "sbuf", "cs:64 tt:64 kb:64 mb8:64 ybx:64", NC)
-_b("int32", "sbuf", "pp:64 kk:64", NC)
-_b("uint16", "sbuf", "hl:64 bl:64", NC)
+SCRATCH["qn"] = ("sbuf", [128, 8, 384], "bfloat16")
+PADS = {}
+for _n, _d, _l in (("padf", "float32", "xf0 xf1 xf2 xk0 xk1 xk2 xa"), ("padb", "bfloat16", "fx0 fx1 fx2 mp0 mp1 mp2 tp0 tp1 tp2")):
+    SCRATCH[_n] = ("sbuf", [128, 18 * len(_l.split()), 8], _d)
+    for _k, _x in enumerate(_l.split()):
+        PADS[_x] = (_n, 18 * _k)
+_b("bfloat16", "sbuf", "qa:1024 qb:1024 zz:1024 dd:1024 ld:1024 nwa:1024 nwb:1024 ra:320 rb:128 fts:128 hit:64 da:384", NC)
+_b("float32", "sbuf", "ta:128 tb:128 cs:64 ybx:64", NC)
+_b("int32", "sbuf", "pp:64 kk:64 ui:128 ac:128", NC)
+_b("uint16", "sbuf", "hl:64 bl:64 ml:64", NC)
 _b("float32", "psum", "pn0:512 pn1:512 pn2:512 pw0:512 pw1:512 pw2:512 vp:512 pe:512")
 
-SEMAPHORES = ["sT", "sV", "sS", "sG", "lw", "lm0", "lm1", "lyb"]
+SEMAPHORES = ["sT", "sV", "sS", "sG", "lw", "lq", "lm0", "lm1", "lyb"]
 for _c in range(NC):
-    SEMAPHORES += ["lq%d" % _c, "slf%d" % _c, "arr%d" % _c, "snt%d" % _c, "out%d" % _c]
+    SEMAPHORES += ["slf%d" % _c, "arr%d" % _c, "snt%d" % _c, "out%d" % _c]
 
-VC, PC, VG, VGS, OV, OS, WAKE = 0.9545, 0.48, 1.5, 1.5, 20.0, 60.0, 110.0
-BIAS = {'000': 140900, '001': -47100, '002': -127700, '003': 161800, '010': 4000, '011': -51400, '012': -46900, '013': -27700, '020': 1000, '021': 118100, '022': -24400, '023': 105800, '100': 47200, '101': -55800, '102': 87400, '103': -14200, '110': 13000, '111': 97800, '112': 23900, '113': -143600, '120': -41600, '121': 44000, '122': 12100, '123': -68100, 'c': 41800, 'e': -87600, 'k': -24900, 'l': -84200}
-Z_V = {(0, 1, 0, 0), (1, 0, 0, 0), (1, 0, 0, 1), (1, 0, 1, 1), (1, 0, 2, 0), (1, 1, 0, 1), (1, 2, 0, 1)}
-L_V = {(0, 2), (1, 1), (1, 2)}
+VC, PC, VG, VGS, OV, OS, WAKE = 1.016, 0.51, 1.56, 1.56, 30.0, 60.0, 120.0
+BIAS = {}
+SOFT = False
+from_plan = True
+Z_V = {(1,2,2,1),(0,0,2,1),(0,1,0,0),(1,1,1,0),(0,1,2,0),(1,2,0,0),(1,0,0,1),(1,2,1,0),(0,2,1,0)}
+L_V = {(1,2,1),(0,2,1),(1,0,1),(1,1,0),(0,1,0),(1,2,0),(0,2,0),(1,0,0),(0,0,1),(1,1,1),(0,1,1)}
+M_V = {(1,0,0),(0,1,2)}
+U_V = {(1,2,1),(0,2,1),(1,0,1),(1,1,0),(1,2,0),(0,2,0),(0,0,0),(1,1,2),(1,0,0),(1,2,2),(0,0,2),(0,1,2),(0,2,2),(1,0,2),(0,0,1),(1,1,1),(0,1,1)}
+U_S = {(1,0,1),(1,1,0),(0,2,0),(1,2,2),(0,2,2),(1,0,2),(0,0,1),(1,1,1)}
+D_S = {(1,1,0),(0,1,0),(1,1,2),(0,1,2),(0,2,2)}
+A_V = {(1,2,2,'c'),(0,1,1,'c'),(0,1,1,'y'),(1,1,0,'r'),(0,1,2,'c'),(1,0,2,'c'),(0,0,2,'c'),(1,2,1,'c'),(0,1,0,'r'),(1,1,0,'y'),(1,2,0,'m'),(1,0,0,'c'),(0,2,2,'c'),(0,1,0,'y'),(0,0,1,'c'),(1,2,0,'y'),(0,0,2,'y')}
+ORDER = "0001040517060<190;0=150>080O0?0A0B0D090C0L0F0E1107121:0:1K0H0G0J0I;20K1>0@1P0M130N1@1O0P1=1?0R0T0Q0S1G021L0W8>1H1A101M1E5O1C1B8?1F0U1D1T2W5P241I0V5Q5S308B5T2633218C1U5W8@1J1Q27253418285U161R601S2A20222?8F2F315V8A2;5R1V8D238G14612D1;3F2E628E2T1<2V632U;>;;;62<;<;=2=;98I;?64;7;88J29652:;:372>8K2G668H8L32678M3568388N698O2@8P6:2H368Q6<8T2I8R6;1W39;@3:8S1N6>2C036=8U3;2J3<2N6?2B2Q3=2M8V3>6@3?3@8W6A2L3A902P3B912O6B3C922R6C6E2K6D9793963D6I94983H6J996H9;9:3I9<6F3E9>3J952S9=6K;03K3G3L;16M3N6L3M3O6G3P4=;39?6N;4;56P9@3R9A3S6O6Q9B3Q3T9C9D9E9F6R3U9G9I6S6T3V9H6U9J413W4042439K6V446W45709L467173479M489N49729O4:749R9S9T9U4;9W4<9V4@:0:275:376:1:44A77:578:64B79:74C7<7=:84D:94E::4H4I9P4>:;7>4J4?9Q7@4F544M:<7?:>4K:?4N7A4L4G7B4P:=7C4Q4O7D:@4R7E4S:A7F4T7G4U7H:B4V7:4W7I:C50:D5351:E7J:F7L:L:G52:M:H557;567K7M:I:J;A:N:O7N57:P7O7P:K:Q5859:T7Q:R7R5:7S5;7T5<7U825=5C5>5D837V:S5E7W5?805F:U:W84;B855@81865A:V;C<P;J;D;I;M88;K87;L;F;N;G;O;P;Q8:5B5G89<H<J<R8;8=<8<I<4<Q<D<2<5<><K5I<3;T<95H<E8<<?;U;E<B;H5K<0<C<6<1;V<S<:;W5J<;<7BI<@5L5N<F<A;R<<BJ<T<GBM<=BL;SBN<LBK<MBQ5M<N<W<O<UBOBR<VBP=0BS=1BTBUBV?NBWC0?OC1?P?Q?R?SC2C3?TC4=2C5C7?U?VC6C8@1?W=3=4@2=5=7=6@3C9=8@4=:@0@5C:@6@7C;@8C<@9C=C>@:@<CAC?C@CB@;=9CC@>@=CDCFCE=;CG@?=<CHCI==@@CJ=>=?@A=@CK=A@B=BCL=C@C@E@DCM@H@I@F=DCN@J=F@M@K@NCO=G@L@OCP=H=E@PCQ=ICRCT=J=L=K=M@G=O=PCS@Q=N=QCU=T=R=U@RCV=S@S@TCW@U=W=VD0@V>0D1@WD2A0>1D5D6A3A1>2D7D3>3D8A2>4A4D:D9D=>5D;A5>6A6D4D>D<>7A7>8>:A8A:A9D?A<A=>9D@A>>;A?AAA@DA><A;ABDBDCADDD>=AEACDE>>DHDF>?>A>@AF>C>DDG>B>EDI>F>H>GAGDJ>IAH>KAIAJDK>L>JAKDLAL>MAMDM>NDN>ODO>PDPAN>QDQDUAP>RDV>SAQDRE1DT>TDW>UE2E0>WARE7ASDSATE8?0>VAOE5?1E>AUE=E3E?E@?2AV?3AW?4B0?5B6?6B1?;?7B7?<?=?8B2???>?:B8B9E6B3?@?DB5E:E<E9E;?9B??EB4?J?K?L?MB:?B?AB@B;B<E4BGBFBHBEB=?C?F?G?H?IB>BABBBDBC"
+Z_V = {(0,1,0,1),(0,2,0,1),(1,1,2,0),(0,1,2,1),(1,1,1,0),(0,0,0,0),(0,1,2,0),(1,0,1,0),(1,2,0,0),(0,0,1,1)}
+L_V = {(1,2,1),(0,2,1),(1,0,1),(1,1,0),(0,1,0),(1,2,0),(0,2,0),(0,0,0),(1,0,0),(1,1,1),(0,1,1)}
+M_V = {(1,0,0),(0,1,2)}
+U_V = {(1,2,1),(0,2,1),(1,0,1),(1,1,0),(0,1,0),(1,2,0),(0,2,0),(0,0,0),(1,1,2),(1,2,2),(0,0,2),(0,1,2),(0,2,2),(1,0,2),(0,0,1),(1,1,1),(0,1,1)}
+U_S = {(1,2,1),(1,1,0),(0,1,0),(0,2,0),(0,0,2),(0,2,2),(0,0,1),(1,1,1)}
+D_S = {(1,0,1),(0,2,0),(1,1,2),(1,2,2),(0,0,2),(0,2,2)}
+A_V = {(0,1,2,'y'),(1,0,0,'r'),(0,1,0,'c'),(0,1,0,'q'),(0,2,0,'q'),(0,0,0,'c'),(1,0,1,'c'),(1,2,2,'y'),(1,2,0,'c'),(1,0,0,'y'),(0,2,0,'c'),(1,2,0,'m'),(1,0,0,'c'),(1,1,1,'y'),(1,0,0,'m'),(0,0,1,'c'),(0,0,2,'y'),(1,2,1,'y')}
+ORDER = "00040708180>0?1<0;0@1:0A0E0D090B0G0O0F0:0R0H0<0L0J0M0I0K0=0N1;271514;50C170P;61=0Q1S1N0S1@240U0T0W0V1R050103028@1V103229131K16121T5T2B331U1A8A2:36281C5U8D1B371J601P111W3:1H341L1I1O268B1M20382;218E252D3;23193I2I8F395V8C1>8H2G8G2H;<;;2W1?3=61;>8I2?3>352>8K2<3?2@8L312A3@2=623<8M5W3A8J8N2J3B8O64633C8P3D8Q3E8R2C3F8S658T3G063H66678V8U3K8W9068693J916:2K6;3L;:926<2L6=2M303M6>;=932O3N6?2R3O6@942N3P953Q3T962U3U3R979;6A3V986C9<3W9:2P2T2Q41409?2S426B9=3S;49@4@;?;B99;C;@;7441D9>22451F;A;86D4643;99A479B1G6E489C6F496G4:9D4;9E4<9F4=6I9G6H9H6J6L6M9I4>6N9J4C6Q9K6R6O9L6S4?9N4D6P4E6T6U4F9M9O4G6K4H6V4L4A9P6W4M9Q704K4N9R719S724I9V734J4P744O4B77572V754Q9T1E9W9U764S2E:0784T:1:3:24U794R:44V2F4W:61Q7:50:7:5517;52:853:9547<::7=:;7@7A55:<565:5;:=58:>7B59:?:A;D7>;E:@7C:C:B5<7D7?7E5=:D7F7G5>:E7H5?7I:F5@7J5A7K;F:G5B:H5C:I5D5H:J7L5I:K7M:P5E:Q5F<T5J:L5K5G:R7N:M5L7P:S5N5M:N5P7O;G:O7Q5O:T;M;N7R;J5Q5S;H7S;O7T;P7U;Q7V;R:V7W:U;S;K5R;T;U;084<U<L<>85<N;V80<V:W<?86;W81<W<O8387;1;3<6<D<@<2<882<<8:<:<H;2<F<B<7<0<3<J<M<4<A<E=0<=88<G8;<I<C<9<;<1<K8=8?<5;I<P;L<Q89<R<S=1=7=38<=2=8=9=:=;=4=<=>=?===58>=6BM=@BNBOBPBQ=ABR=B=CBS=D=E=F=GBTBU=H=I=JC0BV?TBWC1?VC2=K?UC3?W@0C4=L@1C5=MC6@2=NC7=OC8=P=SC;=QC9=R@3@4C:C<@7@5=T=U@8@6@9C=@:@;>0C>@<@=C?@>=VC@>1CBCA@?CC@BCDCFCE=W@@CG>2CH@A@C>3CI>4CJ>5CK@D>6>7CM@ECN>8@F>9@G>:@H>;CO@L@M@I><>>@N@JCPCL@OCQ>=CR>?@KCS@QCTCU@PCVD0>@CW@RD1>A@T>B@U>C>D@VD2>E@S>F@W>J>GD3A0>KD4A1>ID5>NA2D6A3>HD9A4D7A7D:D8A5D;>OD>A6A8>P>LD?D<>MD@D=>Q>RA9>S>TDAA:>UDBA;>VDC>WA<?0A=?1A@DD?2?4DEA>DFAA?3DGAB?5AEACAFDHA??6AGDIADDJ?7?8DLAHDK?9AIDM?:DN?;AJ?<AK?=?AAL?BAM?>?CAN?EAO?D?FDOAP??AQDPAR?@DQATAU?HDRASDS?GDTDUE3DVE4DW?IAVE7E0E8?JE1?NAW?M?L?OE2E5B0E6E9?KB1E;B2B3?PB4?RB:?Q?SB5B;B6B<B>E=B7B=B?B8E<E@EAB9EBE?BAE>B@ECEFE:EEEDBCBBBEBHBFBGBDBLBIBKBJ"
+PICK = "110110101111001110010110000110011011010100110001111010111111001001100101011000100011101101010011010000000010010000111001111110001000101110000111000100011011111000001000000100000101111101111001000000000000000011101000010110000111001011111110000101001010000000100100100010000101010"
+ORDER = "000407081M090?0R0@0:0S0A0;0D0F0B0G1;0>0<1<0=0I0E0K0H0C0O;5170L0P0M1@1S0Q1A1Q0T0U0J0N0V1N1?2@1:05010302312032185N151613121935145O8A1B3336345R1E8B39118C1G5P5S1C8E230W1=5V1024255Q1J1R1H1D3:1I37261K1F1P1L1O5T271T388F28295W5U3<3=222;3>612<1U2:623?2=2>1W8I3@632B3A641>3B8G8J66653C672A3D688H2G692T6:3E2?2S6;2U8D;9;>063J;?;:3K6<;;8L6?8M8N3L21603;8O6=3M6@8P3F8Q6>6A8R3N3G8K6B2C8S;=3H6C2D3O;<6E6I3P;@6F3R3V8T6J3S8W3W6K6M6L426N6D3Q40438U2E3I6G2F906H413U446P916O6Q924A3T93;3958V45966R94466S99;498472H6T9:482I6U9;492K6V4:2M714;6W979<4<2P4?4=702O2J732L9=4>4@4D749@2Q752N9>4E76724F4B9A;69?4G779B4H9C4I789D4J799E4M4N4C557>9F4O9G7?4P4Q7B9H7C7@9I7:9L9M9J4K9K4L4R7;7D7<;74S;84T1V4U;A7A4V;B9N4W2V502W9O537E30547F7=569P7G57519Q9R7H9S52;D7I9T589W:0:12R:2:47J9U:37K599V7L7M7O5::57P5;:75<7N5=7Q:85>5C5?:9::7R5@5D5A;E5E7S5B:;;F5F:<;M:=;L:>;O7T;G;N;P;I:6:?;Q;J5G:A;R:B7U:@;S5H:C5J7V<M7W<N80;H8186;T82;K;C:D5I83:E85<A875M:F8488:G<;8;<K<9<S:H<B;W:I<55K:J<E<0<C89:K:P8<<U<<<F<1<T5L8>8@;U<?<L<3:L;V8:<@<D<4:Q:M<V<6:R:N8=<7<I<G<=<W:O=2:S8?<8<2<J:U<H:T<><:<O<P:W<Q<R:V=0=1;0;2=3=6=4=5=7;1=8=:=;=9=<=>===?=A@5=@=B@6@7@9=C@:=D@8@;=E=F=G@=@<=H=K=I@>@@=J=L@?BQ@ABRBS@BBU=NBV@C=M@DBW@E@FC1@GC0@H@J@KC2=O@I@LC4=PC5BTC3=Q=RC6@M=SC7=V=TC8=W@NC9=U>0C:>1>2@OC=C;@P>3@RC>@S@VC<>6@T@WC?>4A2>5A0>7A3>9@QA1>:C@>;@U><A5CAA6>8>=A4CB>>CC>?CECI>@CFCDCJ>AA7CH>CA8CK>BA9>E>DA:CMCGA;A<CLA=A?>FA>A@AACPCN>G>HCQCO>ICR>JABCS>KCT>M>PACCU>N>QCVADCWD1AE>LAFAJ>OD0AI>RAGAKD3AL>S>TAMAND2>UAH>WAO>V?0D4?1APAQ?2D5AR?3D6?4D7?5D9D<?6ASD8D=?7AT?9D;AU?:D>?8AVD:?;AWD@D?B0B2B3?<B1DCB4DA?=?>DDDB??DE?@DFB5?ADG?BDHB6?CB7?DDIB8?HB9DJ?EB:B??GDL?IDKB@DM?J?F?KB;?LDNDOB<?P?SB>BADPB=BGDQ?TBB?MBC?NDRBD@3BH@4?O@2BE@1DSDTDUBOBNBMBPDVE3DWBF?QE0E6E1BIBKBJE4BLE5?RE7E2E:?V?W@0?UE8E9E<E;E@E>EAE?E=ECEEEBED"
+_R2 = [(r, c) for r in range(2) for c in range(NC)]
+_R3 = [k + (s,) for k in _R2 for s in range(S)]
+OPTS = ([("Z_V", k + (h,)) for k in _R3 for h in range(2)] + [(n, k + (h,)) for n in ("L_V", "L_M") for k in _R2 for h in range(2)]
+        + [(n, k) for n in ("M_V", "U_V", "U_S", "D_S") for k in _R3] + [("A_V", k + (x,)) for k in _R3 for x in "yc"]
+        + [("A_V", k + (0, x)) for k in _R2 for x in "mr"] + [("A_V", (0, c, 0, "q")) for c in range(NC)]
+        + [("A_V", (1, c, 0, "b")) for c in range(NC)] + [("A_V", k + (h, "e")) for k in _R2 for h in range(2)]
+        + [("A_V", k + ("a",)) for k in _R3 if k[2] < 2] + [("A_V", ("k", i)) for i in range(1, 70)])
+SETS = {n: set() for n, _ in OPTS}
+for _c, (_n, _k) in zip(PICK, sorted(OPTS, key=repr)):
+    if _c == "1":
+        SETS[_n].add(_k)
+Z_V, L_V, L_M, M_V, U_V, U_S, D_S, A_V = [SETS[n] for n in ("Z_V", "L_V", "L_M", "M_V", "U_V", "U_S", "D_S", "A_V")]
 COLS = {}
+
+
+RANK = [0]
+
+
+def half(h):
+    return h ^ 1 ^ (RANK[0] // 4)
+
+
+def lanes(T, topo, rank, h):
+    core, out = T.cores[rank], {}
+    dst = [s for s in range(4 * h, 4 * h + 4) if s != rank]
+    far = [s for s in dst if topo.chip(T.cores[s]) != topo.chip(core)]
+    for k, s in enumerate(far):
+        en = topo.engines(core, T.cores[s])
+        out[s] = en[k::len(far)]
+    for s in dst:
+        if s not in far:
+            out[s] = topo.engines(core, T.cores[s])[-4:]
+    return out
 
 
 def graph():
@@ -55,24 +108,30 @@ def graph():
 
     def add(q, dur, fn, R, Wr, sem=None, inc=1, lat=0.0, deps=(), pr=0.0, cont=None):
         i = len(ops)
-        d = set(deps)
+        d, soft = set(deps), set([cont] if cont is not None else [])
         for lst, isw in ((R, False), (Wr, True)):
             for x in lst:
                 b, lo, hi = x[:3]
                 for (k, kq, klo, khi, kw) in acc.get(b, []):
                     if lo < khi and klo < hi and (isw or kw):
-                        d.add(k)
+                        (soft if SOFT and isw and kq == q and sem is None and ops[k]["sem"] is None else d).add(k)
                     elif b in BANKS and kq != q:
                         d.add(k)
         for lst, isw in ((R, False), (Wr, True)):
             for x in lst:
                 b, lo, hi = x[:3]
                 old = acc.setdefault(b, [])
+                if b in BANKS and old and old[-1][1] != q:
+                    k = len(old)
+                    while k and old[k - 1][1] == old[-1][1]:
+                        k -= 1
+                    del old[:k]
                 if isw and b not in BANKS:
                     old[:] = [y for y in old if y[0] == i or not (lo <= y[2] and y[3] <= hi)]
                 old.append((i, q, lo, hi, isw))
-        ops.append({"q": q, "dur": dur, "fn": fn, "deps": d, "sem": sem, "inc": inc, "lat": lat, "pr": pr, "tag": cur[0],
-                    "cont": cont})
+        d.discard(cont)
+        ops.append({"q": q, "dur": dur, "fn": fn, "deps": d | soft, "sem": sem, "inc": inc, "lat": lat, "pr": pr, "tag": cur[0],
+                    "soft": soft - d})
         return i
 
     def ap(T, x):
@@ -132,6 +191,11 @@ def graph():
             return g.scalar.activation(ap(T, out), src, func, bias=ap(T, bias) if isinstance(bias, tuple) else bias, scale=sc)
         return add("S", more + ((65 + n * VGS * VC) if ind else (max(64.0, n) * VC + OS)), f, R, [out])
 
+    def un(out, a, scale, bias, key):
+        if key in A_V:
+            return ts(out, a, scale, A.mult, bias, A.add)
+        return sa(out, a, F.Identity, scale=scale, bias=bias)
+
     def pe(calls, R, Wr, cont=None):
         def f(g, T, e):
             r = None
@@ -155,26 +219,42 @@ def graph():
         nf = wd(w) // 8
         calls = []
         for jl in tiles:
-            l = sl(src[0], src[1] + jl, src[2], 8) if step == 8 else sl(src[0], src[1] + 128 * jl, src[1] + 128 * jl + 128, 1)
-            calls.append((64, sl(bank, base + jl, base + 64 * nf, 8), l, at(w), first, last and (first or jl == tiles[-1])))
+            if len(src) == 2:
+                l = at(qv(src[0], src[1], None, jl))
+            else:
+                l = sl(src[0], src[1] + jl, src[2], 8) if step == 8 else sl(src[0], src[1] + 128 * jl, src[1] + 128 * jl + 128, 1)
+            calls.append((64, sl(bank, base + jl, base + 64 * nf, 8), l, at(w), first and jl == tiles[0], last and jl == tiles[-1]))
         return calls
 
     def pad(n):
-        return (n, 0, 136, lambda T: T[n][:, 1::2, :], 64)
+        b, k = PADS[n]
+        return (b, 8 * k, 8 * k + 144, lambda T: T[b][:, k + 1:k + 17:2, :], 64)
 
-    def whole(n):
-        return (n, 0, 136, lambda T: T[n][:, :, :], 136)
+    def win(n, a):
+        b, k = PADS[n]
+        return lambda T: T[b][:, k + a:k + a + 16, :]
 
-    def turn(out, x, f=None):
+    def top(x):
+        return x[:3] + (lambda T: T[x[0]][0:64, x[1]:x[2]], x[2] - x[1])
+
+    def turn(out, *srcs):
         n = wd(out)
         calls = []
-        for src, idn, cy in ((x, "identf", 256), (f, "ik", 64)):
-            if src:
-                calls.append([cy, at(out), lambda T, s=src: T[s][:, 0:16, :], sl(idn, 1, 2 * n, 2), False, False])
-                calls.append([cy, at(out), lambda T, s=src: T[s][:, 1:17, :], sl(idn, 0, 2 * n, 2), False, False])
+        for src, idn in srcs:
+            cy = 256 if idn == "identf" else 64
+            calls.append([cy, at(out), win(src, 0), sl(idn, 1, 2 * n, 2), False, False])
+            calls.append([cy, at(out), win(src, 1), sl(idn, 0, 2 * n, 2), False, False])
         calls[0][4] = True
         calls[-1][5] = True
-        return pe(calls, [whole(x), full("identf")] + ([whole(f), full("ik")] if f else []), [out])
+        return pe(calls, [pad(s) for s, _ in srcs] + [full(i) for _, i in srcs], [out])
+
+    nk = [0]
+
+    def sc(out, a, x, y=1.0):
+        nk[0] += 1
+        if ("k", nk[0]) in A_V or y != 1.0:
+            return ts(out, a, x, A.mult, y, A.mult)
+        return sa(out, a, F.Copy, scale=x)
 
     def gi(out, pattern, base, cm, flag):
         def f(g, T, e):
@@ -198,20 +278,21 @@ def graph():
         k = COLS.setdefault(n, len(COLS))
         return ("col", k, k + 1)
 
-    def ldq(c, s, q):
-        a = c * CH + 128 * s
+    def qv(rd, c, h=None, jl=None):
+        n = "qb" if rd else "qa"
+        if jl is not None:
+            return (n, c * CH, c * CH + CH, sl(n, c * CH + jl, c * CH + CH, 8), 128)
+        return c_(n, c) if h is None else c_(n, c, 512 * h, 512 * h + 512)
 
-        def f(g, T, e):
-            return (g.sync if q == "Y" else g.scalar).dma_start(T.qa[:, a:a + 128], T.qs[:, 384 * s + 128 * c:384 * s + 128 * c + 128])
-        add(q, 60, f, [], [("qa", a, a + 128)], sem="lq%d" % c, inc=16, lat=2500, pr=1e7 - c * 1e4)
-
-    add("Y", 60, lambda g, T, e: g.sync.dma_start(T.wts[:, :], T.wt[:, :]), [], [full("wts")], sem="lw", inc=16, lat=2000, pr=5e7)
+    k = add("Y", 60, lambda g, T, e: g.sync.dma_start(T.qn[:, :, :], T.qs[:, :]), [], [("qn", 0, 3 * CH)], sem="lq", inc=16,
+            lat=3500, pr=6e7)
     for c in range(NC):
-        for s in range(8):
-            ldq(c, s, "S" if c == 0 and s >= 4 else "Y")
-        if c == 0:
-            lm = add("S", 60, lambda g, T, e: g.scalar.dma_start(T.mk0[:, 0:W], T.mk[:, :]), [], [("mk0", 0, W)], sem="lm0", inc=16,
-                     lat=7000, pr=5e6)
+        cur[0] = "0%d0" % c
+        un(c_("qa", c), ("qn", 0, 3 * CH, lambda T, c=c: T.qn[:, :, 128 * c:128 * c + 128], CH), 1.0, 0.0, (0, c, 0, "q"))
+    cur[0] = ""
+    add("S", 60, lambda g, T, e: g.scalar.dma_start(T.wts[:, :], T.wt[:, :]), [], [full("wts")], sem="lw", inc=16, lat=2000, pr=5e7)
+    lm = add("Y", 60, lambda g, T, e: g.sync.dma_start(T.mk0[:, 0:W], T.mk[:, :]), [], [("mk0", 0, W)], sem="lm0", inc=16,
+             lat=8000, pr=5e6, cont=k)
     add("Y", 60, lambda g, T, e: g.sync.dma_start(T.mk1[:, 0:W], T.mk[:, :]), [], [("mk1", 0, W)], sem="lm1", inc=16, lat=7000,
         deps=(lm,))
 
@@ -226,8 +307,8 @@ def graph():
     gs(full("bda"), ("ones", 0, 128), [[-16, 8], [0, 16]], A.is_ge, 0, 1)
     gs(full("bd"), full("bda"), [[16, 8], [0, 16]], A.is_ge, 15, -1)
     gi(full("mrow"), [[0, 4], [1, 16]], 0, 0, True)
-    ts(full("i16"), full("ip"), 15, A.bitwise_and)
-    cp(icol, full("i16"))
+    ts(("i16", 0, 1), full("ip"), 15, A.bitwise_and)
+    cp(icol, ("i16", 0, 1))
     ts(col("i11"), icol, 11.0, A.min)
     sa(("e3", 0, 1), col("i11"), F.Exp, scale=17 * LN2, bias=-100 * LN2, more=1300.0)
     sa(("e3", 1, 2), col("i11"), F.Exp, scale=-17 * LN2, bias=64 * LN2)
@@ -237,65 +318,86 @@ def graph():
     ts(col("d0"), col("c12"), col("c13"), A.subtract)
     ts(col("d1"), col("c13"), col("c14"), A.subtract)
     for k, n in enumerate(("c12", "c13", "c14", "d0", "d1")):
-        ts(("wq", 8 * k, 8 * k + 8), z8, col(n), A.mult)
+        sc(("wq", 8 * k, 8 * k + 8), z8, col(n))
     ts(col("k0"), icol, 0.0, A.is_gt, m12, A.mult)
     ts(col("k1"), ("e3", 0, 1), col("k0"), A.mult, -255.0 * 2.0 ** -48, A.mult)
-    ts(full("dk1"), idn, col("k1"), A.mult)
-    ts(full("selm"), ("mrow", 0, 8), 8.0, A.add, icol, A.is_equal)
-    mm(("pe", 0, 128), (full("bd"), full("dk1")))
+    sc(full("dk1"), idn, col("k1"))
+    ts(("i16", 2, 3), full("ip"), 7, A.bitwise_and)
+    cp(col("i8"), ("i16", 2, 3))
+    ts(("selm", 8, 16), ("mrow", 0, 8), col("i8"), A.is_equal)
+    pe([(128, at(top(("pe", 0, 128))), sl("bd", 0, 128, 2), at(full("dk1")), True, True)], [full("bd"), full("dk1")], [("pe", 0, 128)])
+    sc(top(full("dk2")), top(("pe", 0, 128)), 1.0)
     for jl in range(8):
-        if jl % 2:
-            ts(("lk", 128 * jl, 128 * jl + 128), ("pe", 0, 128), ("selm", jl, jl + 1), A.mult)
-    for jl in range(8):
-        if jl % 2 == 0:
-            sa(("lk", 128 * jl, 128 * jl + 128), ("pe", 0, 128), F.Copy, scale=("selm", jl, jl + 1))
-    cp(full("ident"), idn)
-    ts(full("i68"), idn, m12, A.mult, 2.0 ** -68, A.mult)
+        sc(top(("lk", 128 * jl, 128 * jl + 128)), top(full("dk2")), top(("selm", 8 + jl, 9 + jl)))
+    sc(full("ident"), idn, 1.0)
+    ts(col("s12"), m12, 2.0 ** -68, A.mult)
+    sc(full("i68"), idn, col("s12"))
     ts(col("zb"), col("c12"), col("c13"), A.add, 2.0 ** -68, A.mult)
-    for c in range(NC):
-        ms(whole("fx%d" % c), 0.0)
-        ms(c_("ra", c, 0, 128), 2.0 ** 29)
+    for b in ("padb", "padf"):
+        n = SCRATCH[b][1][1]
+        ms((b, 0, 8 * n, lambda T, b=b: T[b][:, 0::2, :], 4 * n), 0.0)
+    ms(("cc", 192, 320), 2.0 ** 29)
+    ts(full("thv"), ("mrow", 0, 16), icol, A.is_gt, col("s12"), A.mult)
     cp(full("wtf"), full("wts"))
     ts(col("h13"), col("c13"), 0.5, A.mult)
     ts(col("ca"), col("c12"), -2048.0, A.mult, col("h13"), A.add)
     ts(col("cb"), col("c12"), -4096.0, A.mult, col("h13"), A.add)
     for k, (w, x) in enumerate(((0, "ca"), (1, "ca"), (1, "cb"))):
         ts(col("u%d" % k), ("wtf", w, w + 1), col(x), A.add, 2.0 ** 68, A.mult)
-        ts(("wu1", 8 * k, 8 * k + 8), z8, col("u%d" % k), A.mult)
+        sc(("wu1", 8 * k, 8 * k + 8), z8, col("u%d" % k))
     for k in range(2):
-        ts(("wu2", 8 * k, 8 * k + 8), z8, ("wtf", k, k + 1), A.mult, -2.0 ** 68, A.mult)
-    ts(full("i97"), idn, 97.0, A.mult)
-    ts(full("n97"), idn, -97.0, A.mult)
-    cp(full("identf"), idn)
-    ts(full("ik"), idn, 2.0 ** -66, A.mult)
-    for c in range(NC):
-        ms(whole("xf%d" % c), 0.0)
-        ms(c_("ra", c, 448, 512), 0.0)
-        ms(c_("rb", c, 0, 128), 2.0 ** 29)
-        ms(c_("rb", c, 256, 320), 0.0)
+        sc(("wu2", 8 * k, 8 * k + 8), z8, ("wtf", k, k + 1), -2.0 ** 68)
+    if U_V or U_S:
+        sc(("wu3", 0, 16), full("wu2"), -1.0)
+        sc(("wu3", 16, 24), ("wu1", 16, 24), 1.0)
+    if M_V:
+        ms(full("two"), 0.125)
+        sc(("cc", 0, 128), ("ones", 0, 128), col("ca"))
+        sc(("cc", 128, 192), ("ones", 0, 64), col("cb"))
+    if U_S:
+        sc(("wu1", 24, 40), ("wu3", 0, 16), 1.0)
+    sc(full("i97"), idn, 97.0)
+    sc(full("n97"), idn, -97.0)
+    sc(full("identf"), idn, 1.0)
+    sc(full("ik"), idn, 2.0 ** -66)
     ms(("mk0", W, W + 16), 2.0 ** 20)
     ms(("mk1", W, W + 16), 2.0 ** 20)
-    cp(("wd0", 0, 16), ("wq", 0, 16))
-    cp(("wd1", 0, 8), ("wq", 0, 8))
+    sc(("wd0", 8, 24), ("wq", 0, 16), 1.0)
     ts(col("we"), ("e3", 1, 2), m12, A.mult)
-    ts(("wd0", 16, 24), z8, col("we"), A.mult)
-    ts(("wd1", 8, 16), z8, col("we"), A.mult)
-    ts(full("nident"), idn, -1.0, A.mult)
-    ms(whole("xk"), 0.0)
-    ms(whole("xa"), 0.0)
+    sc(("wd0", 0, 8), z8, col("we"))
+    sc(full("nident"), idn, -1.0)
+    if D_S:
+        ts(("i16", 1, 2), full("ip"), 1, A.bitwise_and)
+        ts(col("odd"), ("i16", 1, 2), 3.0, A.mult, 1.0, A.add)
+        ts(col("ev"), ("i16", 1, 2), -1.0, A.mult, icol, A.add)
+        ts(("mrow", 16, 22), ("mrow", 0, 6), 2.0, A.mult, col("ev"), A.is_equal)
+        ts(("mrow", 24, 30), ("mrow", 16, 22), col("we"), A.mult, col("odd"), A.mult)
+        for k in range(6):
+            sa(("wg", 8 * k, 8 * k + 8), z8, F.Copy, scale=("mrow", 24 + k, 25 + k))
+        sc(("wg", 48, 64), ("wq", 0, 16), 1.0)
+        sc(("wg", 64, 112), ("wg", 0, 48), -1.0)
+        sc(("wg", 112, 128), ("wq", 8, 24), -1.0)
+        sc(("wg", 128, 176), ("wg", 0, 48), -1.0)
+        sc(("wg", 176, 184), z8, 0.0)
 
     def learn_constants():
-        ts(col("th"), col("i11"), -3.0, A.add, 0.0, A.max)
+        sa(col("th"), col("i11"), F.Relu, bias=-3.0)
         sa(("e3", 2, 3), col("th"), F.Exp, scale=21 * LN2, bias=-102 * LN2)
-        ts(col("k3"), ("e3", 2, 3), m12, A.mult)
-        ts(full("dk3"), idn, col("k3"), A.mult)
+        sc(col("k3"), ("e3", 2, 3), m12)
+        sc(full("dk3"), idn, col("k3"))
+        ts(("selm", 0, 8), ("mrow", 0, 8), 8.0, A.add, icol, A.is_equal)
         mm(("pe", 128, 256), (full("bd"), full("dk3")))
+        sc(full("dk4"), ("pe", 128, 256), 1.0)
         for jl in range(8):
-            sa(("lp", 128 * jl, 128 * jl + 128), ("pe", 128, 256), F.Copy, scale=("selm", jl, jl + 1))
-        ts(full("ln"), full("lp"), -1.0, A.mult)
-        ts(full("i75"), idn, m12, A.mult, 2.0 ** -75, A.mult)
-        ts(full("n75"), idn, m12, A.mult, -2.0 ** -75, A.mult)
-        ts(full("f75"), idn, 2.0 ** -75, A.mult)
+            sc(("lp", 128 * jl, 128 * jl + 128), full("dk4"), ("selm", jl, jl + 1))
+        sc(full("ln"), full("lp"), -1.0)
+        sc(full("i75"), full("i68"), 2.0 ** -7)
+        sc(full("n75"), full("i68"), -2.0 ** -7)
+        sc(full("f75"), idn, 2.0 ** -75)
+        if L_M:
+            ts(("mrow", 32, 48), ("mrow", 0, 16), 3.0, A.add, icol, A.is_gt)
+            ts(("mrow", 48, 64), ("mrow", 0, 16), 0.0, A.is_gt, m12, A.mult)
+            tt(full("th3"), ("mrow", 32, 48), ("mrow", 48, 64), A.mult)
 
     def edit_constants():
         gi(full("trow"), [[0, 2], [1, 128]], 0, 0, True)
@@ -306,172 +408,225 @@ def graph():
         ts(full("dump16"), full("t16"), 8208.0, A.add)
         ts(col("ge13"), icol, 13.0, A.is_ge)
         ts(col("ge14"), icol, 14.0, A.is_ge)
-        ts(full("isym"), idn, m12, A.mult)
-        ts(full("sh1"), ("idw", 3, 131), col("ge13"), A.mult)
-        ts(full("sh2"), ("idw", 4, 132), col("ge14"), A.mult)
+        sc(full("isym"), idn, m12)
+        sc(full("sh1"), ("idw", 3, 131), col("ge13"))
+        sc(full("sh2"), ("idw", 4, 132), col("ge14"))
         ts(full("sel1"), ("mrow", 0, 16), 2.0, A.is_equal)
         ts(full("sel2"), ("mrow", 0, 16), 1.0, A.is_equal)
-        ts(full("mt"), ("mrow", 0, 16), col("c12"), A.mult)
+        sc(full("mt"), ("mrow", 0, 16), col("c12"))
         ts(col("wcm"), icol, 15.0, A.is_lt, m12, A.subtract)
-        ts(full("spa"), ("idw", 1, 129), col("wcm"), A.mult)
+        sc(full("spa"), ("idw", 1, 129), col("wcm"))
         tt(full("spl"), full("spa"), full("isym"), A.add)
 
-    def flip(c):
-        fx, pw = "fx%d" % c, "pw%d" % c
-        pe([(128, at((pw, 0, 128)), lambda T: T[fx][:, 0:16, :], at(full("ident")), True, True)],
-           [whole(fx), full("ident")], [(pw, 0, 128)])
-        sa(c_("fts", c), (pw, 0, 128), F.Copy)
-
     def search(rd, c):
-        q = c_("qa" if rd == 0 else "qb", c)
+        q = qv(rd, c)
         mk = ("mk0" if rd == 0 else "mk1", 0, W + 16)
         pn, pw, fx, xf = "pn%d" % c, "pw%d" % c, "fx%d" % c, "xf%d" % c
         ss, key = ("vp", c * 128, c * 128 + 64), ("vp", c * 128 + 64, c * 128 + 128)
         hit, zz, dd = c_("hit", c), c_("zz", c), c_("dd", c)
-        kb = pad("xk") if c == 0 else c_("kb", c)
-        r = lambda k: c_("ra", c, 128 + 64 * k, 192 + 64 * k)
-        n2 = c_("rb", c, 192, 256)
+        kb = pad("xk%d" % c)
+        r = lambda k: c_("ra", c, 64 * k, 64 + 64 * k)
+        n2, mp, tp, xm = c_("rb", c, 0, 64), "mp%d" % c, "tp%d" % c, c_("rb", c, 64, 128)
+        m = pad(mp)
         cur[0] = "%d%d0" % (rd, c)
-        pe(feats(pn, 0, full("wq"), q, True, True), [q, full("wq")], [(pn, 0, 320)])
-        sa(r(0), (pn, 0, 64), F.Copy)
-        sa(c_("ra", c, 192, 448), (pn, 64, 320), F.Copy)
+        pe(feats(pn, 0, full("wq"), (rd, c), True, True), [q, full("wq")], [(pn, 0, 320)])
+        un(m if (rd, c, 0) in M_V else r(0), (pn, 0, 64), 1.0, 0.0, (rd, c, 0, "m"))
+        if (rd, c, 0) in M_V:
+            un(c_("ra", c, 0, 320), (pn, 0, 320), 1.0, 0.0, (rd, c, 0, "r"))
+        else:
+            un(c_("ra", c, 64, 320), (pn, 64, 320), 1.0, 0.0, (rd, c, 0, "r"))
+            m = r(0)
         for st in range(S):
             cur[0] = "%d%d%d" % (rd, c, st)
-            mx = "ra" if st == 0 else "rb"
-            m = c_(mx, c, 128, 192)
+            byv, umv = (rd, c, st) in M_V, (rd, c, st) in U_V
             sa(pad(fx), m, F.Exp, scale=-17 * LN2, bias=80 * LN2)
-            flip(c)
-            for h, bank in ((0, pn), (1, pw)):
-                calls = []
-                for jl in range(4 * h, 4 * h + 4):
-                    o = (bank, 128 * (jl % 4), 128 * (jl % 4) + 128)
-                    calls.append((128, at(o), at(full("i68")), sl(q[0], q[1] + jl, q[2], 8), True, False))
-                    calls.append((128, at(o), at(("lk", 128 * jl, 128 * jl + 128)), at(c_("fts", c)), False, True))
-                pe(calls, [q, full("i68"), ("lk", 512 * h, 512 * h + 512), c_("fts", c)], [(bank, 0, 512)])
-                if (rd, c, st, h) in Z_V:
-                    ts(c_("zz", c, 512 * h, 512 * h + 512), (bank, 0, 512), col("zb"), A.add, 0.0, A.max)
-                else:
-                    sa(c_("zz", c, 512 * h, 512 * h + 512), (bank, 0, 512), F.Relu, bias=col("zb"))
+            if byv:
+                turn((pw, 64, 128), (mp, "ident"))
+                cp(c_("ml", c), (pw, 64, 128))
+                tt(zz, full("thv"), q, A.mult, ind=c_("ml", c))
+            else:
+                parts = [r(0)] if st == 0 else [r(1) if st == 1 else n2, xm]
+                o = top((pw, 0, 128))
+                pe([(128, at(o), at(x), at(full("ident")), k == 0, k == len(parts) - 1) for k, x in enumerate(parts)],
+                   parts + [full("ident")], [o])
+                sa(top(c_("fts", c)), o, F.Exp, scale=-17 * LN2, bias=80 * LN2)
+                for h, bank in ((0, pn), (1, pw)):
+                    calls = []
+                    for jl in range(4 * h, 4 * h + 4):
+                        o = (bank, 128 * (jl % 4), 128 * (jl % 4) + 128)
+                        calls.append((128, at(o), at(full("i68")), at(qv(rd, c, None, jl)), True, False))
+                        calls.append((128, at(o), at(top(("lk", 128 * jl, 128 * jl + 128))), at(top(c_("fts", c))), False, True))
+                    pe(calls, [q, full("i68"), ("lk", 512 * h, 512 * h + 512), c_("fts", c)], [(bank, 0, 512)])
+                    if (rd, c, st, h) in Z_V:
+                        ts(c_("zz", c, 512 * h, 512 * h + 512), (bank, 0, 512), col("zb"), A.add, 0.0, A.max)
+                    else:
+                        sa(c_("zz", c, 512 * h, 512 * h + 512), (bank, 0, 512), F.Relu, bias=col("zb"))
             ky = (pw, 0, 64)
-            sa(ky, m, F.Identity, scale=8192.0, bias=float((st + 1) << 18))
-            u = (pn, 0, 192)
-            k = pe([(192, at(u), at(full("i97")), at(c_(mx, c, 0, 192)), True, False)]
-                   + feats(pn, 0, full("wu1"), zz, False, False, range(4), 1),
-                   [full("i97"), c_(mx, c, 0, 192), full("wu1"), c_("zz", c, 0, 512)], [u])
-            pe(feats(pn, 0, full("wu1"), zz, False, False, range(4, 8), 1)
-               + [(128, at((pn, 0, 128)), at(full("n97")), at(c_(mx, c, 0, 128)), False, False)]
-               + feats(pn, 0, full("wu2"), zz, False, True, range(8), 1),
-               [full("n97"), full("wu1"), full("wu2"), zz], [u], cont=k)
-            sa(c_("cs", c), (pn, 64, 128), F.Copy)
-            tt(c_("pp", c), (pn, 0, 64), c_("cs", c), A.mult)
+            un(ky, m, 8192.0, float((st + 1) << 18), (rd, c, st, "y"))
+            ums = (rd, c, st) in U_S and not umv
+            u, u12, ta = (pn, 0, 320 if ums else 192), (pn, 0, 128), (pn, 128, 192)
+            wu = full("wu3") if umv else ("wu1", 0, 40 if ums else 24)
+            big = lambda l: (128, at(u12), at(full(l)), at(("cc", 192, 320)), False, False)
+            m97 = lambda first, last: (64, at(ta), at(full("i97")), at(m), first, last)
+            cst = lambda lo, first: (192 - lo, at((pn, lo, 192)), at(full("two")), at(("cc", lo, 192)), first, False)
+            R = [full(x) for x in ("i97", "n97", "two", "cc", "wu2")] + [wu, m]
+            step, late = 8 if byv else 1, umv or ums
+            head = [] if late else [cst(0, True), m97(False, False)] if byv else [m97(True, False), big("i97")]
+            if not byv:
+                head += feats(pn, 0, wu, zz, late, False, range(4), 1)
+            k = pe(head, R + ([] if byv else [c_("zz", c, 0, 512)]), [u]) if head else None
+            rest = feats(pn, 0, wu, zz, not head, False, range(8) if byv else range(4, 8), step)
+            if late:
+                rest += ([cst(128 if umv else 0, False)] if byv else []) + [m97(False, True)]
+            else:
+                rest += ([big("i97")] if byv else []) + [big("n97")] + feats(pn, 0, full("wu2"), zz, False, True, range(8), step)
+            pe(rest, R + [zz], [u], cont=k)
+            if umv:
+                cp(c_("ui", c), u12)
+                ts(c_("ac", c), c_("ui", c), 4095, A.bitwise_and)
+                tt(c_("pp", c), c_("ac", c, 0, 64), c_("ac", c, 64, 128), A.mult)
+            elif ums:
+                sa(c_("ta", c), u12, F.Identity, bias=M12)
+                sa(c_("tb", c), c_("ta", c), F.Identity, bias=-M12)
+                tt(c_("cs", c), (pn, 256, 320), c_("tb", c, 64, 128), A.subtract)
+                tt(key, (pn, 192, 256), c_("tb", c, 0, 64), A.subtract)
+                tt(c_("pp", c), key, c_("cs", c), A.mult)
+            else:
+                un(c_("cs", c), (pn, 64, 128), 1.0, 0.0, (rd, c, st, "c"))
+                tt(c_("pp", c), (pn, 0, 64), c_("cs", c), A.mult)
             ts(c_("kk", c), c_("pp", c), 5, A.arith_shift_right)
-            tt(ss, (pn, 128, 192), c_("kk", c), A.add)
-            ts(c_("tt", c), ss, M13, A.add, M13, A.subtract)
-            tt(pad(xf), ss, c_("tt", c), A.subtract)
-            turn((pn, 192, 256), xf, fx)
+            tt(pad(xf), (pn, 128, 192), c_("kk", c), A.add)
+            ts(pad(tp), pad(xf), M13, A.add, M13, A.subtract)
+            turn((pn, 192, 256), (xf, "identf"), (fx, "ik"), (tp, "nident"))
             ts(c_("hl", c), (pn, 192, 256), HALF, A.add, float(W), A.min)
-            tt(key, ky, pad(xf), A.add)
+            tt(ss, ky, pad(tp), A.subtract)
+            tt(key, ss, pad(xf), A.add)
             if rd == 0 and c == 0:
-                ts(full("act"), m, 0.0, A.is_gt)
+                sa(full("act"), m, F.Sign)
                 if st == 0:
                     tt(pad("xa"), key, full("act"), A.mult)
                 else:
                     tt(("vp", 384, 448), key, full("act"), A.mult)
                     tt(pad("xa"), ("vp", 384, 448), pad("xa"), A.max)
-            tt(dd, mk, q, A.subtract, ind=c_("hl", c))
-            if st == 0:
-                o, x = (pn, 256, 448), c_("ra", c, 320, 512)
-                pe([(192, at(o), at(full("ident")), at(x), True, False)] + feats(pn, 256, full("wd0"), dd, False, True),
-                   [full("ident"), x, full("wd0"), dd], [o])
-            elif st == 1:
-                o, x = (pn, 256, 384), c_("rb", c, 192, 320)
-                pe([(128, at(o), at(full("nident")), at(x), True, False),
-                    (64, at((pn, 256, 320)), at(full("ident")), at(r(0)), False, False)]
-                   + feats(pn, 256, full("wd1"), dd, False, True), [full("ident"), full("nident"), x, r(0), full("wd1"), dd], [o])
+            nf, d0, d1 = 64 - 8 * st, (pn, 384, 448), (pn, 448, 512)
+            if (rd, c, st) in D_S:
+                sa(dd, mk, F.Copy, ind=c_("hl", c))
+                o, wq = (pn, 0, 8 * nf), (("wg", 64, 128), ("wg", 128, 184), ("wg", 64, 112))[st]
+                k = pe(feats(pn, 0, wq, (rd, c), True, False) + ([(64, at(d0), at(full("nident")), at(n2), False, False)] if st == 1 else []),
+                       [q, wq, full("nident"), n2], [o])
+                pe(feats(pn, 0, ("wg", 0, nf), dd, False, True), [("wg", 0, nf), dd], [o], cont=k)
+                sa(c_("da", c), (pn, 0, 384), F.Abs)
+                ea = (pn, 0, 64)
+                mm(ea, *[(full("ident"), c_("da", c, 64 * i, 64 * i + 64)) for i in range(6)])
             else:
-                o = (pn, 256, 320)
-                pe(feats(pn, 256, ("wd1", 8, 16), dd, True, True), [full("wd1"), dd], [o])
-            sa((pn, 448, 512), (pn, o[2] - 64, o[2]), F.Abs)
-            tt(hit, (pn, 448, 512), pad(fx), A.is_lt)
+                tt(dd, mk, q, A.subtract, ind=c_("hl", c))
+                o, ea = (pn, 320, 512 - 64 * st), (pn, 256, 320)
+                calls = feats(pn, 320, ("wd0", 0, 24 - 8 * st), dd, True, st == 2)
+                if st == 0:
+                    calls.append((128, at((pn, 384, 512)), at(full("ident")), at(c_("ra", c, 192, 320)), False, True))
+                if st == 1:
+                    calls += [(64, at(d0), at(full("nident")), at(n2), False, False), (64, at(d0), at(full("ident")), at(r(0)), False, True)]
+                pe(calls, [full("ident"), full("nident"), c_("ra", c), full("wd0"), dd] + ([n2] if st == 1 else []), [o])
+                sa(ea, (pn, 320, 384), F.Abs)
+            tt(hit, ea, pad(fx), A.is_lt)
             if st < 2:
-                tt(ss, (pn, 256, 320), hit, A.mult)
-                tt(c_("rb", c, 128, 192), ss, r(1) if st == 0 else n2, A.add)
+                tt(xm, d0, hit, A.mult)
+                m = pad(mp)
+                if (rd, c, st, "a") in A_V:
+                    tt(m, xm, r(1) if st == 0 else n2, A.add)
+                else:
+                    x = (pw, 128, 192)
+                    mm(x, (full("ident"), r(1) if st == 0 else n2), (full("ident"), xm))
+                    sa(m, x, F.Copy)
             if st == 0:
-                tt(ss, (pn, 320, 384), hit, A.mult)
-                tt(n2, ss, r(2), A.add)
+                tt(d1, d1, hit, A.mult)
+                tt(n2, d1, r(2), A.add)
                 tt(kb, key, hit, A.mult)
             else:
                 tt(key, key, hit, A.mult)
                 tt(kb, key, kb, A.max)
 
     def learn(rd, c):
-        qn = "qa" if rd == 0 else "qb"
         nw = "nwa" if rd == 0 else "nwb"
         mk = ("mk0" if rd == 0 else "mk1", 0, W + 16)
         pn, pw, fx, xf = "pn%d" % c, "pw%d" % c, "fx%d" % c, "xf%d" % c
-        kb = pad("xk") if c == 0 else c_("kb", c)
-        ta = ("vp", c * 128, c * 128 + 64)
+        xk, tp, mp = "xk%d" % c, "tp%d" % c, "mp%d" % c
+        kb = pad(xk)
         cur[0] = "%d%d3" % (rd, c)
-        ts(ta, kb, M13, A.add, M13, A.subtract)
-        tt(pad(xf), kb, ta, A.subtract)
-        turn((pn, 192, 256), xf)
+        ts(pad(tp), kb, M13, A.add, M13, A.subtract)
+        turn((pn, 192, 256), (xk, "identf"), (tp, "nident"))
         ts(c_("bl", c), (pn, 192, 256), HALF, A.add, float(W), A.min)
-        if (rd, c) in L_V:
-            tt(c_("ld", c), mk, c_(qn, c), A.subtract, ind=c_("bl", c))
-        else:
-            sa(c_("ld", c), mk, F.Copy, ind=c_("bl", c))
-        ts(c_("tt", c), kb, M18, A.add, M18, A.subtract)
-        tt(c_("mb8", c), ta, c_("tt", c), A.subtract)
-        sa(pad(fx), c_("mb8", c), F.Exp, scale=-21 * LN2 / 8192, bias=60 * LN2)
-        flip(c)
+
+        def hv(n, h, w):
+            x = c_(n, c)
+            return (n, x[1] + w * h, x[1] + w * h + w, lambda T: T[n][:, x[1] + w * half(h):x[1] + w * half(h) + w], w)
+
+        def qh_(h):
+            return qv(rd, c)[:3] + (lambda T: ap(T, qv(rd, c, half(h))), 512)
+        for h in (0, 1):
+            if (rd, c, h) in L_V:
+                tt(hv("ld", h, 512), mk, qh_(h), A.subtract, ind=c_("bl", c)[:3] + hv("bl", h, 32)[3:])
+            else:
+                sa(hv("ld", h, 512), mk, F.Copy, ind=c_("bl", c)[:3] + hv("bl", h, 32)[3:])
+        ts(pad(mp), kb, M18, A.add, M18, A.subtract)
+        bym = [(rd, c, h) in L_M and (rd, c, h) in L_V for h in (0, 1)]
+        if any(bym):
+            turn((pw, 128, 192), (tp, "ident"), (mp, "nident"))
+            ts(c_("ml", c), (pw, 128, 192), 2.0 ** -13, A.mult)
+        if not all(bym):
+            o = (pw, 0, 128)
+            pe([(128, at(o), win(tp, 0), at(full("ident")), True, False), (128, at(o), win(mp, 0), at(full("nident")), False, True)],
+               [pad(tp), pad(mp), full("ident"), full("nident")], [o])
+            sa(c_("fts", c), o, F.Exp, scale=-21 * LN2 / 8192, bias=60 * LN2)
         if rd == 1:
             blocks(c)
         for h, bank in ((0, pn), (1, pw)):
-            o, qh, lh = (bank, 0, 512), c_(qn, c, 512 * h, 512 * h + 512), c_("ld", c, 512 * h, 512 * h + 512)
+            o, qh, lh = (bank, 0, 512), qh_(h), hv("ld", h, 512)
+            if bym[h]:
+                tt(hv("zz", h, 512), full("th3"), lh, A.mult, ind=c_("ml", c)[:3] + hv("ml", h, 32)[3:])
+                mm(o, (full("ident"), qh), (full("ident"), hv("zz", h, 512)))
+                un(hv(nw, h, 512), o, 1.0, 0.0, (rd, c, h, "e"))
+                continue
             calls = [(512, at(o), at(full("i75")), at(lh), True, False)]
-            if (rd, c) not in L_V:
+            if (rd, c, h) not in L_V:
                 calls.append((512, at(o), at(full("n75")), at(qh), False, False))
             for l in ("lp", "ln"):
                 for jl in range(8):
                     calls.append((64, sl(bank, jl, 512, 8), at((l, 128 * jl, 128 * jl + 128)),
-                                  at(c_("fts", c, 64 * h, 64 * h + 64)), False, False))
+                                  at(hv("fts", h, 64)), False, False))
             calls.append((512, at(o), at(full("f75")), at(qh), False, True))
             pe(calls, [qh, lh, full("i75"), full("n75"), full("f75"), full("lp"), full("ln"), c_("fts", c)], [o])
-            sa(c_(nw, c, 512 * h, 512 * h + 512), o, F.Relu, scale=2.0 ** 75, bias=-2.0 ** -10)
+            sa(hv(nw, h, 512), o, F.Relu, scale=2.0 ** 75, bias=-2.0 ** -10)
+
+    first = []
 
     def move(c):
-        def f(g, T, e):
+        def f(g, T, e, h):
             core, rank, topo = e
-            moves, k = [], 0
-            for d in range(1, 8):
-                s = (rank + d) % 8
-                dst = T.cores[s]
-                en = topo.engines(core, dst)
-                if topo.chip(dst) == topo.chip(core):
-                    eng = en[-1]
-                else:
-                    eng = (en[0::2] + en[1::2])[k]
-                    k += 1
-                ad = topo.addr(dst)
+            moves = []
+            for s, en in lanes(T, topo, rank, half(h)).items():
+                ad = topo.addr(T.cores[s])
                 moves.append(RemoteDMATransfer(
-                    dst_ids=[DstId(rid=ad[0], pnc=ad[1])], dma_engine_mask=1 << eng, remote_sem=T.sem["arr%d" % c],
+                    dst_ids=[DstId(rid=ad[0], pnc=ad[1])], dma_engine_mask=sum(1 << x for x in en), remote_sem=T.sem["arr%d" % c],
                     src=T.nwa[:, c * CH + 128 * s:c * CH + 128 * s + 128],
                     dst=T.qb[:, c * CH + 128 * rank:c * CH + 128 * rank + 128]))
             return g.remote_dma_fused(moves, local_sem=T.sem["snt%d" % c])
-        i = add("G", 1500, f, [c_("nwa", c)], [], sem="none%d" % c, inc=0)
-        add("arr%d" % c, 0, None, [], [c_("qb", c)], sem="arr%d" % c, inc=7, lat=7000, deps=(i,))
+        i = [add("G", 1000 if c or h else 4000, lambda g, T, e, h=h: f(g, T, e, h), [c_("nwa", c, 512 * h, 512 * h + 512)], [], sem="none%d%d" % (c, h), inc=0,
+                 cont=first[0] if c or h else first.append(len(ops)))
+             for h in (0, 1)]
+        add("arr%d" % c, 0, None, [], [c_("qb", c)], sem="arr%d" % c, inc=1, lat=5500, deps=i)
 
         def f2(g, T, e):
             a = c * CH + 128 * e[1]
             return g.sync.dma_start(T.qb[:, a:a + 128], T.nwa[:, a:a + 128])
-        k = add("Y", 60, f2, [c_("nwa", c)], [], sem="slf%d" % c, inc=16, lat=2500)
+        k = add("Y", 60, f2, [c_("nwa", c, 512, CH)], [], sem="slf%d" % c, inc=16, lat=2500)
         acc["qb"].append((k, "Y", c * CH, c * CH + CH, True))
 
     def edits():
         a8 = lambda n, k: (n, 8 * k, 8 * k + 8)
         bl = ("bl", 0, 8)
-        turn(("pe", 256, 264), "xa")
-        turn(("pe", 264, 272), "xk")
+        turn(("pe", 256, 264), ("xa", "identf"))
+        turn(("pe", 264, 272), ("xk0", "identf"))
         ts(full("k2"), ("pe", 256, 272), HALF, A.add)
         ts(full("fb"), full("k2"), W - 1, A.bitwise_and)
         ts(full("mfi"), a8("k2", 0), 13, A.arith_shift_right, 15, A.bitwise_and)
@@ -514,8 +669,8 @@ def graph():
     def blocks(c):
         v, x = ("pn%d" % c, 192, 256), ("vp", c * 128 + 64, c * 128 + 128)
         ts(c_("ybx", c), v, 0.0, A.is_equal, -HALF - 1.0, A.mult)
-        tt(x, v, c_("ybx", c), A.add)
-        ts(("yby", 64 * c, 64 * c + 64, lambda T: T.yby[:, :, 8 * c:8 * c + 8], 64), x, HALF, A.add)
+        tt(c_("cs", c), v, c_("ybx", c), A.add)
+        un(("yby", 64 * c, 64 * c + 64, lambda T: T.yby[:, :, 8 * c:8 * c + 8], 64), c_("cs", c), 1.0, HALF, (1, c, 0, "b"))
         if c == NC - 1:
             add("Y", 60, lambda g, T, e: g.sync.dma_start(T.yb[:, :], T.yby[:, :, :]),
                 [("yby", 0, 192)], [], sem="lyb", inc=16, lat=2500)
@@ -525,9 +680,10 @@ def graph():
             q = "S" if c == NC - 1 and s >= 6 else "Y"
             a = c * CH + 128 * s
 
-            def f(g, T, e, a=a, s=s, q=q):
+            def f(g, T, e, s=s, q=q):
+                x = 4 * half(s // 4) + s % 4
                 return (g.sync if q == "Y" else g.scalar).dma_start(
-                    T.yq[:, 384 * s + 128 * c:384 * s + 128 * c + 128], T.nwb[:, a:a + 128])
+                    T.yq[:, 384 * x + 128 * c:384 * x + 128 * c + 128], T.nwb[:, c * CH + 128 * x:c * CH + 128 * x + 128])
             add(q, 60, f, [("nwb", a, a + 128)], [], sem="out%d" % c, inc=16, lat=2500)
 
     cur[0] = "l"
@@ -582,11 +738,21 @@ def schedule(ops):
         done[i] = free[q] + ops[i]["lat"]
         order.append(i)
         for k in kids[i]:
-            est[k] = max(est[k], done[i] + WAKE)
+            est[k] = max(est[k], done[i] + (0.0 if i in ops[k]["soft"] else WAKE))
             need[k] -= 1
             if need[k] == 0:
                 ready[ops[k]["q"]].append(k)
     return order, max(done), done
+
+
+def plan(ops):
+    order = [(ord(ORDER[k]) - 48) * 40 + ord(ORDER[k + 1]) - 48 for k in range(0, len(ORDER), 2)]
+    seen = set()
+    for i in order:
+        if i >= len(ops) or not ops[i]["deps"] <= seen:
+            break
+        seen.add(i)
+    return order if len(seen) == len(ops) == len(order) else schedule(ops)[0]
 
 
 PLAN = {}
@@ -598,7 +764,7 @@ def rank_program(g, core, T, topo):
         return
     if not PLAN:
         PLAN["ops"] = graph()
-        PLAN["order"] = schedule(PLAN["ops"])[0]
+        PLAN["order"] = plan(PLAN["ops"])
     ops, order = PLAN["ops"], PLAN["order"]
     env = (core, rank, topo)
     eng = {"T": g.tensor, "V": g.vector, "S": g.scalar, "G": g, "Y": g.sync}
@@ -606,6 +772,10 @@ def rank_program(g, core, T, topo):
     for o in ops:
         if o["sem"] and o["inc"]:
             total[o["sem"]] = total.get(o["sem"], 0) + o["inc"]
+    for c in range(NC):
+        total["arr%d" % c] = sum(len(lanes(T, topo, s, rank // 4)[rank]) for s in range(8) if s != rank)
+        total["snt%d" % c] = sum(len(en) for h in (0, 1) for en in lanes(T, topo, rank, h).values())
+    RANK[0] = rank
     count, stamp, clock, known = {}, {}, {}, {}
     for i in order:
         o = ops[i]
@@ -613,7 +783,7 @@ def rank_program(g, core, T, topo):
         kn = known.setdefault(q, {})
         want = {}
         for d in o["deps"]:
-            if d == o["cont"]:
+            if d in o["soft"]:
                 continue
             s, v = stamp[d]
             if kn.get(s, 0) < v:
@@ -651,4 +821,4 @@ def rank_program(g, core, T, topo):
         if s in count:
             g.wait_ge(T.sem[s], count[s])
         else:
-            g.wait_ge(T.sem[s], total[s] if s in total else 7)
+            g.wait_ge(T.sem[s], total[s])

@@ -21,28 +21,31 @@ def _b(dtype, where, spec, k=1):
 
 
 _b("bfloat16", "sbuf", "mk0:8208 mk1:8336 wts:2 ones:132 idw:132 ident:128 nident:128 i97:128 n97:128 i68:128 ik:128 i75:128 "
-   "n75:128 f75:128 bda:128 bd:128 dk1:128 dk2:128 dk3:128 dk4:128 lk:1024 lp:1024 ln:1024 e3:3 wu1:40 wu2:16 wu3:24 cc:320 two:128 thv:16 th3:16 wq:40 wd0:24 wg:184 "
+   "n75:128 f75:128 bda:128 bd:128 dk1:128 dk2:128 dk3:128 dk4:128 lk:1024 lp:1024 ln:1024 e3:3 wu1:40 wu2:16 wu3:24 cc:512 i8k:128 two:128 thv:16 th3:16 zero:128 wd0:24 wg:184 "
    "isym:128 sh1:128 sh2:128 spl:128 spa:128 z8a:8 z8:8 sel1:16 sel2:16 "
    "mt:16 g0:128 ga1:128 ga2:128 wnew:128 g1:128 mfw:128 snew:128")
-_b("int32", "sbuf", "ip:1 i16:3 k2:16 fb:16 mfi:8 sbi:8")
-_b("uint16", "sbuf", "flu:16 tgu:16 sbl:8 mfl:8")
-_b("float32", "sbuf", "col:40 identf:128 selm:16 wtf:2 mrow:64 iot:8208 trow:256 "
+_b("int32", "sbuf", "ip:1 i16:3 k2:16 fb:16 mfi:16")
+_b("uint16", "sbuf", "flu:16 tgu:16 mfl:16")
+_b("float32", "sbuf", "col:40 identf:128 selm:16 wtf:8 cmp:48 mrow:64 iot:8208 trow:256 "
    "t16a:16 t16:16 t16b:16 dump16:16 act:64 ed1:8 ed0:8 ed:16 fbm:16 fbe:16 nb:16 krow:256 dk:2048 first:16 win:16 "
    "gg:16 tgt:16")
 SCRATCH["yby"] = ("sbuf", [128, 8, 24], "float32")
 SCRATCH["qn"] = ("sbuf", [128, 8, 384], "bfloat16")
+SCRATCH["ohw"] = ("sbuf", [128, 17, 8], "bfloat16")
+SCRATCH["ro1"] = ("dram", [8, 128, 120], "bfloat16")
+SCRATCH["ro2"] = ("dram", [8, 128, 120], "bfloat16")
 PADS = {}
 for _n, _d, _l in (("padf", "float32", "xf0 xf1 xf2 xk0 xk1 xk2 xa"), ("padb", "bfloat16", "fx0 fx1 fx2 mp0 mp1 mp2 tp0 tp1 tp2")):
     SCRATCH[_n] = ("sbuf", [128, 18 * len(_l.split()), 8], _d)
     for _k, _x in enumerate(_l.split()):
         PADS[_x] = (_n, 18 * _k)
-_b("bfloat16", "sbuf", "qa:1024 qb:1024 zz:1024 dd:1024 ld:1024 nwa:1024 nwb:1024 ra:320 rb:128 fts:128 hit:64 da:384", NC)
+_b("bfloat16", "sbuf", "qa:1024 qb:1024 zz:1024 dd:1024 ld:1024 nwa:1024 nwb:1024 ra:320 ra2:320 rb:128 fts:128 hit:64 da:384", NC)
 _b("float32", "sbuf", "ta:128 tb:128 cs:64 ybx:64", NC)
 _b("int32", "sbuf", "pp:64 kk:64 ui:128 ac:128", NC)
 _b("uint16", "sbuf", "hl:64 bl:64 ml:64", NC)
 _b("float32", "psum", "pn0:512 pn1:512 pn2:512 pw0:512 pw1:512 pw2:512 vp:512 pe:512")
 
-SEMAPHORES = ["sT", "sV", "sS", "sG", "lw", "lq", "lm0", "lm1", "lyb"]
+SEMAPHORES = ["sT", "sV", "sS", "sG", "lw", "lq", "lm0", "lm1", "lyb", "r1", "r2", "r3", "arrr", "sntr"]
 for _c in range(NC):
     SEMAPHORES += ["slf%d" % _c, "arr%d" % _c, "snt%d" % _c, "out%d" % _c]
 
@@ -68,6 +71,10 @@ A_V = {(0,1,2,'y'),(1,0,0,'r'),(0,1,0,'c'),(0,1,0,'q'),(0,2,0,'q'),(0,0,0,'c'),(
 ORDER = "00040708180>0?1<0;0@1:0A0E0D090B0G0O0F0:0R0H0<0L0J0M0I0K0=0N1;271514;50C170P;61=0Q1S1N0S1@240U0T0W0V1R050103028@1V103229131K16121T5T2B331U1A8A2:36281C5U8D1B371J601P111W3:1H341L1I1O268B1M20382;218E252D3;23193I2I8F395V8C1>8H2G8G2H;<;;2W1?3=61;>8I2?3>352>8K2<3?2@8L312A3@2=623<8M5W3A8J8N2J3B8O64633C8P3D8Q3E8R2C3F8S658T3G063H66678V8U3K8W9068693J916:2K6;3L;:926<2L6=2M303M6>;=932O3N6?2R3O6@942N3P953Q3T962U3U3R979;6A3V986C9<3W9:2P2T2Q41409?2S426B9=3S;49@4@;?;B99;C;@;7441D9>22451F;A;86D4643;99A479B1G6E489C6F496G4:9D4;9E4<9F4=6I9G6H9H6J6L6M9I4>6N9J4C6Q9K6R6O9L6S4?9N4D6P4E6T6U4F9M9O4G6K4H6V4L4A9P6W4M9Q704K4N9R719S724I9V734J4P744O4B77572V754Q9T1E9W9U764S2E:0784T:1:3:24U794R:44V2F4W:61Q7:50:7:5517;52:853:9547<::7=:;7@7A55:<565:5;:=58:>7B59:?:A;D7>;E:@7C:C:B5<7D7?7E5=:D7F7G5>:E7H5?7I:F5@7J5A7K;F:G5B:H5C:I5D5H:J7L5I:K7M:P5E:Q5F<T5J:L5K5G:R7N:M5L7P:S5N5M:N5P7O;G:O7Q5O:T;M;N7R;J5Q5S;H7S;O7T;P7U;Q7V;R:V7W:U;S;K5R;T;U;084<U<L<>85<N;V80<V:W<?86;W81<W<O8387;1;3<6<D<@<2<882<<8:<:<H;2<F<B<7<0<3<J<M<4<A<E=0<=88<G8;<I<C<9<;<1<K8=8?<5;I<P;L<Q89<R<S=1=7=38<=2=8=9=:=;=4=<=>=?===58>=6BM=@BNBOBPBQ=ABR=B=CBS=D=E=F=GBTBU=H=I=JC0BV?TBWC1?VC2=K?UC3?W@0C4=L@1C5=MC6@2=NC7=OC8=P=SC;=QC9=R@3@4C:C<@7@5=T=U@8@6@9C=@:@;>0C>@<@=C?@>=VC@>1CBCA@?CC@BCDCFCE=W@@CG>2CH@A@C>3CI>4CJ>5CK@D>6>7CM@ECN>8@F>9@G>:@H>;CO@L@M@I><>>@N@JCPCL@OCQ>=CR>?@KCS@QCTCU@PCVD0>@CW@RD1>A@T>B@U>C>D@VD2>E@S>F@W>J>GD3A0>KD4A1>ID5>NA2D6A3>HD9A4D7A7D:D8A5D;>OD>A6A8>P>LD?D<>MD@D=>Q>RA9>S>TDAA:>UDBA;>VDC>WA<?0A=?1A@DD?2?4DEA>DFAA?3DGAB?5AEACAFDHA??6AGDIADDJ?7?8DLAHDK?9AIDM?:DN?;AJ?<AK?=?AAL?BAM?>?CAN?EAO?D?FDOAP??AQDPAR?@DQATAU?HDRASDS?GDTDUE3DVE4DW?IAVE7E0E8?JE1?NAW?M?L?OE2E5B0E6E9?KB1E;B2B3?PB4?RB:?Q?SB5B;B6B<B>E=B7B=B?B8E<E@EAB9EBE?BAE>B@ECEFE:EEEDBCBBBEBHBFBGBDBLBIBKBJ"
 PICK = "110110101111001110010110000110011011010100110001111010111111001001100101011000100011101101010011010000000010010000111001111110001000101110000111000100011011111000001000000100000101111101111001000000000000000011101000010110000111001011111110000101001010000000100100100010000101010"
 ORDER = "000407081M090?0R0@0:0S0A0;0D0F0B0G1;0>0<1<0=0I0E0K0H0C0O;5170L0P0M1@1S0Q1A1Q0T0U0J0N0V1N1?2@1:05010302312032185N151613121935145O8A1B3336345R1E8B39118C1G5P5S1C8E230W1=5V1024255Q1J1R1H1D3:1I37261K1F1P1L1O5T271T388F28295W5U3<3=222;3>612<1U2:623?2=2>1W8I3@632B3A641>3B8G8J66653C672A3D688H2G692T6:3E2?2S6;2U8D;9;>063J;?;:3K6<;;8L6?8M8N3L21603;8O6=3M6@8P3F8Q6>6A8R3N3G8K6B2C8S;=3H6C2D3O;<6E6I3P;@6F3R3V8T6J3S8W3W6K6M6L426N6D3Q40438U2E3I6G2F906H413U446P916O6Q924A3T93;3958V45966R94466S99;498472H6T9:482I6U9;492K6V4:2M714;6W979<4<2P4?4=702O2J732L9=4>4@4D749@2Q752N9>4E76724F4B9A;69?4G779B4H9C4I789D4J799E4M4N4C557>9F4O9G7?4P4Q7B9H7C7@9I7:9L9M9J4K9K4L4R7;7D7<;74S;84T1V4U;A7A4V;B9N4W2V502W9O537E30547F7=569P7G57519Q9R7H9S52;D7I9T589W:0:12R:2:47J9U:37K599V7L7M7O5::57P5;:75<7N5=7Q:85>5C5?:9::7R5@5D5A;E5E7S5B:;;F5F:<;M:=;L:>;O7T;G;N;P;I:6:?;Q;J5G:A;R:B7U:@;S5H:C5J7V<M7W<N80;H8186;T82;K;C:D5I83:E85<A875M:F8488:G<;8;<K<9<S:H<B;W:I<55K:J<E<0<C89:K:P8<<U<<<F<1<T5L8>8@;U<?<L<3:L;V8:<@<D<4:Q:M<V<6:R:N8=<7<I<G<=<W:O=2:S8?<8<2<J:U<H:T<><:<O<P:W<Q<R:V=0=1;0;2=3=6=4=5=7;1=8=:=;=9=<=>===?=A@5=@=B@6@7@9=C@:=D@8@;=E=F=G@=@<=H=K=I@>@@=J=L@?BQ@ABRBS@BBU=NBV@C=M@DBW@E@FC1@GC0@H@J@KC2=O@I@LC4=PC5BTC3=Q=RC6@M=SC7=V=TC8=W@NC9=U>0C:>1>2@OC=C;@P>3@RC>@S@VC<>6@T@WC?>4A2>5A0>7A3>9@QA1>:C@>;@U><A5CAA6>8>=A4CB>>CC>?CECI>@CFCDCJ>AA7CH>CA8CK>BA9>E>DA:CMCGA;A<CLA=A?>FA>A@AACPCN>G>HCQCO>ICR>JABCS>KCT>M>PACCU>N>QCVADCWD1AE>LAFAJ>OD0AI>RAGAKD3AL>S>TAMAND2>UAH>WAO>V?0D4?1APAQ?2D5AR?3D6?4D7?5D9D<?6ASD8D=?7AT?9D;AU?:D>?8AVD:?;AWD@D?B0B2B3?<B1DCB4DA?=?>DDDB??DE?@DFB5?ADG?BDHB6?CB7?DDIB8?HB9DJ?EB:B??GDL?IDKB@DM?J?F?KB;?LDNDOB<?P?SB>BADPB=BGDQ?TBB?MBC?NDRBD@3BH@4?O@2BE@1DSDTDUBOBNBMBPDVE3DWBF?QE0E6E1BIBKBJE4BLE5?RE7E2E:?V?W@0?UE8E9E<E;E@E>EAE?E=ECEEEBED"
+PICK = "001001100100001011101101010111111100111000100001111011011100010011001101011011110011101000001011001000101001110111111101010000001000111111011110111111010000011000000000001001000101110001101011100100000000000000011000011101010011011000111100001000101110000110000010000001010000000111000101111111000000111110001110110011110011000001000000110000000000000001011101000100000000000101000001000110010001110010110110101101010111"
+ORDER = "00040708180@0A0M0=0B090C0N0>0F0D1L160:1;1N0H0;0G150?0J1<1G1:0<210K1=1M1R0O0L1I1A131H0I0P1219140Q1>:U1J1?0T110501030S0W022L0R1B1025731D;22M2:0U2F4T1P741C2N1775772P781E4U7:1@502Q7;0E2R0V1U1S2S4V791O2U2T932V:V54512W1W30527<762O53234W317=3:1F26327>271V55;81T7?9633;97@342G7A;3357B56:W3657;020;137582224591K7C5:39385=5;067E3<3>7D3=5<3;5?3?7F3@7G3A7H3B5@7I7M3C7K7O3D5A3G7P5B7L3I3H5C3V3E3J5I3F3K7T5J7U5N7V7Q7R5O7S5E5>3L5F7J285P5K3M7W293N7N5L5G3O;4803P;73Q2I3R2;5D813S5M2J822K833U3T5H845Q41855R3W865S405T42875U888:2<4344455V2@898;5W46602=4749618<482>8=4;2D4<4I6263944=648>4>8C668D658E8F8H;:8G4?8?4:8@8I8B4@8A674A8J8K4B4C688L4D4E2B95698M2C4F6:8N6;2A8O6<4G8P4H6=2?8Q4L4J8R6>2H4K6?;;8S;66A:T8U4M8T;56B4N1Q6@6C4O6D2E8V6E4P6F8W4Q6G4R904S6I916H98929=99:=:B:>9:979;<H;<9>6J9?:C9<6K9@:?6L9A;=6M9B;@6N:A9C;?6O;>9E6P:@9F9D6Q9G;A:D6R9K;B9H<O6T9I<SBQ:E9J:J6U:F:G9N9L:K;C<J6V;F;D:H;E6W9M6S70:I;G:L71;H:M72<C;I:N9O:P?S;J9P:O9T<T9Q9U<39R:Q:SBR<U9V;O;M<5;Q<I9W;U9S;W:R:0<?<A:1<;:2<1<6<9;V:4;S<4:3;P:5<:;N<B:6<@<7;R:7:9;T<=<<;K<K<>:8<2<0<8<V;L<L<D<W:::<BS<E=1<F=0=2<G?T=3=4?U:;<M=5=6<N=7<P=8BW<Q=9BT=:=;C0<R=<C1BU===>=?BVC2C3C4=@C5C6=A@1C7C8@2=B=EC9=C@3=G=D?V=FC:=H?WC==I@0C;C>=J@4@5=K@6=LC<@7C?@8=N@9C@=M=O@:CA@;CBCD@<=PCCCECFCH@==QCI@@=RCGCMCNCJCOCK@>CL=S@A@?=TCP=UCQ@BCR=V@C=W@DCS>0@F@J@HCT>1@G@KCVCU@E>3>2@LCW>4>5@MD0D1>7D2@ND3>6D5@OD4D6@PD:@I@S@QD8>8D9>9@TD7@R>:@UD;@V>;@W><A0D<>>>AA1D=>BA2A4D>>=D?>C>@A3DB>?DCA6>FDD>GDH>H>DDE>EDFA5D@A7DADG>I>JA8DI>KA9DL>LDJA:>MA?A<>NA=A@DM>ODK>PAADN>QDOA;DPABA>>RDQ>T>UDRADDSACDTDVAEDUDWAHE2AF>VE0>S>WE1AIAJE3?0AK?1E4ALAM?2AN?3E5AO?4AP?5E6AQE7?9ARAG?6E8?<?8E9?:ASE>AVE?E:?;?7?E?F?GE@?H?=E;AWATE<E=???I?@AUB0EA?J?AB1EB?BB2?>B3?CEC?R?OB4?QB9?PEK?DEEB:B5?KB;?M?L?NELB>B6EMB?B8ENB@EDB<EFB=B7EGEOEHBDETEVEUEWEIBABEEJBFBGESBBEREQBHEPBCBPBOBMBNBIBKBJBL"
+PICK = "111000100110001101001001110111100000111001100101111000100100110111001100001011010011001001001111000101100101110111111101010000111100111011110111101111010000011000000000000011100000110001101011100100000000000010001000110001111011110000111110001001101110010110000010000001000000000000011100101110100000010010001101100010111010000110110000010100000100000101010001100111010001110000101101100010000111000011111001111011110111"
+ORDER = "00040708090=0A0M0B0N0@0C1N0D16180O0H0G0F0J151;1<1I1O2:1:;P0E0:0K131>0L191=0>1S0I141V1?1W121R1J20212F23050?01030;0P021M7A0<0Q;T2J1L2L7B1B0R1A1F7E110W2M551T0U7F2N0S2R100T7I2P561C1H592Q7G1D2S1@0V2O7J227K172T2U7H2V7D5:311E2W5;7L1U58301P26321G7M7C;I33577N345=7O355<9H7P36245>3=382737;Q5?7Q392G5@7R;O3;5A1K7S3:;U5B7T;V5C5D3<063@7V5E3A7U8:3?9K5F5G;H3B5I7W3C5U803D3E815J3F843G825K853L3K863M885L3N898=8;3O8>8<9I5O8?5M3P5P833>5S3Q448A255T3R8B87283S5H3T5V3H8C3U3I3V3W5W8D3J8E408@4241608F29478G8H5N438I8K61458J5Q488M2H9J63;F2;628N49;S;G4:64;R1Q8L5R654;2<46668O2=2@4<67;L4=912A688P4>;M698Q4A4B2B6:4Q6;4C;N8R4D2D8W6<906>;J929493958S964E6=6?4?2?974F6@2C984G8T4H6B4@4I8V8U994J2I6A4L9:4K9;2K4M9<4O4N9>9=4P4T4R6N2>4S9?6C9@;K4U4V9B<09A6D4W506E6F9C6G2E6L9D516M9E526Q9F539G6R54;49M6O9L9S6S6H9N6P9O6K9T<19P9U:V6I9Q:W<26J6T<8<36U<7<;;0<9;5<:9R;19V<4;29W:06V:4<<6W<5:5<===70:671;3<672:7=873:874:175:9<?7679;677:;:=7::2<>78<@;77;:3;8;<<V;9::<P<F=0;:<T<H;=<D<R=I=?=67<<B=><J;><A7=<Q;;<W;?:<7><G;@7?<I7@=2=1;B;A:>:?:D<E:@<S<C:E:A=H=@<U;E=7:FCS<K:B;C:C=4=3:G<N;D=5<L:H<O=D<M:I=J=9:J=A=:CT:K=;CR@Q:M=<:L=B:N:O;W:P=C:R=K:Q=N=L:S:U=O=M=E=PD0=F=Q=G:T=RCU=S@R=T@S=U=VCV=W>0>1CW>2D1>3D3>5D2@W@TD4>6>4D5>BD6D7>7D8D9D:>8D;>9D<D=>:><>>D>>;@UD?>?>=A0DA@VD@>@A1A3DM>AA4A5DBA2A6>EA7DC>CA8DD>FA9DG>DDEA:A;DHDFDIA<>GA>DKA=A?>HA@DL>IDJDNDPDODQALDR>JAA>KDS>LABDT>MACDU>NADAF>P>ODVAGAEAJDWE0AI>QAHAK>SE1>RE2AM>T>UE3E4E5AN?0E8E6?1>VE7E9E:AO>WAPE<?=AQASE;?2E=AT?3EHAUE>ARAV?4AWE?E@B0EAB1?5EFB2?6B3EBEG?7B4EEB6EI?:B5?8EKB8EJEL?;EMBCEO?<EP?@EQB9ECERED?AESB:B7ET?>B;EUB<EVEW??EN?9B=F0F2BAF1B@B>?CBBF4?BBDBFBEBG?DBHBI?EF5F3?FB?BJ?GF6BK?HF7?IBLF8?J?KF9BNBM?LF:F;BO?MBPF<?PF@?NBQF=FABRBSF?BTBV?Q?OBUFC?RBWFB?SC2FM?TFNC0FOF>C1?UFP?VFDC3?WFE@0FGC4@7FQ@1@2C5FHC6C7@3@8FWG1FVG0@4FIC8C>@9@:C9@6@;C:@<C?CAFJC;C@CBFKC<@5@C@D@EC=FL@F@GCCFTFS@=FUCDFF@HFR@>@?@@@O@PCG@M@N@ACE@BCHCF@I@L@J@KCICKCJCLCMCOCQCNCP"
 _R2 = [(r, c) for r in range(2) for c in range(NC)]
 _R3 = [k + (s,) for k in _R2 for s in range(S)]
 OPTS = ([("Z_V", k + (h,)) for k in _R3 for h in range(2)] + [(n, k + (h,)) for n in ("L_V", "L_M") for k in _R2 for h in range(2)]
@@ -75,11 +82,15 @@ OPTS = ([("Z_V", k + (h,)) for k in _R3 for h in range(2)] + [(n, k + (h,)) for 
         + [("A_V", k + (0, x)) for k in _R2 for x in "mr"] + [("A_V", (0, c, 0, "q")) for c in range(NC)]
         + [("A_V", (1, c, 0, "b")) for c in range(NC)] + [("A_V", k + (h, "e")) for k in _R2 for h in range(2)]
         + [("A_V", k + ("a",)) for k in _R3 if k[2] < 2] + [("A_V", ("k", i)) for i in range(1, 70)])
+OPTS = (sorted(OPTS, key=repr) + [("G_K", (n, j)) for n, k in (("lk", 8), ("lp", 8), ("ln", 1), ("q", 3)) for j in range(k)]
+        + [("K_T", k + (x,)) for k in _R3 for x in (1, 2)] + [("G_N", k + (x, n)) for k in _R3 for x in "md" for n in (2, 4)]
+        + [("G_K", ("d", n)) for n in "ident nident i97 n97 ik i8k f75".split()]
+        + [("G_K", ("f", n)) for n in "padb padf c0 two m0 m1".split()])
 SETS = {n: set() for n, _ in OPTS}
-for _c, (_n, _k) in zip(PICK, sorted(OPTS, key=repr)):
+for _c, (_n, _k) in zip(PICK, OPTS):
     if _c == "1":
         SETS[_n].add(_k)
-Z_V, L_V, L_M, M_V, U_V, U_S, D_S, A_V = [SETS[n] for n in ("Z_V", "L_V", "L_M", "M_V", "U_V", "U_S", "D_S", "A_V")]
+Z_V, L_V, L_M, M_V, U_V, U_S, D_S, A_V, G_K, K_T, G_N = [SETS[n] for n in "Z_V L_V L_M M_V U_V U_S D_S A_V G_K K_T G_N".split()]
 COLS = {}
 
 
@@ -100,6 +111,15 @@ def lanes(T, topo, rank, h):
     for s in dst:
         if s not in far:
             out[s] = topo.engines(core, T.cores[s])[-4:]
+    return out
+
+
+def single(T, topo, rank):
+    out = {}
+    for d in range(1, 8):
+        s = (rank + d) % 8
+        en = [x for x in topo.engines(T.cores[rank], T.cores[s]) if x not in out.values()]
+        out[s] = en[-1] if topo.chip(T.cores[s]) == topo.chip(T.cores[rank]) else en[0]
     return out
 
 
@@ -196,13 +216,26 @@ def graph():
             return ts(out, a, scale, A.mult, bias, A.add)
         return sa(out, a, F.Identity, scale=scale, bias=bias)
 
-    def pe(calls, R, Wr, cont=None):
+    def pe(calls, R, Wr, cont=None, more=60):
         def f(g, T, e):
             r = None
             for cy, o, l, x, st, sp in calls:
                 r = g.tensor.matmul(o(T), l(T), x(T), st, sp)
             return r
-        return add("T", sum(k[0] for k in calls) * PC + 60, f, R, Wr, cont=cont)
+        return add("T", sum(k[0] for k in calls) * PC + more, f, R, Wr, cont=cont)
+
+    def pes(calls, R, Wr, most=520):
+        k, part = None, []
+        for i, x in enumerate(calls):
+            part.append(x)
+            if i == len(calls) - 1 or sum(y[0] for y in part) + calls[i + 1][0] > most:
+                k, part = pe(part, R, Wr, k, 60 if i == len(calls) - 1 else 10), []
+
+    def gather(f, key, out, ind, *ins):
+        n = 4 if key + (4,) in G_N else 2 if key + (2,) in G_N else 1
+        cut = lambda x, k, w: (x[0], x[1] + k * w // n, x[1] + (k + 1) * w // n)
+        for k in range(n):
+            f(cut(out, k, CH), cut(ind, k, NN), *[cut(x, k, CH) for x in ins])
 
     def at(x):
         return lambda T: ap(T, x)
@@ -237,7 +270,7 @@ def graph():
     def top(x):
         return x[:3] + (lambda T: T[x[0]][0:64, x[1]:x[2]], x[2] - x[1])
 
-    def turn(out, *srcs):
+    def turn(out, *srcs, cut=False):
         n = wd(out)
         calls = []
         for src, idn in srcs:
@@ -246,6 +279,9 @@ def graph():
             calls.append([cy, at(out), win(src, 1), sl(idn, 0, 2 * n, 2), False, False])
         calls[0][4] = True
         calls[-1][5] = True
+        if cut:
+            k = pe(calls[:-2], [pad(s) for s, _ in srcs[:-1]] + [full(i) for _, i in srcs], [out], None, 10)
+            return pe(calls[-2:], [pad(srcs[-1][0]), full(srcs[-1][1])], [out], k)
         return pe(calls, [pad(s) for s, _ in srcs] + [full(i) for _, i in srcs], [out])
 
     nk = [0]
@@ -263,9 +299,9 @@ def graph():
             return g.iota(ap(T, out), pattern, base, cm)
         return add("G", 130 + wd(out) * 2 * VC, f, [], [out])
 
-    def gs(out, a, pattern, op, base, cm):
+    def gs(out, a, pattern, op, base, cm, other=0.0):
         return add("G", 170 + 2 * VC * wd(out),
-                   lambda g, T, e: g.affine_select(ap(T, out), ap(T, a), pattern, op, 0.0, base, cm), [a], [out])
+                   lambda g, T, e: g.affine_select(ap(T, out), ap(T, a), pattern, op, other, base, cm), [a], [out])
 
     def full(n):
         return (n, 0, SCRATCH[n][1][1])
@@ -288,7 +324,11 @@ def graph():
             lat=3500, pr=6e7)
     for c in range(NC):
         cur[0] = "0%d0" % c
-        un(c_("qa", c), ("qn", 0, 3 * CH, lambda T, c=c: T.qn[:, :, 128 * c:128 * c + 128], CH), 1.0, 0.0, (0, c, 0, "q"))
+        x = ("qn", 0, 3 * CH, lambda T, c=c: T.qn[:, :, 128 * c:128 * c + 128], CH)
+        if ("q", c) in G_K:
+            gs(c_("qa", c), x, [[0, CH]], A.is_ge, 0, 0)
+        else:
+            un(c_("qa", c), x, 1.0, 0.0, (0, c, 0, "q"))
     cur[0] = ""
     add("S", 60, lambda g, T, e: g.scalar.dma_start(T.wts[:, :], T.wt[:, :]), [], [full("wts")], sem="lw", inc=16, lat=2000, pr=5e7)
     lm = add("Y", 60, lambda g, T, e: g.sync.dma_start(T.mk0[:, 0:W], T.mk[:, :]), [], [("mk0", 0, W)], sem="lm0", inc=16,
@@ -298,9 +338,27 @@ def graph():
 
     cur[0] = "c"
     idn = ("idw", 2, 130)
-    icol, m12 = col("i"), col("m12")
+    icol = col("i")
+    eq, ge, lt = [lambda k, a=a: ("cmp", a + k, a + k + 1) for a in (0, 16, 32)]
+    m12 = lt(12)
+
+    def diag(n, v):
+        if ("d", n) in G_K:
+            nk[0] += 1
+            return gs(full(n), full("zero"), [[-1, 128]], A.not_equal, 0, 1, v)
+        return sc(full(n), idn, v)
+
+    def fill(key, out, v):
+        if ("f", key) in G_K:
+            return gs(out, ("ones", 0, wd(out)), [[0, wd(out)]], A.is_gt, 0, 0, v)
+        return ms(out, v)
+
+    def oh(lo, hi, step=1):
+        return ("ohw", 8 * lo, 8 * hi, lambda T: T.ohw[:, lo:hi:step, :], 8 * len(range(lo, hi, step)))
     gi(full("ip"), [[0, 1]], 0, 1, False)
     ms(full("ones"), 1.0)
+    ms(full("zero"), 0.0)
+    gs(oh(0, 16), ("ones", 0, 128), [[-1, 16], [-16, 8]], A.is_equal, 0, 1)
     gs(full("z8a"), ("ones", 0, 8), [[-16, 8]], A.is_ge, 0, 1)
     gs(full("z8"), full("z8a"), [[16, 8]], A.is_ge, 15, -1)
     gs(full("idw"), full("ones"), [[1, 132]], A.is_equal, -2, -1)
@@ -312,71 +370,78 @@ def graph():
     ts(col("i11"), icol, 11.0, A.min)
     sa(("e3", 0, 1), col("i11"), F.Exp, scale=17 * LN2, bias=-100 * LN2, more=1300.0)
     sa(("e3", 1, 2), col("i11"), F.Exp, scale=-17 * LN2, bias=64 * LN2)
-    for n, op, v in (("m12", A.is_lt, 12.0), ("c12", A.is_equal, 12.0), ("c13", A.is_equal, 13.0), ("c14", A.is_equal, 14.0)):
-        ts(col(n), icol, v, op)
+    for k, op in enumerate((A.is_equal, A.is_le, A.is_gt)):
+        ts(("cmp", 16 * k, 16 * k + 16), ("mrow", 0, 16), icol, op)
     z8 = full("z8")
-    ts(col("d0"), col("c12"), col("c13"), A.subtract)
-    ts(col("d1"), col("c13"), col("c14"), A.subtract)
-    for k, n in enumerate(("c12", "c13", "c14", "d0", "d1")):
-        sc(("wq", 8 * k, 8 * k + 8), z8, col(n))
-    ts(col("k0"), icol, 0.0, A.is_gt, m12, A.mult)
-    ts(col("k1"), ("e3", 0, 1), col("k0"), A.mult, -255.0 * 2.0 ** -48, A.mult)
+    tt(oh(15, 17), oh(12, 14), oh(13, 15), A.subtract)
+    ts(col("k0"), ge(1), m12, A.mult, -255.0 * 2.0 ** -48, A.mult)
+    sc(col("k1"), ("e3", 0, 1), col("k0"))
     sc(full("dk1"), idn, col("k1"))
-    ts(("i16", 2, 3), full("ip"), 7, A.bitwise_and)
-    cp(col("i8"), ("i16", 2, 3))
-    ts(("selm", 8, 16), ("mrow", 0, 8), col("i8"), A.is_equal)
+    if any(("lk", jl) not in G_K for jl in range(8)):
+        ts(("i16", 2, 3), full("ip"), 7, A.bitwise_and)
+        cp(col("i8"), ("i16", 2, 3))
+        ts(("selm", 8, 16), ("mrow", 0, 8), col("i8"), A.is_equal)
     pe([(128, at(top(("pe", 0, 128))), sl("bd", 0, 128, 2), at(full("dk1")), True, True)], [full("bd"), full("dk1")], [("pe", 0, 128)])
     sc(top(full("dk2")), top(("pe", 0, 128)), 1.0)
     for jl in range(8):
-        sc(top(("lk", 128 * jl, 128 * jl + 128)), top(full("dk2")), top(("selm", 8 + jl, 9 + jl)))
-    sc(full("ident"), idn, 1.0)
-    ts(col("s12"), m12, 2.0 ** -68, A.mult)
+        if ("lk", jl) in G_K:
+            gs(top(("lk", 128 * jl, 128 * jl + 128)), top(full("dk2")), [[-8, 8], [0, 16]], A.is_equal, -jl, 1)
+            nk[0] += 1
+        else:
+            sc(top(("lk", 128 * jl, 128 * jl + 128)), top(full("dk2")), top(("selm", 8 + jl, 9 + jl)))
+    diag("ident", 1.0)
+    sc(col("s12"), m12, 2.0 ** -68)
     sc(full("i68"), idn, col("s12"))
-    ts(col("zb"), col("c12"), col("c13"), A.add, 2.0 ** -68, A.mult)
+    ts(col("zb"), eq(12), eq(13), A.add, 2.0 ** -68, A.mult)
     for b in ("padb", "padf"):
         n = SCRATCH[b][1][1]
-        ms((b, 0, 8 * n, lambda T, b=b: T[b][:, 0::2, :], 4 * n), 0.0)
-    ms(("cc", 192, 320), 2.0 ** 29)
-    ts(full("thv"), ("mrow", 0, 16), icol, A.is_gt, col("s12"), A.mult)
-    cp(full("wtf"), full("wts"))
-    ts(col("h13"), col("c13"), 0.5, A.mult)
-    ts(col("ca"), col("c12"), -2048.0, A.mult, col("h13"), A.add)
-    ts(col("cb"), col("c12"), -4096.0, A.mult, col("h13"), A.add)
-    for k, (w, x) in enumerate(((0, "ca"), (1, "ca"), (1, "cb"))):
-        ts(col("u%d" % k), ("wtf", w, w + 1), col(x), A.add, 2.0 ** 68, A.mult)
-        sc(("wu1", 8 * k, 8 * k + 8), z8, col("u%d" % k))
+        x = (b, 0, 8 * n, lambda T, b=b: T[b][:, 0::2, :], 4 * n)
+        if ("f", b) in G_K:
+            gi(x, [[0, 4 * n]], 0, 0, True)
+        else:
+            ms(x, 0.0)
+    fill("c0", ("cc", 192, 320), 2.0 ** 29)
+    if M_V:
+        ts(full("thv"), ("mrow", 0, 16), icol, A.is_gt, col("s12"), A.mult)
+    sc(("wtf", 0, 2), full("wts"), 2.0)
+    ts(col("ca"), eq(12), -4096.0, A.mult, eq(13), A.add)
+    ts(col("cb"), eq(12), -8192.0, A.mult, eq(13), A.add)
+    ts(("wtf", 2, 4), ("wtf", 0, 2), col("ca"), A.add, 2.0 ** 67, A.mult)
+    ts(("wtf", 4, 5), ("wtf", 1, 2), col("cb"), A.add, 2.0 ** 67, A.mult)
+    sc(("wtf", 6, 8), ("wtf", 0, 2), -2.0 ** 67)
+    for k in range(3):
+        sc(("wu1", 8 * k, 8 * k + 8), z8, ("wtf", 2 + k, 3 + k))
     for k in range(2):
-        sc(("wu2", 8 * k, 8 * k + 8), z8, ("wtf", k, k + 1), -2.0 ** 68)
+        sc(("wu2", 8 * k, 8 * k + 8), z8, ("wtf", 6 + k, 7 + k))
     if U_V or U_S:
         sc(("wu3", 0, 16), full("wu2"), -1.0)
         sc(("wu3", 16, 24), ("wu1", 16, 24), 1.0)
+    if K_T:
+        diag("i8k", 8192.0)
     if M_V:
-        ms(full("two"), 0.125)
+        fill("two", full("two"), 0.0625)
+    if M_V:
         sc(("cc", 0, 128), ("ones", 0, 128), col("ca"))
         sc(("cc", 128, 192), ("ones", 0, 64), col("cb"))
     if U_S:
         sc(("wu1", 24, 40), ("wu3", 0, 16), 1.0)
-    sc(full("i97"), idn, 97.0)
-    sc(full("n97"), idn, -97.0)
+    diag("i97", 97.0)
+    diag("n97", -97.0)
     sc(full("identf"), idn, 1.0)
-    sc(full("ik"), idn, 2.0 ** -66)
-    ms(("mk0", W, W + 16), 2.0 ** 20)
-    ms(("mk1", W, W + 16), 2.0 ** 20)
-    sc(("wd0", 8, 24), ("wq", 0, 16), 1.0)
-    ts(col("we"), ("e3", 1, 2), m12, A.mult)
+    diag("ik", 2.0 ** -66)
+    fill("m0", ("mk0", W, W + 16), 2.0 ** 20)
+    fill("m1", ("mk1", W, W + 16), 2.0 ** 20)
+    sc(("wd0", 8, 24), oh(12, 14), 1.0)
+    sc(col("we"), ("e3", 1, 2), m12)
     sc(("wd0", 0, 8), z8, col("we"))
-    sc(full("nident"), idn, -1.0)
+    diag("nident", -1.0)
     if D_S:
-        ts(("i16", 1, 2), full("ip"), 1, A.bitwise_and)
-        ts(col("odd"), ("i16", 1, 2), 3.0, A.mult, 1.0, A.add)
-        ts(col("ev"), ("i16", 1, 2), -1.0, A.mult, icol, A.add)
-        ts(("mrow", 16, 22), ("mrow", 0, 6), 2.0, A.mult, col("ev"), A.is_equal)
-        ts(("mrow", 24, 30), ("mrow", 16, 22), col("we"), A.mult, col("odd"), A.mult)
-        for k in range(6):
-            sa(("wg", 8 * k, 8 * k + 8), z8, F.Copy, scale=("mrow", 24 + k, 25 + k))
-        sc(("wg", 48, 64), ("wq", 0, 16), 1.0)
+        sc(("wg", 64, 112), oh(1, 12, 2), col("we"), 4.0)
+        sc(("wg", 128, 176), oh(0, 12, 2), col("we"))
+        tt(("wg", 0, 48), ("wg", 64, 112), ("wg", 128, 176), A.add)
+        sc(("wg", 48, 64), oh(12, 14), 1.0)
         sc(("wg", 64, 112), ("wg", 0, 48), -1.0)
-        sc(("wg", 112, 128), ("wq", 8, 24), -1.0)
+        sc(("wg", 112, 128), oh(13, 15), -1.0)
         sc(("wg", 128, 176), ("wg", 0, 48), -1.0)
         sc(("wg", 176, 184), z8, 0.0)
 
@@ -389,11 +454,20 @@ def graph():
         mm(("pe", 128, 256), (full("bd"), full("dk3")))
         sc(full("dk4"), ("pe", 128, 256), 1.0)
         for jl in range(8):
-            sc(("lp", 128 * jl, 128 * jl + 128), full("dk4"), ("selm", jl, jl + 1))
-        sc(full("ln"), full("lp"), -1.0)
+            if ("lp", jl) in G_K:
+                gs(("lp", 128 * jl, 128 * jl + 128), full("dk4"), [[-16, 8], [0, 16]], A.is_equal, -8 - jl, 1)
+                nk[0] += 1
+            else:
+                sc(("lp", 128 * jl, 128 * jl + 128), full("dk4"), ("selm", jl, jl + 1))
+        if ("ln", 0) in G_K:
+            sc(full("dk3"), ("pe", 128, 256), -1.0)
+            for jl in range(8):
+                gs(("ln", 128 * jl, 128 * jl + 128), full("dk3"), [[-16, 8], [0, 16]], A.is_equal, -8 - jl, 1)
+        else:
+            sc(full("ln"), full("lp"), -1.0)
         sc(full("i75"), full("i68"), 2.0 ** -7)
         sc(full("n75"), full("i68"), -2.0 ** -7)
-        sc(full("f75"), idn, 2.0 ** -75)
+        diag("f75", 2.0 ** -75)
         if L_M:
             ts(("mrow", 32, 48), ("mrow", 0, 16), 3.0, A.add, icol, A.is_gt)
             ts(("mrow", 48, 64), ("mrow", 0, 16), 0.0, A.is_gt, m12, A.mult)
@@ -402,19 +476,18 @@ def graph():
     def edit_constants():
         gi(full("trow"), [[0, 2], [1, 128]], 0, 0, True)
         gi(full("t16a"), [[0, 2], [16, 8]], 0, 0, True)
-        gi(full("iot"), [[256, 8208]], 0, 0, True)
-        ts(full("t16"), full("t16a"), icol, A.add)
-        ts(full("t16b"), full("t16"), 16.0, A.add)
-        ts(full("dump16"), full("t16"), 8208.0, A.add)
-        ts(col("ge13"), icol, 13.0, A.is_ge)
-        ts(col("ge14"), icol, 14.0, A.is_ge)
+        for k in range(4):
+            gi(("iot", 2052 * k, 2052 * k + 2052), [[256, 2052]], 256 * 2052 * k, 0, True)
+        sa(full("t16"), full("t16a"), F.Identity, bias=icol)
+        sa(full("t16b"), full("t16"), F.Identity, bias=15.0)
+        sa(full("dump16"), full("t16"), F.Identity, bias=8208.0)
         sc(full("isym"), idn, m12)
-        sc(full("sh1"), ("idw", 3, 131), col("ge13"))
-        sc(full("sh2"), ("idw", 4, 132), col("ge14"))
-        ts(full("sel1"), ("mrow", 0, 16), 2.0, A.is_equal)
-        ts(full("sel2"), ("mrow", 0, 16), 1.0, A.is_equal)
-        sc(full("mt"), ("mrow", 0, 16), col("c12"))
-        ts(col("wcm"), icol, 15.0, A.is_lt, m12, A.subtract)
+        sc(full("sh1"), ("idw", 3, 131), ge(13))
+        sc(full("sh2"), ("idw", 4, 132), ge(14))
+        gs(full("sel1"), ("ones", 0, 16), [[1, 16]], A.is_equal, -2, 0)
+        gs(full("sel2"), ("ones", 0, 16), [[1, 16]], A.is_equal, -1, 0)
+        sc(full("mt"), ("mrow", 0, 16), eq(12))
+        sc(col("wcm"), lt(15), ge(12))
         sc(full("spa"), ("idw", 1, 129), col("wcm"))
         tt(full("spl"), full("spa"), full("isym"), A.add)
 
@@ -425,61 +498,75 @@ def graph():
         ss, key = ("vp", c * 128, c * 128 + 64), ("vp", c * 128 + 64, c * 128 + 128)
         hit, zz, dd = c_("hit", c), c_("zz", c), c_("dd", c)
         kb = pad("xk%d" % c)
-        r = lambda k: c_("ra", c, 64 * k, 64 + 64 * k)
+        ra = "ra2" if rd else "ra"
+        r = lambda k: c_(ra, c, 64 * k, 64 + 64 * k)
         n2, mp, tp, xm = c_("rb", c, 0, 64), "mp%d" % c, "tp%d" % c, c_("rb", c, 64, 128)
         m = pad(mp)
         cur[0] = "%d%d0" % (rd, c)
-        pe(feats(pn, 0, full("wq"), (rd, c), True, True), [q, full("wq")], [(pn, 0, 320)])
-        un(m if (rd, c, 0) in M_V else r(0), (pn, 0, 64), 1.0, 0.0, (rd, c, 0, "m"))
+        if rd == 0:
+            pe(feats(pn, 0, oh(12, 17), (rd, c), True, True), [q, oh(12, 17)], [(pn, 0, 320)])
         if (rd, c, 0) in M_V:
-            un(c_("ra", c, 0, 320), (pn, 0, 320), 1.0, 0.0, (rd, c, 0, "r"))
+            un(m, r(0) if rd else (pn, 0, 64), 1.0, 0.0, (rd, c, 0, "m"))
+            if rd == 0:
+                un(c_("ra", c, 0, 320), (pn, 0, 320), 1.0, 0.0, (rd, c, 0, "r"))
         else:
-            un(c_("ra", c, 64, 320), (pn, 64, 320), 1.0, 0.0, (rd, c, 0, "r"))
+            if rd == 0:
+                un(r(0), (pn, 0, 64), 1.0, 0.0, (rd, c, 0, "m"))
+                un(c_("ra", c, 64, 320), (pn, 64, 320), 1.0, 0.0, (rd, c, 0, "r"))
             m = r(0)
         for st in range(S):
             cur[0] = "%d%d%d" % (rd, c, st)
             byv, umv = (rd, c, st) in M_V, (rd, c, st) in U_V
             sa(pad(fx), m, F.Exp, scale=-17 * LN2, bias=80 * LN2)
             if byv:
-                turn((pw, 64, 128), (mp, "ident"))
-                cp(c_("ml", c), (pw, 64, 128))
-                tt(zz, full("thv"), q, A.mult, ind=c_("ml", c))
+                turn((pw, 448, 512), (mp, "ident"))
+                cp(c_("ml", c), (pw, 448, 512))
+                gather(lambda o, i, x: tt(o, full("thv"), x, A.mult, ind=i), (rd, c, st, "m"), zz, c_("ml", c), q)
             else:
                 parts = [r(0)] if st == 0 else [r(1) if st == 1 else n2, xm]
-                o = top((pw, 0, 128))
+                o = top((pn, 128, 256))
                 pe([(128, at(o), at(x), at(full("ident")), k == 0, k == len(parts) - 1) for k, x in enumerate(parts)],
                    parts + [full("ident")], [o])
                 sa(top(c_("fts", c)), o, F.Exp, scale=-17 * LN2, bias=80 * LN2)
-                for h, bank in ((0, pn), (1, pw)):
-                    calls = []
-                    for jl in range(4 * h, 4 * h + 4):
-                        o = (bank, 128 * (jl % 4), 128 * (jl % 4) + 128)
-                        calls.append((128, at(o), at(full("i68")), at(qv(rd, c, None, jl)), True, False))
-                        calls.append((128, at(o), at(top(("lk", 128 * jl, 128 * jl + 128))), at(top(c_("fts", c))), False, True))
-                    pe(calls, [q, full("i68"), ("lk", 512 * h, 512 * h + 512), c_("fts", c)], [(bank, 0, 512)])
+                for h, bank in ((0, pw), (1, pn)):
+                    k, both = None, ["q", "f"][::-1 if rd == 1 and st == 0 else 1]
+                    for x in both:
+                        calls = []
+                        for jl in range(4 * h, 4 * h + 4):
+                            o, a, z = (bank, 128 * (jl % 4), 128 * (jl % 4) + 128), k is None and jl % 4 == 0, k is not None and jl % 4 == 3
+                            if x == "q":
+                                calls.append((128, at(o), at(full("i68")), at(qv(rd, c, None, jl)), a, z))
+                            else:
+                                calls.append((128, at(o), at(top(("lk", 128 * jl, 128 * jl + 128))), at(top(c_("fts", c))), a, z))
+                        k = pe(calls, [q, full("i68")] if x == "q" else [("lk", 512 * h, 512 * h + 512), c_("fts", c)],
+                               [(bank, 0, 512)], k, 10 if k is None else 60)
                     if (rd, c, st, h) in Z_V:
                         ts(c_("zz", c, 512 * h, 512 * h + 512), (bank, 0, 512), col("zb"), A.add, 0.0, A.max)
                     else:
                         sa(c_("zz", c, 512 * h, 512 * h + 512), (bank, 0, 512), F.Relu, bias=col("zb"))
-            ky = (pw, 0, 64)
-            un(ky, m, 8192.0, float((st + 1) << 18), (rd, c, st, "y"))
+            kt = 2 if (rd, c, st, 2) in K_T else 1 if (rd, c, st, 1) in K_T else 0
+            if (rd, c, st) in D_S:
+                kt = min(kt, 1)
+            ky = (pn, 64, 128)
+            if not kt:
+                un(ky, m, 8192.0, 0.0, (rd, c, st, "y"))
             ums = (rd, c, st) in U_S and not umv
-            u, u12, ta = (pn, 0, 320 if ums else 192), (pn, 0, 128), (pn, 128, 192)
+            u, u12, ta = (pw, 0, 320 if ums else 192), (pw, 0, 128), (pw, 128, 192)
             wu = full("wu3") if umv else ("wu1", 0, 40 if ums else 24)
             big = lambda l: (128, at(u12), at(full(l)), at(("cc", 192, 320)), False, False)
             m97 = lambda first, last: (64, at(ta), at(full("i97")), at(m), first, last)
-            cst = lambda lo, first: (192 - lo, at((pn, lo, 192)), at(full("two")), at(("cc", lo, 192)), first, False)
+            cst = lambda lo, first: (192 - lo, at((pw, lo, 192)), at(full("two")), at(("cc", lo, 192)), first, False)
             R = [full(x) for x in ("i97", "n97", "two", "cc", "wu2")] + [wu, m]
             step, late = 8 if byv else 1, umv or ums
             head = [] if late else [cst(0, True), m97(False, False)] if byv else [m97(True, False), big("i97")]
             if not byv:
-                head += feats(pn, 0, wu, zz, late, False, range(4), 1)
+                head += feats(pw, 0, wu, zz, late, False, range(4), 1)
             k = pe(head, R + ([] if byv else [c_("zz", c, 0, 512)]), [u]) if head else None
-            rest = feats(pn, 0, wu, zz, not head, False, range(8) if byv else range(4, 8), step)
+            rest = feats(pw, 0, wu, zz, not head, False, range(8) if byv else range(4, 8), step)
             if late:
                 rest += ([cst(128 if umv else 0, False)] if byv else []) + [m97(False, True)]
             else:
-                rest += ([big("i97")] if byv else []) + [big("n97")] + feats(pn, 0, full("wu2"), zz, False, True, range(8), step)
+                rest += ([big("i97")] if byv else []) + [big("n97")] + feats(pw, 0, full("wu2"), zz, False, True, range(8), step)
             pe(rest, R + [zz], [u], cont=k)
             if umv:
                 cp(c_("ui", c), u12)
@@ -488,19 +575,32 @@ def graph():
             elif ums:
                 sa(c_("ta", c), u12, F.Identity, bias=M12)
                 sa(c_("tb", c), c_("ta", c), F.Identity, bias=-M12)
-                tt(c_("cs", c), (pn, 256, 320), c_("tb", c, 64, 128), A.subtract)
-                tt(key, (pn, 192, 256), c_("tb", c, 0, 64), A.subtract)
-                tt(c_("pp", c), key, c_("cs", c), A.mult)
+                tt(c_("cs", c), (pw, 256, 320), c_("tb", c, 64, 128), A.subtract)
+                tt(ss, (pw, 192, 256), c_("tb", c, 0, 64), A.subtract)
+                tt(c_("pp", c), ss, c_("cs", c), A.mult)
             else:
-                un(c_("cs", c), (pn, 64, 128), 1.0, 0.0, (rd, c, st, "c"))
-                tt(c_("pp", c), (pn, 0, 64), c_("cs", c), A.mult)
+                un(c_("cs", c), (pw, 64, 128), 1.0, 0.0, (rd, c, st, "c"))
+                tt(c_("pp", c), (pw, 0, 64), c_("cs", c), A.mult)
             ts(c_("kk", c), c_("pp", c), 5, A.arith_shift_right)
-            tt(pad(xf), (pn, 128, 192), c_("kk", c), A.add)
-            ts(pad(tp), pad(xf), M13, A.add, M13, A.subtract)
-            turn((pn, 192, 256), (xf, "identf"), (fx, "ik"), (tp, "nident"))
-            ts(c_("hl", c), (pn, 192, 256), HALF, A.add, float(W), A.min)
-            tt(ss, ky, pad(tp), A.subtract)
-            tt(key, ss, pad(xf), A.add)
+            tt(pad(xf), ta, c_("kk", c), A.add)
+            tag = float((st + 1) << 18)
+            ts(pad(tp), pad(xf), M13, A.add, M13 + tag, A.subtract)
+            turn((pw, 384, 448), (fx, "ik"), (xf, "identf"), (tp, "nident"), cut=True)
+            ts(c_("hl", c), (pw, 384, 448), HALF - tag, A.add, float(W), A.min)
+            key = ("vp", c * 128 + 64, c * 128 + 128)
+            if kt:
+                parts = [(full("i8k"), m), (full("nident"), pad(tp))]
+                calls = [(64, at(ky), at(l), at(x), k == 0, k == 1 and kt == 1) for k, (l, x) in enumerate(parts)]
+                if kt == 2:
+                    calls.append((256, at(ky), at(full("identf")), at(pad(xf)), False, True))
+                pe(calls, [x for p in parts for x in p] + [pad(xf), full("identf")], [ky])
+                if kt == 2:
+                    key = ky
+                else:
+                    tt(key, ky, pad(xf), A.add)
+            else:
+                tt(ss, ky, pad(tp), A.subtract)
+                tt(key, ss, pad(xf), A.add)
             if rd == 0 and c == 0:
                 sa(full("act"), m, F.Sign)
                 if st == 0:
@@ -510,7 +610,7 @@ def graph():
                     tt(pad("xa"), ("vp", 384, 448), pad("xa"), A.max)
             nf, d0, d1 = 64 - 8 * st, (pn, 384, 448), (pn, 448, 512)
             if (rd, c, st) in D_S:
-                sa(dd, mk, F.Copy, ind=c_("hl", c))
+                gather(lambda o, i: sa(o, mk, F.Copy, ind=i), (rd, c, st, "d"), dd, c_("hl", c))
                 o, wq = (pn, 0, 8 * nf), (("wg", 64, 128), ("wg", 128, 184), ("wg", 64, 112))[st]
                 k = pe(feats(pn, 0, wq, (rd, c), True, False) + ([(64, at(d0), at(full("nident")), at(n2), False, False)] if st == 1 else []),
                        [q, wq, full("nident"), n2], [o])
@@ -519,14 +619,14 @@ def graph():
                 ea = (pn, 0, 64)
                 mm(ea, *[(full("ident"), c_("da", c, 64 * i, 64 * i + 64)) for i in range(6)])
             else:
-                tt(dd, mk, q, A.subtract, ind=c_("hl", c))
+                gather(lambda o, i, x: tt(o, mk, x, A.subtract, ind=i), (rd, c, st, "d"), dd, c_("hl", c), q)
                 o, ea = (pn, 320, 512 - 64 * st), (pn, 256, 320)
                 calls = feats(pn, 320, ("wd0", 0, 24 - 8 * st), dd, True, st == 2)
                 if st == 0:
-                    calls.append((128, at((pn, 384, 512)), at(full("ident")), at(c_("ra", c, 192, 320)), False, True))
+                    calls.append((128, at((pn, 384, 512)), at(full("ident")), at(c_(ra, c, 192, 320)), False, True))
                 if st == 1:
                     calls += [(64, at(d0), at(full("nident")), at(n2), False, False), (64, at(d0), at(full("ident")), at(r(0)), False, True)]
-                pe(calls, [full("ident"), full("nident"), c_("ra", c), full("wd0"), dd] + ([n2] if st == 1 else []), [o])
+                pe(calls, [full("ident"), full("nident"), c_(ra, c), full("wd0"), dd] + ([n2] if st == 1 else []), [o])
                 sa(ea, (pn, 320, 384), F.Abs)
             tt(hit, ea, pad(fx), A.is_lt)
             if st < 2:
@@ -535,7 +635,7 @@ def graph():
                 if (rd, c, st, "a") in A_V:
                     tt(m, xm, r(1) if st == 0 else n2, A.add)
                 else:
-                    x = (pw, 128, 192)
+                    x = (pn, 0, 64)
                     mm(x, (full("ident"), r(1) if st == 0 else n2), (full("ident"), xm))
                     sa(m, x, F.Copy)
             if st == 0:
@@ -543,8 +643,8 @@ def graph():
                 tt(n2, d1, r(2), A.add)
                 tt(kb, key, hit, A.mult)
             else:
-                tt(key, key, hit, A.mult)
-                tt(kb, key, kb, A.max)
+                tt(ss, key, hit, A.mult)
+                tt(kb, ss, kb, A.max)
 
     def learn(rd, c):
         nw = "nwa" if rd == 0 else "nwb"
@@ -554,7 +654,7 @@ def graph():
         kb = pad(xk)
         cur[0] = "%d%d3" % (rd, c)
         ts(pad(tp), kb, M13, A.add, M13, A.subtract)
-        turn((pn, 192, 256), (xk, "identf"), (tp, "nident"))
+        turn((pn, 192, 256), (xk, "identf"), (tp, "nident"), cut=True)
         ts(c_("bl", c), (pn, 192, 256), HALF, A.add, float(W), A.min)
 
         def hv(n, h, w):
@@ -595,8 +695,27 @@ def graph():
                     calls.append((64, sl(bank, jl, 512, 8), at((l, 128 * jl, 128 * jl + 128)),
                                   at(hv("fts", h, 64)), False, False))
             calls.append((512, at(o), at(full("f75")), at(qh), False, True))
-            pe(calls, [qh, lh, full("i75"), full("n75"), full("f75"), full("lp"), full("ln"), c_("fts", c)], [o])
+            pes(calls, [qh, lh, full("i75"), full("n75"), full("f75"), full("lp"), full("ln"), c_("fts", c)], [o])
             sa(hv(nw, h, 512), o, F.Relu, scale=2.0 ** 75, bias=-2.0 ** -10)
+
+    def ropes():
+        add("Y", 60, lambda g, T, e: g.sync.dma_start(T.ro1[:, :, :], T.ra[:, :]), [full("ra")], [("ro1", 0, 8)], sem="r1", inc=16,
+            lat=2500)
+
+        def f(g, T, e):
+            core, rank, topo = e
+            moves = []
+            for s, en in single(T, topo, rank).items():
+                ad = topo.addr(T.cores[s])
+                moves.append(RemoteDMATransfer(dst_ids=[DstId(rid=ad[0], pnc=ad[1])], dma_engine_mask=1 << en,
+                                               remote_sem=T.sem["arrr"], src=T.ro1[s], dst=T.ro2[rank]))
+            return g.remote_dma_fused(moves, local_sem=T.sem["sntr"])
+        i = add("G", 4000, f, [("ro1", 0, 8)], [], sem="noner", inc=0)
+        first.append(i)
+        j = add("arrr", 0, None, [], [], sem="arrr", inc=7, lat=12000, deps=(i,))
+        k = add("Y", 60, lambda g, T, e: g.sync.dma_start(T.ro2[e[1]], T.ro1[e[1]]), [("ro1", 0, 8)], [], sem="r2", inc=16, lat=2500)
+        add("Y", 60, lambda g, T, e: g.sync.dma_start(T.ra2[:, :], T.ro2[:, :, :]), [], [full("ra2")], sem="r3", inc=16, lat=2500,
+            deps=(j, k))
 
     first = []
 
@@ -611,8 +730,8 @@ def graph():
                     src=T.nwa[:, c * CH + 128 * s:c * CH + 128 * s + 128],
                     dst=T.qb[:, c * CH + 128 * rank:c * CH + 128 * rank + 128]))
             return g.remote_dma_fused(moves, local_sem=T.sem["snt%d" % c])
-        i = [add("G", 1000 if c or h else 4000, lambda g, T, e, h=h: f(g, T, e, h), [c_("nwa", c, 512 * h, 512 * h + 512)], [], sem="none%d%d" % (c, h), inc=0,
-                 cont=first[0] if c or h else first.append(len(ops)))
+        i = [add("G", 1000 if c or h else 1500, lambda g, T, e, h=h: f(g, T, e, h), [c_("nwa", c, 512 * h, 512 * h + 512)], [], sem="none%d%d" % (c, h), inc=0,
+                 cont=first[0])
              for h in (0, 1)]
         add("arr%d" % c, 0, None, [], [c_("qb", c)], sem="arr%d" % c, inc=1, lat=5500, deps=i)
 
@@ -629,18 +748,17 @@ def graph():
         turn(("pe", 264, 272), ("xk0", "identf"))
         ts(full("k2"), ("pe", 256, 272), HALF, A.add)
         ts(full("fb"), full("k2"), W - 1, A.bitwise_and)
-        ts(full("mfi"), a8("k2", 0), 13, A.arith_shift_right, 15, A.bitwise_and)
-        ts(full("sbi"), a8("k2", 1), 18, A.arith_shift_right)
-        cp(full("sbl"), full("sbi"))
+        ts(a8("mfi", 0), a8("k2", 0), 13, A.arith_shift_right, 15, A.bitwise_and)
+        ts(a8("mfi", 1), a8("k2", 1), 18, A.arith_shift_right)
         cp(full("mfl"), full("mfi"))
         tt(full("ed1"), a8("k2", 0), a8("k2", 1), A.is_gt)
         ts(full("ed0"), a8("k2", 1), 8192.0, A.is_gt)
         for k in (0, 1):
             tt(a8("ed", k), full("ed1"), full("ed0"), A.mult)
-        ts(full("fbm"), full("fb"), -8192.0, A.add)
+        ts(full("fbm"), full("fb"), -8193.0, A.add)
         tt(full("fbe"), full("fbm"), full("ed"), A.mult)
-        ts(full("flu"), full("fbe"), 8192.0, A.add)
-        ts(full("nb"), full("fbe"), -256.0, A.mult, -2097152.0, A.add)
+        ts(full("flu"), full("fbe"), 8193.0, A.add)
+        sa(full("nb"), full("fbe"), F.Identity, scale=-256.0, bias=-256.0 * 8193)
         tt(full("krow"), full("iot"), full("trow"), A.add, ind=full("flu"))
         for k in range(16):
             h, n = 128 * (k // 8), 16 * (k % 8 + 1)
@@ -648,20 +766,19 @@ def graph():
             add("V", vdur(n), lambda g, T, e, k=k, n=n: g.vector.tensor_reduce(
                 T.first[:, k:k + 1], T.dk[:, 128 * k:128 * k + n], AxisListType.X, A.min, apply_absolute_value=True),
                 [("dk", 128 * k, 128 * k + n)], [("first", k, k + 1)])
-        tt(full("gg"), full("fbm"), full("t16b"), A.subtract)
-        tt(full("gg"), full("gg"), full("ed"), A.mult)
+        tt(full("gg"), full("fbe"), full("t16b"), A.subtract)
         tt(full("win"), full("first"), full("t16"), A.is_equal)
         tt(full("gg"), full("gg"), full("win"), A.mult)
         tt(full("tgt"), full("gg"), full("dump16"), A.add)
         cp(full("tgu"), full("tgt"))
         sa(full("g0"), ("mk0", 0, W + 16), F.Copy, ind=bl)
-        tt(full("ga1"), full("sel1"), full("g0"), A.mult, ind=full("sbl"))
-        tt(full("ga2"), full("sel2"), full("g0"), A.mult, ind=full("sbl"))
+        tt(full("ga1"), full("sel1"), full("g0"), A.mult, ind=a8("mfl", 1))
+        tt(full("ga2"), full("sel2"), full("g0"), A.mult, ind=a8("mfl", 1))
         mm(("pe", 0, 128), (full("sh1"), full("ga1")), (full("sh2"), full("ga2")), (full("isym"), ("qa", 0, 128)))
         sa(full("wnew"), ("pe", 0, 128), F.Copy)
         scat(full("mk1"), ("tgu", 0, 8), full("wnew"))
         sa(full("g1"), ("mk1", 0, W + 16), F.Copy, ind=bl)
-        sa(full("mfw"), full("mt"), F.Copy, ind=full("mfl"))
+        sa(full("mfw"), full("mt"), F.Copy, ind=a8("mfl", 0))
         mm(("pe", 0, 128), (full("spl"), full("g1")), (full("ident"), full("mfw")))
         sa(full("snew"), ("pe", 0, 128), F.Copy)
         scat(full("mk1"), ("tgu", 8, 16), full("snew"))
@@ -690,6 +807,9 @@ def graph():
     learn_constants()
     for c in range(NC):
         search(0, c)
+    cur[0] = "r"
+    ropes()
+    for c in range(NC):
         learn(0, c)
         move(c)
     cur[0] = "k"
@@ -775,6 +895,7 @@ def rank_program(g, core, T, topo):
     for c in range(NC):
         total["arr%d" % c] = sum(len(lanes(T, topo, s, rank // 4)[rank]) for s in range(8) if s != rank)
         total["snt%d" % c] = sum(len(en) for h in (0, 1) for en in lanes(T, topo, rank, h).values())
+    total["sntr"] = 7
     RANK[0] = rank
     count, stamp, clock, known = {}, {}, {}, {}
     for i in order:

import math
from concourse.bass import DstId, RemoteDMATransfer
from concourse.mybir import AluOpType, AxisListType, ActivationFunctionType

A = AluOpType
F = ActivationFunctionType
W, NC, CH, NN, S = 8192, 3, 1024, 64, 3
LN2 = math.log(2.0)
M12, M13, M18 = 1.5 * 2.0 ** 35, 1.5 * 2.0 ** 36, 1.5 * 2.0 ** 41
HALF = 4095.5

SCRATCH, BANKS = {}, []


def _b(dtype, where, spec, k=1):
    for x in spec.split():
        n, w = x.split(":")
        SCRATCH[n] = (where, [128, k * int(w)], dtype)
        if where == "psum":
            BANKS.append(n)


_b("bfloat16", "sbuf", "mk0:8208 mk1:8336 wts:2 ones:132 idw:132 ident:128 nident:128 i97:128 n97:128 i68:128 ik:128 i75:128 "
   "n75:128 f75:128 bda:128 bd:128 dk1:128 dk2:128 dk3:128 dk4:128 lk:1024 lp:1024 ln:1024 e3:3 wu1:40 wu2:16 wu3:24 cc:512 i8k:128 two:128 thv:16 th3:16 zero:128 wd0:24 wg:184 "
   "isym:128 sh1:128 sh2:128 spl:128 spa:128 z8a:8 z8:8 sel1:16 sel2:16 "
   "mt:16 g0:128 ga1:128 ga2:128 wnew:128 g1:128 mfw:128 snew:128")
_b("int32", "sbuf", "ip:1 i16:3 k2:16 fb:16 mfi:16")
_b("uint16", "sbuf", "flu:16 tgu:16 mfl:16")
_b("float32", "sbuf", "col:40 identf:128 selm:16 wtf:8 cmp:48 mrow:64 iot:8208 trow:256 "
   "t16a:16 t16:16 t16b:16 dump16:16 act:64 ed1:8 ed0:8 ed:16 fbm:16 fbe:16 nb:16 krow:256 dk:2048 first:16 win:16 "
   "gg:16 tgt:16")
SCRATCH["yby"] = ("sbuf", [128, 8, 24], "float32")
SCRATCH["qn"] = ("sbuf", [128, 8, 384], "bfloat16")
SCRATCH["ohw"] = ("sbuf", [128, 17, 8], "bfloat16")
SCRATCH["ro1"] = ("dram", [8, 128, 120], "bfloat16")
SCRATCH["ro2"] = ("dram", [8, 128, 120], "bfloat16")
PADS = {}
for _n, _d, _l in (("padf", "float32", "xf0 xf1 xf2 xk0 xk1 xk2 xa"), ("padb", "bfloat16", "fx0 fx1 fx2 mp0 mp1 mp2 tp0 tp1 tp2")):
    SCRATCH[_n] = ("sbuf", [128, 18 * len(_l.split()), 8], _d)
    for _k, _x in enumerate(_l.split()):
        PADS[_x] = (_n, 18 * _k)
_b("bfloat16", "sbuf", "qa:1024 qb:1024 zz:1024 dd:1024 ld:1024 nwa:1024 nwb:1024 ra:320 ra2:320 rb:128 fts:128 hit:64 da:384", NC)
_b("float32", "sbuf", "ta:128 tb:128 cs:64 ybx:64", NC)
_b("int32", "sbuf", "pp:64 kk:64 ui:128 ac:128", NC)
_b("uint16", "sbuf", "hl:64 bl:64 ml:64", NC)
_b("float32", "psum", "pn0:512 pn1:512 pn2:512 pw0:512 pw1:512 pw2:512 vp:512 pe:512")

SEMAPHORES = ["sT", "sV", "sS", "sG", "lw", "lq", "lm0", "lm1", "lyb", "r1", "r2", "r3", "arrr", "sntr"]
for _c in range(NC):
    SEMAPHORES += ["slf%d" % _c, "arr%d" % _c, "snt%d" % _c, "out%d" % _c]

VC, PC, VG, VGS, OV, OS, WAKE = 1.016, 0.51, 1.56, 1.56, 30.0, 60.0, 120.0
BIAS = {}
SOFT = False
from_plan = True
Z_V = {(1,2,2,1),(0,0,2,1),(0,1,0,0),(1,1,1,0),(0,1,2,0),(1,2,0,0),(1,0,0,1),(1,2,1,0),(0,2,1,0)}
L_V = {(1,2,1),(0,2,1),(1,0,1),(1,1,0),(0,1,0),(1,2,0),(0,2,0),(1,0,0),(0,0,1),(1,1,1),(0,1,1)}
M_V = {(1,0,0),(0,1,2)}
U_V = {(1,2,1),(0,2,1),(1,0,1),(1,1,0),(1,2,0),(0,2,0),(0,0,0),(1,1,2),(1,0,0),(1,2,2),(0,0,2),(0,1,2),(0,2,2),(1,0,2),(0,0,1),(1,1,1),(0,1,1)}
U_S = {(1,0,1),(1,1,0),(0,2,0),(1,2,2),(0,2,2),(1,0,2),(0,0,1),(1,1,1)}
D_S = {(1,1,0),(0,1,0),(1,1,2),(0,1,2),(0,2,2)}
A_V = {(1,2,2,'c'),(0,1,1,'c'),(0,1,1,'y'),(1,1,0,'r'),(0,1,2,'c'),(1,0,2,'c'),(0,0,2,'c'),(1,2,1,'c'),(0,1,0,'r'),(1,1,0,'y'),(1,2,0,'m'),(1,0,0,'c'),(0,2,2,'c'),(0,1,0,'y'),(0,0,1,'c'),(1,2,0,'y'),(0,0,2,'y')}
ORDER = "0001040517060<190;0=150>080O0?0A0B0D090C0L0F0E1107121:0:1K0H0G0J0I;20K1>0@1P0M130N1@1O0P1=1?0R0T0Q0S1G021L0W8>1H1A101M1E5O1C1B8?1F0U1D1T2W5P241I0V5Q5S308B5T2633218C1U5W8@1J1Q27253418285U161R601S2A20222?8F2F315V8A2;5R1V8D238G14612D1;3F2E628E2T1<2V632U;>;;;62<;<;=2=;98I;?64;7;88J29652:;:372>8K2G668H8L32678M3568388N698O2@8P6:2H368Q6<8T2I8R6;1W39;@3:8S1N6>2C036=8U3;2J3<2N6?2B2Q3=2M8V3>6@3?3@8W6A2L3A902P3B912O6B3C922R6C6E2K6D9793963D6I94983H6J996H9;9:3I9<6F3E9>3J952S9=6K;03K3G3L;16M3N6L3M3O6G3P4=;39?6N;4;56P9@3R9A3S6O6Q9B3Q3T9C9D9E9F6R3U9G9I6S6T3V9H6U9J413W4042439K6V446W45709L467173479M489N49729O4:749R9S9T9U4;9W4<9V4@:0:275:376:1:44A77:578:64B79:74C7<7=:84D:94E::4H4I9P4>:;7>4J4?9Q7@4F544M:<7?:>4K:?4N7A4L4G7B4P:=7C4Q4O7D:@4R7E4S:A7F4T7G4U7H:B4V7:4W7I:C50:D5351:E7J:F7L:L:G52:M:H557;567K7M:I:J;A:N:O7N57:P7O7P:K:Q5859:T7Q:R7R5:7S5;7T5<7U825=5C5>5D837V:S5E7W5?805F:U:W84;B855@81865A:V;C<P;J;D;I;M88;K87;L;F;N;G;O;P;Q8:5B5G89<H<J<R8;8=<8<I<4<Q<D<2<5<><K5I<3;T<95H<E8<<?;U;E<B;H5K<0<C<6<1;V<S<:;W5J<;<7BI<@5L5N<F<A;R<<BJ<T<GBM<=BL;SBN<LBK<MBQ5M<N<W<O<UBOBR<VBP=0BS=1BTBUBV?NBWC0?OC1?P?Q?R?SC2C3?TC4=2C5C7?U?VC6C8@1?W=3=4@2=5=7=6@3C9=8@4=:@0@5C:@6@7C;@8C<@9C=C>@:@<CAC?C@CB@;=9CC@>@=CDCFCE=;CG@?=<CHCI==@@CJ=>=?@A=@CK=A@B=BCL=C@C@E@DCM@H@I@F=DCN@J=F@M@K@NCO=G@L@OCP=H=E@PCQ=ICRCT=J=L=K=M@G=O=PCS@Q=N=QCU=T=R=U@RCV=S@S@TCW@U=W=VD0@V>0D1@WD2A0>1D5D6A3A1>2D7D3>3D8A2>4A4D:D9D=>5D;A5>6A6D4D>D<>7A7>8>:A8A:A9D?A<A=>9D@A>>;A?AAA@DA><A;ABDBDCADDD>=AEACDE>>DHDF>?>A>@AF>C>DDG>B>EDI>F>H>GAGDJ>IAH>KAIAJDK>L>JAKDLAL>MAMDM>NDN>ODO>PDPAN>QDQDUAP>RDV>SAQDRE1DT>TDW>UE2E0>WARE7ASDSATE8?0>VAOE5?1E>AUE=E3E?E@?2AV?3AW?4B0?5B6?6B1?;?7B7?<?=?8B2???>?:B8B9E6B3?@?DB5E:E<E9E;?9B??EB4?J?K?L?MB:?B?AB@B;B<E4BGBFBHBEB=?C?F?G?H?IB>BABBBDBC"
Z_V = {(0,1,0,1),(0,2,0,1),(1,1,2,0),(0,1,2,1),(1,1,1,0),(0,0,0,0),(0,1,2,0),(1,0,1,0),(1,2,0,0),(0,0,1,1)}
L_V = {(1,2,1),(0,2,1),(1,0,1),(1,1,0),(0,1,0),(1,2,0),(0,2,0),(0,0,0),(1,0,0),(1,1,1),(0,1,1)}
M_V = {(1,0,0),(0,1,2)}
U_V = {(1,2,1),(0,2,1),(1,0,1),(1,1,0),(0,1,0),(1,2,0),(0,2,0),(0,0,0),(1,1,2),(1,2,2),(0,0,2),(0,1,2),(0,2,2),(1,0,2),(0,0,1),(1,1,1),(0,1,1)}
U_S = {(1,2,1),(1,1,0),(0,1,0),(0,2,0),(0,0,2),(0,2,2),(0,0,1),(1,1,1)}
D_S = {(1,0,1),(0,2,0),(1,1,2),(1,2,2),(0,0,2),(0,2,2)}
A_V = {(0,1,2,'y'),(1,0,0,'r'),(0,1,0,'c'),(0,1,0,'q'),(0,2,0,'q'),(0,0,0,'c'),(1,0,1,'c'),(1,2,2,'y'),(1,2,0,'c'),(1,0,0,'y'),(0,2,0,'c'),(1,2,0,'m'),(1,0,0,'c'),(1,1,1,'y'),(1,0,0,'m'),(0,0,1,'c'),(0,0,2,'y'),(1,2,1,'y')}
ORDER = "00040708180>0?1<0;0@1:0A0E0D090B0G0O0F0:0R0H0<0L0J0M0I0K0=0N1;271514;50C170P;61=0Q1S1N0S1@240U0T0W0V1R050103028@1V103229131K16121T5T2B331U1A8A2:36281C5U8D1B371J601P111W3:1H341L1I1O268B1M20382;218E252D3;23193I2I8F395V8C1>8H2G8G2H;<;;2W1?3=61;>8I2?3>352>8K2<3?2@8L312A3@2=623<8M5W3A8J8N2J3B8O64633C8P3D8Q3E8R2C3F8S658T3G063H66678V8U3K8W9068693J916:2K6;3L;:926<2L6=2M303M6>;=932O3N6?2R3O6@942N3P953Q3T962U3U3R979;6A3V986C9<3W9:2P2T2Q41409?2S426B9=3S;49@4@;?;B99;C;@;7441D9>22451F;A;86D4643;99A479B1G6E489C6F496G4:9D4;9E4<9F4=6I9G6H9H6J6L6M9I4>6N9J4C6Q9K6R6O9L6S4?9N4D6P4E6T6U4F9M9O4G6K4H6V4L4A9P6W4M9Q704K4N9R719S724I9V734J4P744O4B77572V754Q9T1E9W9U764S2E:0784T:1:3:24U794R:44V2F4W:61Q7:50:7:5517;52:853:9547<::7=:;7@7A55:<565:5;:=58:>7B59:?:A;D7>;E:@7C:C:B5<7D7?7E5=:D7F7G5>:E7H5?7I:F5@7J5A7K;F:G5B:H5C:I5D5H:J7L5I:K7M:P5E:Q5F<T5J:L5K5G:R7N:M5L7P:S5N5M:N5P7O;G:O7Q5O:T;M;N7R;J5Q5S;H7S;O7T;P7U;Q7V;R:V7W:U;S;K5R;T;U;084<U<L<>85<N;V80<V:W<?86;W81<W<O8387;1;3<6<D<@<2<882<<8:<:<H;2<F<B<7<0<3<J<M<4<A<E=0<=88<G8;<I<C<9<;<1<K8=8?<5;I<P;L<Q89<R<S=1=7=38<=2=8=9=:=;=4=<=>=?===58>=6BM=@BNBOBPBQ=ABR=B=CBS=D=E=F=GBTBU=H=I=JC0BV?TBWC1?VC2=K?UC3?W@0C4=L@1C5=MC6@2=NC7=OC8=P=SC;=QC9=R@3@4C:C<@7@5=T=U@8@6@9C=@:@;>0C>@<@=C?@>=VC@>1CBCA@?CC@BCDCFCE=W@@CG>2CH@A@C>3CI>4CJ>5CK@D>6>7CM@ECN>8@F>9@G>:@H>;CO@L@M@I><>>@N@JCPCL@OCQ>=CR>?@KCS@QCTCU@PCVD0>@CW@RD1>A@T>B@U>C>D@VD2>E@S>F@W>J>GD3A0>KD4A1>ID5>NA2D6A3>HD9A4D7A7D:D8A5D;>OD>A6A8>P>LD?D<>MD@D=>Q>RA9>S>TDAA:>UDBA;>VDC>WA<?0A=?1A@DD?2?4DEA>DFAA?3DGAB?5AEACAFDHA??6AGDIADDJ?7?8DLAHDK?9AIDM?:DN?;AJ?<AK?=?AAL?BAM?>?CAN?EAO?D?FDOAP??AQDPAR?@DQATAU?HDRASDS?GDTDUE3DVE4DW?IAVE7E0E8?JE1?NAW?M?L?OE2E5B0E6E9?KB1E;B2B3?PB4?RB:?Q?SB5B;B6B<B>E=B7B=B?B8E<E@EAB9EBE?BAE>B@ECEFE:EEEDBCBBBEBHBFBGBDBLBIBKBJ"
PICK = "110110101111001110010110000110011011010100110001111010111111001001100101011000100011101101010011010000000010010000111001111110001000101110000111000100011011111000001000000100000101111101111001000000000000000011101000010110000111001011111110000101001010000000100100100010000101010"
ORDER = "000407081M090?0R0@0:0S0A0;0D0F0B0G1;0>0<1<0=0I0E0K0H0C0O;5170L0P0M1@1S0Q1A1Q0T0U0J0N0V1N1?2@1:05010302312032185N151613121935145O8A1B3336345R1E8B39118C1G5P5S1C8E230W1=5V1024255Q1J1R1H1D3:1I37261K1F1P1L1O5T271T388F28295W5U3<3=222;3>612<1U2:623?2=2>1W8I3@632B3A641>3B8G8J66653C672A3D688H2G692T6:3E2?2S6;2U8D;9;>063J;?;:3K6<;;8L6?8M8N3L21603;8O6=3M6@8P3F8Q6>6A8R3N3G8K6B2C8S;=3H6C2D3O;<6E6I3P;@6F3R3V8T6J3S8W3W6K6M6L426N6D3Q40438U2E3I6G2F906H413U446P916O6Q924A3T93;3958V45966R94466S99;498472H6T9:482I6U9;492K6V4:2M714;6W979<4<2P4?4=702O2J732L9=4>4@4D749@2Q752N9>4E76724F4B9A;69?4G779B4H9C4I789D4J799E4M4N4C557>9F4O9G7?4P4Q7B9H7C7@9I7:9L9M9J4K9K4L4R7;7D7<;74S;84T1V4U;A7A4V;B9N4W2V502W9O537E30547F7=569P7G57519Q9R7H9S52;D7I9T589W:0:12R:2:47J9U:37K599V7L7M7O5::57P5;:75<7N5=7Q:85>5C5?:9::7R5@5D5A;E5E7S5B:;;F5F:<;M:=;L:>;O7T;G;N;P;I:6:?;Q;J5G:A;R:B7U:@;S5H:C5J7V<M7W<N80;H8186;T82;K;C:D5I83:E85<A875M:F8488:G<;8;<K<9<S:H<B;W:I<55K:J<E<0<C89:K:P8<<U<<<F<1<T5L8>8@;U<?<L<3:L;V8:<@<D<4:Q:M<V<6:R:N8=<7<I<G<=<W:O=2:S8?<8<2<J:U<H:T<><:<O<P:W<Q<R:V=0=1;0;2=3=6=4=5=7;1=8=:=;=9=<=>===?=A@5=@=B@6@7@9=C@:=D@8@;=E=F=G@=@<=H=K=I@>@@=J=L@?BQ@ABRBS@BBU=NBV@C=M@DBW@E@FC1@GC0@H@J@KC2=O@I@LC4=PC5BTC3=Q=RC6@M=SC7=V=TC8=W@NC9=U>0C:>1>2@OC=C;@P>3@RC>@S@VC<>6@T@WC?>4A2>5A0>7A3>9@QA1>:C@>;@U><A5CAA6>8>=A4CB>>CC>?CECI>@CFCDCJ>AA7CH>CA8CK>BA9>E>DA:CMCGA;A<CLA=A?>FA>A@AACPCN>G>HCQCO>ICR>JABCS>KCT>M>PACCU>N>QCVADCWD1AE>LAFAJ>OD0AI>RAGAKD3AL>S>TAMAND2>UAH>WAO>V?0D4?1APAQ?2D5AR?3D6?4D7?5D9D<?6ASD8D=?7AT?9D;AU?:D>?8AVD:?;AWD@D?B0B2B3?<B1DCB4DA?=?>DDDB??DE?@DFB5?ADG?BDHB6?CB7?DDIB8?HB9DJ?EB:B??GDL?IDKB@DM?J?F?KB;?LDNDOB<?P?SB>BADPB=BGDQ?TBB?MBC?NDRBD@3BH@4?O@2BE@1DSDTDUBOBNBMBPDVE3DWBF?QE0E6E1BIBKBJE4BLE5?RE7E2E:?V?W@0?UE8E9E<E;E@E>EAE?E=ECEEEBED"
PICK = "001001100100001011101101010111111100111000100001111011011100010011001101011011110011101000001011001000101001110111111101010000001000111111011110111111010000011000000000001001000101110001101011100100000000000000011000011101010011011000111100001000101110000110000010000001010000000111000101111111000000111110001110110011110011000001000000110000000000000001011101000100000000000101000001000110010001110010110110101101010111"
ORDER = "00040708180@0A0M0=0B090C0N0>0F0D1L160:1;1N0H0;0G150?0J1<1G1:0<210K1=1M1R0O0L1I1A131H0I0P1219140Q1>:U1J1?0T110501030S0W022L0R1B1025731D;22M2:0U2F4T1P741C2N1775772P781E4U7:1@502Q7;0E2R0V1U1S2S4V791O2U2T932V:V54512W1W30527<762O53234W317=3:1F26327>271V55;81T7?9633;97@342G7A;3357B56:W3657;020;137582224591K7C5:39385=5;067E3<3>7D3=5<3;5?3?7F3@7G3A7H3B5@7I7M3C7K7O3D5A3G7P5B7L3I3H5C3V3E3J5I3F3K7T5J7U5N7V7Q7R5O7S5E5>3L5F7J285P5K3M7W293N7N5L5G3O;4803P;73Q2I3R2;5D813S5M2J822K833U3T5H845Q41855R3W865S405T42875U888:2<4344455V2@898;5W46602=4749618<482>8=4;2D4<4I6263944=648>4>8C668D658E8F8H;:8G4?8?4:8@8I8B4@8A674A8J8K4B4C688L4D4E2B95698M2C4F6:8N6;2A8O6<4G8P4H6=2?8Q4L4J8R6>2H4K6?;;8S;66A:T8U4M8T;56B4N1Q6@6C4O6D2E8V6E4P6F8W4Q6G4R904S6I916H98929=99:=:B:>9:979;<H;<9>6J9?:C9<6K9@:?6L9A;=6M9B;@6N:A9C;?6O;>9E6P:@9F9D6Q9G;A:D6R9K;B9H<O6T9I<SBQ:E9J:J6U:F:G9N9L:K;C<J6V;F;D:H;E6W9M6S70:I;G:L71;H:M72<C;I:N9O:P?S;J9P:O9T<T9Q9U<39R:Q:SBR<U9V;O;M<5;Q<I9W;U9S;W:R:0<?<A:1<;:2<1<6<9;V:4;S<4:3;P:5<:;N<B:6<@<7;R:7:9;T<=<<;K<K<>:8<2<0<8<V;L<L<D<W:::<BS<E=1<F=0=2<G?T=3=4?U:;<M=5=6<N=7<P=8BW<Q=9BT=:=;C0<R=<C1BU===>=?BVC2C3C4=@C5C6=A@1C7C8@2=B=EC9=C@3=G=D?V=FC:=H?WC==I@0C;C>=J@4@5=K@6=LC<@7C?@8=N@9C@=M=O@:CA@;CBCD@<=PCCCECFCH@==QCI@@=RCGCMCNCJCOCK@>CL=S@A@?=TCP=UCQ@BCR=V@C=W@DCS>0@F@J@HCT>1@G@KCVCU@E>3>2@LCW>4>5@MD0D1>7D2@ND3>6D5@OD4D6@PD:@I@S@QD8>8D9>9@TD7@R>:@UD;@V>;@W><A0D<>>>AA1D=>BA2A4D>>=D?>C>@A3DB>?DCA6>FDD>GDH>H>DDE>EDFA5D@A7DADG>I>JA8DI>KA9DL>LDJA:>MA?A<>NA=A@DM>ODK>PAADN>QDOA;DPABA>>RDQ>T>UDRADDSACDTDVAEDUDWAHE2AF>VE0>S>WE1AIAJE3?0AK?1E4ALAM?2AN?3E5AO?4AP?5E6AQE7?9ARAG?6E8?<?8E9?:ASE>AVE?E:?;?7?E?F?GE@?H?=E;AWATE<E=???I?@AUB0EA?J?AB1EB?BB2?>B3?CEC?R?OB4?QB9?PEK?DEEB:B5?KB;?M?L?NELB>B6EMB?B8ENB@EDB<EFB=B7EGEOEHBDETEVEUEWEIBABEEJBFBGESBBEREQBHEPBCBPBOBMBNBIBKBJBL"
PICK = "111000100110001101001001110111100000111001100101111000100100110111001100001011010011001001001111000101100101110111111101010000111100111011110111101111010000011000000000000011100000110001101011100100000000000010001000110001111011110000111110001001101110010110000010000001000000000000011100101110100000010010001101100010111010000110110000010100000100000101010001100111010001110000101101100010000111000011111001111011110111"
ORDER = "00040708090=0A0M0B0N0@0C1N0D16180O0H0G0F0J151;1<1I1O2:1:;P0E0:0K131>0L191=0>1S0I141V1?1W121R1J20212F23050?01030;0P021M7A0<0Q;T2J1L2L7B1B0R1A1F7E110W2M551T0U7F2N0S2R100T7I2P561C1H592Q7G1D2S1@0V2O7J227K172T2U7H2V7D5:311E2W5;7L1U58301P26321G7M7C;I33577N345=7O355<9H7P36245>3=382737;Q5?7Q392G5@7R;O3;5A1K7S3:;U5B7T;V5C5D3<063@7V5E3A7U8:3?9K5F5G;H3B5I7W3C5U803D3E815J3F843G825K853L3K863M885L3N898=8;3O8>8<9I5O8?5M3P5P833>5S3Q448A255T3R8B87283S5H3T5V3H8C3U3I3V3W5W8D3J8E408@4241608F29478G8H5N438I8K61458J5Q488M2H9J63;F2;628N49;S;G4:64;R1Q8L5R654;2<46668O2=2@4<67;L4=912A688P4>;M698Q4A4B2B6:4Q6;4C;N8R4D2D8W6<906>;J929493958S964E6=6?4?2?974F6@2C984G8T4H6B4@4I8V8U994J2I6A4L9:4K9;2K4M9<4O4N9>9=4P4T4R6N2>4S9?6C9@;K4U4V9B<09A6D4W506E6F9C6G2E6L9D516M9E526Q9F539G6R54;49M6O9L9S6S6H9N6P9O6K9T<19P9U:V6I9Q:W<26J6T<8<36U<7<;;0<9;5<:9R;19V<4;29W:06V:4<<6W<5:5<===70:671;3<672:7=873:874:175:9<?7679;677:;:=7::2<>78<@;77;:3;8;<<V;9::<P<F=0;:<T<H;=<D<R=I=?=67<<B=><J;><A7=<Q;;<W;?:<7><G;@7?<I7@=2=1;B;A:>:?:D<E:@<S<C:E:A=H=@<U;E=7:FCS<K:B;C:C=4=3:G<N;D=5<L:H<O=D<M:I=J=9:J=A=:CT:K=;CR@Q:M=<:L=B:N:O;W:P=C:R=K:Q=N=L:S:U=O=M=E=PD0=F=Q=G:T=RCU=S@R=T@S=U=VCV=W>0>1CW>2D1>3D3>5D2@W@TD4>6>4D5>BD6D7>7D8D9D:>8D;>9D<D=>:><>>D>>;@UD?>?>=A0DA@VD@>@A1A3DM>AA4A5DBA2A6>EA7DC>CA8DD>FA9DG>DDEA:A;DHDFDIA<>GA>DKA=A?>HA@DL>IDJDNDPDODQALDR>JAA>KDS>LABDT>MACDU>NADAF>P>ODVAGAEAJDWE0AI>QAHAK>SE1>RE2AM>T>UE3E4E5AN?0E8E6?1>VE7E9E:AO>WAPE<?=AQASE;?2E=AT?3EHAUE>ARAV?4AWE?E@B0EAB1?5EFB2?6B3EBEG?7B4EEB6EI?:B5?8EKB8EJEL?;EMBCEO?<EP?@EQB9ECERED?AESB:B7ET?>B;EUB<EVEW??EN?9B=F0F2BAF1B@B>?CBBF4?BBDBFBEBG?DBHBI?EF5F3?FB?BJ?GF6BK?HF7?IBLF8?J?KF9BNBM?LF:F;BO?MBPF<?PF@?NBQF=FABRBSF?BTBV?Q?OBUFC?RBWFB?SC2FM?TFNC0FOF>C1?UFP?VFDC3?WFE@0FGC4@7FQ@1@2C5FHC6C7@3@8FWG1FVG0@4FIC8C>@9@:C9@6@;C:@<C?CAFJC;C@CBFKC<@5@C@D@EC=FL@F@GCCFTFS@=FUCDFF@HFR@>@?@@@O@PCG@M@N@ACE@BCHCF@I@L@J@KCICKCJCLCMCOCQCNCP"
_R2 = [(r, c) for r in range(2) for c in range(NC)]
_R3 = [k + (s,) for k in _R2 for s in range(S)]
OPTS = ([("Z_V", k + (h,)) for k in _R3 for h in range(2)] + [(n, k + (h,)) for n in ("L_V", "L_M") for k in _R2 for h in range(2)]
        + [(n, k) for n in ("M_V", "U_V", "U_S", "D_S") for k in _R3] + [("A_V", k + (x,)) for k in _R3 for x in "yc"]
        + [("A_V", k + (0, x)) for k in _R2 for x in "mr"] + [("A_V", (0, c, 0, "q")) for c in range(NC)]
        + [("A_V", (1, c, 0, "b")) for c in range(NC)] + [("A_V", k + (h, "e")) for k in _R2 for h in range(2)]
        + [("A_V", k + ("a",)) for k in _R3 if k[2] < 2] + [("A_V", ("k", i)) for i in range(1, 70)])
OPTS = (sorted(OPTS, key=repr) + [("G_K", (n, j)) for n, k in (("lk", 8), ("lp", 8), ("ln", 1), ("q", 3)) for j in range(k)]
        + [("K_T", k + (x,)) for k in _R3 for x in (1, 2)] + [("G_N", k + (x, n)) for k in _R3 for x in "md" for n in (2, 4)]
        + [("G_K", ("d", n)) for n in "ident nident i97 n97 ik i8k f75".split()]
        + [("G_K", ("f", n)) for n in "padb padf c0 two m0 m1".split()])
SETS = {n: set() for n, _ in OPTS}
for _c, (_n, _k) in zip(PICK, OPTS):
    if _c == "1":
        SETS[_n].add(_k)
Z_V, L_V, L_M, M_V, U_V, U_S, D_S, A_V, G_K, K_T, G_N = [SETS[n] for n in "Z_V L_V L_M M_V U_V U_S D_S A_V G_K K_T G_N".split()]
COLS = {}


RANK = [0]


def half(h):
    return h ^ 1 ^ (RANK[0] // 4)


def lanes(T, topo, rank, h):
    core, out = T.cores[rank], {}
    dst = [s for s in range(4 * h, 4 * h + 4) if s != rank]
    far = [s for s in dst if topo.chip(T.cores[s]) != topo.chip(core)]
    for k, s in enumerate(far):
        en = topo.engines(core, T.cores[s])
        out[s] = en[k::len(far)]
    for s in dst:
        if s not in far:
            out[s] = topo.engines(core, T.cores[s])[-4:]
    return out


def single(T, topo, rank):
    out = {}
    for d in range(1, 8):
        s = (rank + d) % 8
        en = [x for x in topo.engines(T.cores[rank], T.cores[s]) if x not in out.values()]
        out[s] = en[-1] if topo.chip(T.cores[s]) == topo.chip(T.cores[rank]) else en[0]
    return out


def graph():
    ops, acc, cur = [], {}, [""]

    def add(q, dur, fn, R, Wr, sem=None, inc=1, lat=0.0, deps=(), pr=0.0, cont=None):
        i = len(ops)
        d, soft = set(deps), set([cont] if cont is not None else [])
        for lst, isw in ((R, False), (Wr, True)):
            for x in lst:
                b, lo, hi = x[:3]
                for (k, kq, klo, khi, kw) in acc.get(b, []):
                    if lo < khi and klo < hi and (isw or kw):
                        (soft if SOFT and isw and kq == q and sem is None and ops[k]["sem"] is None else d).add(k)
                    elif b in BANKS and kq != q:
                        d.add(k)
        for lst, isw in ((R, False), (Wr, True)):
            for x in lst:
                b, lo, hi = x[:3]
                old = acc.setdefault(b, [])
                if b in BANKS and old and old[-1][1] != q:
                    k = len(old)
                    while k and old[k - 1][1] == old[-1][1]:
                        k -= 1
                    del old[:k]
                if isw and b not in BANKS:
                    old[:] = [y for y in old if y[0] == i or not (lo <= y[2] and y[3] <= hi)]
                old.append((i, q, lo, hi, isw))
        d.discard(cont)
        ops.append({"q": q, "dur": dur, "fn": fn, "deps": d | soft, "sem": sem, "inc": inc, "lat": lat, "pr": pr, "tag": cur[0],
                    "soft": soft - d})
        return i

    def ap(T, x):
        return x[3](T) if len(x) > 3 else T[x[0]][:, x[1]:x[2]]

    def wd(x):
        return x[4] if len(x) > 3 else x[2] - x[1]

    def two(*xs):
        return all(SCRATCH[x[0]][2] in ("bfloat16", "uint16") for x in xs)

    def vdur(n, k=1.0):
        return max(64.0, n * k) * VC + OV

    def insb(x):
        return x[0] not in BANKS

    def tt(out, a, b, op, ind=None):
        n = wd(out)
        if ind is None:
            f = lambda g, T, e: g.vector.tensor_tensor(ap(T, out), ap(T, a), ap(T, b), op)
            return add("V", vdur(n, 2.0 if insb(a) and insb(b) else 1.0), f, [a, b], [out])
        f = lambda g, T, e: g.vector.tensor_tensor(ap(T, out), ap(T, a).indirect(ap(T, ind)), ap(T, b), op)
        return add("V", 50 + n * VG * VC, f, [a, b, ind], [out])

    def ts(out, a, s1, op0, s2=None, op1=None):
        R = [a] + [s for s in (s1, s2) if isinstance(s, tuple)]

        def f(g, T, e):
            v1 = ap(T, s1) if isinstance(s1, tuple) else s1
            v2 = ap(T, s2) if isinstance(s2, tuple) else s2
            if op1 is None:
                return g.vector.tensor_scalar(ap(T, out), ap(T, a), v1, None, op0)
            return g.vector.tensor_scalar(ap(T, out), ap(T, a), v1, v2, op0, op1)
        return add("V", vdur(wd(out), 0.5 if two(out, a) else 1.0), f, R, [out])

    def cp(out, a):
        return add("V", vdur(wd(out), 0.5 if two(out, a) else 1.0),
                   lambda g, T, e: g.vector.tensor_copy(ap(T, out), ap(T, a)), [a], [out])

    def scat(win, ind, src):
        return add("V", 50 + wd(src) * 3 * VC,
                   lambda g, T, e: g.vector.tensor_copy(ap(T, win).indirect(ap(T, ind)), ap(T, src)), [src, ind], [win])

    def ms(out, v):
        return add("V", vdur(wd(out), 0.5 if two(out) else 1.0), lambda g, T, e: g.vector.memset(ap(T, out), v), [], [out])

    def sa(out, a, func, scale=1.0, bias=0.0, ind=None, more=0.0):
        n = wd(out)
        R = [a] + ([ind] if ind else []) + [x for x in (bias, scale) if isinstance(x, tuple)]

        def f(g, T, e):
            src = ap(T, a).indirect(ap(T, ind)) if ind else ap(T, a)
            sc = ap(T, scale) if isinstance(scale, tuple) else scale
            if func is F.Copy:
                return g.scalar.activation(ap(T, out), src, func, scale=sc)
            return g.scalar.activation(ap(T, out), src, func, bias=ap(T, bias) if isinstance(bias, tuple) else bias, scale=sc)
        return add("S", more + ((65 + n * VGS * VC) if ind else (max(64.0, n) * VC + OS)), f, R, [out])

    def un(out, a, scale, bias, key):
        if key in A_V:
            return ts(out, a, scale, A.mult, bias, A.add)
        return sa(out, a, F.Identity, scale=scale, bias=bias)

    def pe(calls, R, Wr, cont=None, more=60):
        def f(g, T, e):
            r = None
            for cy, o, l, x, st, sp in calls:
                r = g.tensor.matmul(o(T), l(T), x(T), st, sp)
            return r
        return add("T", sum(k[0] for k in calls) * PC + more, f, R, Wr, cont=cont)

    def pes(calls, R, Wr, most=520):
        k, part = None, []
        for i, x in enumerate(calls):
            part.append(x)
            if i == len(calls) - 1 or sum(y[0] for y in part) + calls[i + 1][0] > most:
                k, part = pe(part, R, Wr, k, 60 if i == len(calls) - 1 else 10), []

    def gather(f, key, out, ind, *ins):
        n = 4 if key + (4,) in G_N else 2 if key + (2,) in G_N else 1
        cut = lambda x, k, w: (x[0], x[1] + k * w // n, x[1] + (k + 1) * w // n)
        for k in range(n):
            f(cut(out, k, CH), cut(ind, k, NN), *[cut(x, k, CH) for x in ins])

    def at(x):
        return lambda T: ap(T, x)

    def sl(name, lo, hi, step):
        return lambda T: T[name][:, lo:hi:step]

    def mm(out, *pairs):
        n = max(wd(out), 64)
        return pe([(n, at(out), at(l), at(x), k == 0, k == len(pairs) - 1) for k, (l, x) in enumerate(pairs)],
                  [p[0] for p in pairs] + [p[1] for p in pairs], [out])

    def feats(bank, base, w, src, first, last, tiles=range(8), step=8):
        nf = wd(w) // 8
        calls = []
        for jl in tiles:
            if len(src) == 2:
                l = at(qv(src[0], src[1], None, jl))
            else:
                l = sl(src[0], src[1] + jl, src[2], 8) if step == 8 else sl(src[0], src[1] + 128 * jl, src[1] + 128 * jl + 128, 1)
            calls.append((64, sl(bank, base + jl, base + 64 * nf, 8), l, at(w), first and jl == tiles[0], last and jl == tiles[-1]))
        return calls

    def pad(n):
        b, k = PADS[n]
        return (b, 8 * k, 8 * k + 144, lambda T: T[b][:, k + 1:k + 17:2, :], 64)

    def win(n, a):
        b, k = PADS[n]
        return lambda T: T[b][:, k + a:k + a + 16, :]

    def top(x):
        return x[:3] + (lambda T: T[x[0]][0:64, x[1]:x[2]], x[2] - x[1])

    def turn(out, *srcs, cut=False):
        n = wd(out)
        calls = []
        for src, idn in srcs:
            cy = 256 if idn == "identf" else 64
            calls.append([cy, at(out), win(src, 0), sl(idn, 1, 2 * n, 2), False, False])
            calls.append([cy, at(out), win(src, 1), sl(idn, 0, 2 * n, 2), False, False])
        calls[0][4] = True
        calls[-1][5] = True
        if cut:
            k = pe(calls[:-2], [pad(s) for s, _ in srcs[:-1]] + [full(i) for _, i in srcs], [out], None, 10)
            return pe(calls[-2:], [pad(srcs[-1][0]), full(srcs[-1][1])], [out], k)
        return pe(calls, [pad(s) for s, _ in srcs] + [full(i) for _, i in srcs], [out])

    nk = [0]

    def sc(out, a, x, y=1.0):
        nk[0] += 1
        if ("k", nk[0]) in A_V or y != 1.0:
            return ts(out, a, x, A.mult, y, A.mult)
        return sa(out, a, F.Copy, scale=x)

    def gi(out, pattern, base, cm, flag):
        def f(g, T, e):
            if flag:
                return g.iota(ap(T, out), pattern, base, cm, allow_small_or_imprecise_dtypes=True)
            return g.iota(ap(T, out), pattern, base, cm)
        return add("G", 130 + wd(out) * 2 * VC, f, [], [out])

    def gs(out, a, pattern, op, base, cm, other=0.0):
        return add("G", 170 + 2 * VC * wd(out),
                   lambda g, T, e: g.affine_select(ap(T, out), ap(T, a), pattern, op, other, base, cm), [a], [out])

    def full(n):
        return (n, 0, SCRATCH[n][1][1])

    def c_(n, c, lo=0, hi=None):
        w = SCRATCH[n][1][1] // NC
        return (n, c * w + lo, c * w + (w if hi is None else hi))

    def col(n):
        k = COLS.setdefault(n, len(COLS))
        return ("col", k, k + 1)

    def qv(rd, c, h=None, jl=None):
        n = "qb" if rd else "qa"
        if jl is not None:
            return (n, c * CH, c * CH + CH, sl(n, c * CH + jl, c * CH + CH, 8), 128)
        return c_(n, c) if h is None else c_(n, c, 512 * h, 512 * h + 512)

    k = add("Y", 60, lambda g, T, e: g.sync.dma_start(T.qn[:, :, :], T.qs[:, :]), [], [("qn", 0, 3 * CH)], sem="lq", inc=16,
            lat=3500, pr=6e7)
    for c in range(NC):
        cur[0] = "0%d0" % c
        x = ("qn", 0, 3 * CH, lambda T, c=c: T.qn[:, :, 128 * c:128 * c + 128], CH)
        if ("q", c) in G_K:
            gs(c_("qa", c), x, [[0, CH]], A.is_ge, 0, 0)
        else:
            un(c_("qa", c), x, 1.0, 0.0, (0, c, 0, "q"))
    cur[0] = ""
    add("S", 60, lambda g, T, e: g.scalar.dma_start(T.wts[:, :], T.wt[:, :]), [], [full("wts")], sem="lw", inc=16, lat=2000, pr=5e7)
    lm = add("Y", 60, lambda g, T, e: g.sync.dma_start(T.mk0[:, 0:W], T.mk[:, :]), [], [("mk0", 0, W)], sem="lm0", inc=16,
             lat=8000, pr=5e6, cont=k)
    add("Y", 60, lambda g, T, e: g.sync.dma_start(T.mk1[:, 0:W], T.mk[:, :]), [], [("mk1", 0, W)], sem="lm1", inc=16, lat=7000,
        deps=(lm,))

    cur[0] = "c"
    idn = ("idw", 2, 130)
    icol = col("i")
    eq, ge, lt = [lambda k, a=a: ("cmp", a + k, a + k + 1) for a in (0, 16, 32)]
    m12 = lt(12)

    def diag(n, v):
        if ("d", n) in G_K:
            nk[0] += 1
            return gs(full(n), full("zero"), [[-1, 128]], A.not_equal, 0, 1, v)
        return sc(full(n), idn, v)

    def fill(key, out, v):
        if ("f", key) in G_K:
            return gs(out, ("ones", 0, wd(out)), [[0, wd(out)]], A.is_gt, 0, 0, v)
        return ms(out, v)

    def oh(lo, hi, step=1):
        return ("ohw", 8 * lo, 8 * hi, lambda T: T.ohw[:, lo:hi:step, :], 8 * len(range(lo, hi, step)))
    gi(full("ip"), [[0, 1]], 0, 1, False)
    ms(full("ones"), 1.0)
    ms(full("zero"), 0.0)
    gs(oh(0, 16), ("ones", 0, 128), [[-1, 16], [-16, 8]], A.is_equal, 0, 1)
    gs(full("z8a"), ("ones", 0, 8), [[-16, 8]], A.is_ge, 0, 1)
    gs(full("z8"), full("z8a"), [[16, 8]], A.is_ge, 15, -1)
    gs(full("idw"), full("ones"), [[1, 132]], A.is_equal, -2, -1)
    gs(full("bda"), ("ones", 0, 128), [[-16, 8], [0, 16]], A.is_ge, 0, 1)
    gs(full("bd"), full("bda"), [[16, 8], [0, 16]], A.is_ge, 15, -1)
    gi(full("mrow"), [[0, 4], [1, 16]], 0, 0, True)
    ts(("i16", 0, 1), full("ip"), 15, A.bitwise_and)
    cp(icol, ("i16", 0, 1))
    ts(col("i11"), icol, 11.0, A.min)
    sa(("e3", 0, 1), col("i11"), F.Exp, scale=17 * LN2, bias=-100 * LN2, more=1300.0)
    sa(("e3", 1, 2), col("i11"), F.Exp, scale=-17 * LN2, bias=64 * LN2)
    for k, op in enumerate((A.is_equal, A.is_le, A.is_gt)):
        ts(("cmp", 16 * k, 16 * k + 16), ("mrow", 0, 16), icol, op)
    z8 = full("z8")
    tt(oh(15, 17), oh(12, 14), oh(13, 15), A.subtract)
    ts(col("k0"), ge(1), m12, A.mult, -255.0 * 2.0 ** -48, A.mult)
    sc(col("k1"), ("e3", 0, 1), col("k0"))
    sc(full("dk1"), idn, col("k1"))
    if any(("lk", jl) not in G_K for jl in range(8)):
        ts(("i16", 2, 3), full("ip"), 7, A.bitwise_and)
        cp(col("i8"), ("i16", 2, 3))
        ts(("selm", 8, 16), ("mrow", 0, 8), col("i8"), A.is_equal)
    pe([(128, at(top(("pe", 0, 128))), sl("bd", 0, 128, 2), at(full("dk1")), True, True)], [full("bd"), full("dk1")], [("pe", 0, 128)])
    sc(top(full("dk2")), top(("pe", 0, 128)), 1.0)
    for jl in range(8):
        if ("lk", jl) in G_K:
            gs(top(("lk", 128 * jl, 128 * jl + 128)), top(full("dk2")), [[-8, 8], [0, 16]], A.is_equal, -jl, 1)
            nk[0] += 1
        else:
            sc(top(("lk", 128 * jl, 128 * jl + 128)), top(full("dk2")), top(("selm", 8 + jl, 9 + jl)))
    diag("ident", 1.0)
    sc(col("s12"), m12, 2.0 ** -68)
    sc(full("i68"), idn, col("s12"))
    ts(col("zb"), eq(12), eq(13), A.add, 2.0 ** -68, A.mult)
    for b in ("padb", "padf"):
        n = SCRATCH[b][1][1]
        x = (b, 0, 8 * n, lambda T, b=b: T[b][:, 0::2, :], 4 * n)
        if ("f", b) in G_K:
            gi(x, [[0, 4 * n]], 0, 0, True)
        else:
            ms(x, 0.0)
    fill("c0", ("cc", 192, 320), 2.0 ** 29)
    if M_V:
        ts(full("thv"), ("mrow", 0, 16), icol, A.is_gt, col("s12"), A.mult)
    sc(("wtf", 0, 2), full("wts"), 2.0)
    ts(col("ca"), eq(12), -4096.0, A.mult, eq(13), A.add)
    ts(col("cb"), eq(12), -8192.0, A.mult, eq(13), A.add)
    ts(("wtf", 2, 4), ("wtf", 0, 2), col("ca"), A.add, 2.0 ** 67, A.mult)
    ts(("wtf", 4, 5), ("wtf", 1, 2), col("cb"), A.add, 2.0 ** 67, A.mult)
    sc(("wtf", 6, 8), ("wtf", 0, 2), -2.0 ** 67)
    for k in range(3):
        sc(("wu1", 8 * k, 8 * k + 8), z8, ("wtf", 2 + k, 3 + k))
    for k in range(2):
        sc(("wu2", 8 * k, 8 * k + 8), z8, ("wtf", 6 + k, 7 + k))
    if U_V or U_S:
        sc(("wu3", 0, 16), full("wu2"), -1.0)
        sc(("wu3", 16, 24), ("wu1", 16, 24), 1.0)
    if K_T:
        diag("i8k", 8192.0)
    if M_V:
        fill("two", full("two"), 0.0625)
    if M_V:
        sc(("cc", 0, 128), ("ones", 0, 128), col("ca"))
        sc(("cc", 128, 192), ("ones", 0, 64), col("cb"))
    if U_S:
        sc(("wu1", 24, 40), ("wu3", 0, 16), 1.0)
    diag("i97", 97.0)
    diag("n97", -97.0)
    sc(full("identf"), idn, 1.0)
    diag("ik", 2.0 ** -66)
    fill("m0", ("mk0", W, W + 16), 2.0 ** 20)
    fill("m1", ("mk1", W, W + 16), 2.0 ** 20)
    sc(("wd0", 8, 24), oh(12, 14), 1.0)
    sc(col("we"), ("e3", 1, 2), m12)
    sc(("wd0", 0, 8), z8, col("we"))
    diag("nident", -1.0)
    if D_S:
        sc(("wg", 64, 112), oh(1, 12, 2), col("we"), 4.0)
        sc(("wg", 128, 176), oh(0, 12, 2), col("we"))
        tt(("wg", 0, 48), ("wg", 64, 112), ("wg", 128, 176), A.add)
        sc(("wg", 48, 64), oh(12, 14), 1.0)
        sc(("wg", 64, 112), ("wg", 0, 48), -1.0)
        sc(("wg", 112, 128), oh(13, 15), -1.0)
        sc(("wg", 128, 176), ("wg", 0, 48), -1.0)
        sc(("wg", 176, 184), z8, 0.0)

    def learn_constants():
        sa(col("th"), col("i11"), F.Relu, bias=-3.0)
        sa(("e3", 2, 3), col("th"), F.Exp, scale=21 * LN2, bias=-102 * LN2)
        sc(col("k3"), ("e3", 2, 3), m12)
        sc(full("dk3"), idn, col("k3"))
        ts(("selm", 0, 8), ("mrow", 0, 8), 8.0, A.add, icol, A.is_equal)
        mm(("pe", 128, 256), (full("bd"), full("dk3")))
        sc(full("dk4"), ("pe", 128, 256), 1.0)
        for jl in range(8):
            if ("lp", jl) in G_K:
                gs(("lp", 128 * jl, 128 * jl + 128), full("dk4"), [[-16, 8], [0, 16]], A.is_equal, -8 - jl, 1)
                nk[0] += 1
            else:
                sc(("lp", 128 * jl, 128 * jl + 128), full("dk4"), ("selm", jl, jl + 1))
        if ("ln", 0) in G_K:
            sc(full("dk3"), ("pe", 128, 256), -1.0)
            for jl in range(8):
                gs(("ln", 128 * jl, 128 * jl + 128), full("dk3"), [[-16, 8], [0, 16]], A.is_equal, -8 - jl, 1)
        else:
            sc(full("ln"), full("lp"), -1.0)
        sc(full("i75"), full("i68"), 2.0 ** -7)
        sc(full("n75"), full("i68"), -2.0 ** -7)
        diag("f75", 2.0 ** -75)
        if L_M:
            ts(("mrow", 32, 48), ("mrow", 0, 16), 3.0, A.add, icol, A.is_gt)
            ts(("mrow", 48, 64), ("mrow", 0, 16), 0.0, A.is_gt, m12, A.mult)
            tt(full("th3"), ("mrow", 32, 48), ("mrow", 48, 64), A.mult)

    def edit_constants():
        gi(full("trow"), [[0, 2], [1, 128]], 0, 0, True)
        gi(full("t16a"), [[0, 2], [16, 8]], 0, 0, True)
        for k in range(4):
            gi(("iot", 2052 * k, 2052 * k + 2052), [[256, 2052]], 256 * 2052 * k, 0, True)
        sa(full("t16"), full("t16a"), F.Identity, bias=icol)
        sa(full("t16b"), full("t16"), F.Identity, bias=15.0)
        sa(full("dump16"), full("t16"), F.Identity, bias=8208.0)
        sc(full("isym"), idn, m12)
        sc(full("sh1"), ("idw", 3, 131), ge(13))
        sc(full("sh2"), ("idw", 4, 132), ge(14))
        gs(full("sel1"), ("ones", 0, 16), [[1, 16]], A.is_equal, -2, 0)
        gs(full("sel2"), ("ones", 0, 16), [[1, 16]], A.is_equal, -1, 0)
        sc(full("mt"), ("mrow", 0, 16), eq(12))
        sc(col("wcm"), lt(15), ge(12))
        sc(full("spa"), ("idw", 1, 129), col("wcm"))
        tt(full("spl"), full("spa"), full("isym"), A.add)

    def search(rd, c):
        q = qv(rd, c)
        mk = ("mk0" if rd == 0 else "mk1", 0, W + 16)
        pn, pw, fx, xf = "pn%d" % c, "pw%d" % c, "fx%d" % c, "xf%d" % c
        ss, key = ("vp", c * 128, c * 128 + 64), ("vp", c * 128 + 64, c * 128 + 128)
        hit, zz, dd = c_("hit", c), c_("zz", c), c_("dd", c)
        kb = pad("xk%d" % c)
        ra = "ra2" if rd else "ra"
        r = lambda k: c_(ra, c, 64 * k, 64 + 64 * k)
        n2, mp, tp, xm = c_("rb", c, 0, 64), "mp%d" % c, "tp%d" % c, c_("rb", c, 64, 128)
        m = pad(mp)
        cur[0] = "%d%d0" % (rd, c)
        if rd == 0:
            pe(feats(pn, 0, oh(12, 17), (rd, c), True, True), [q, oh(12, 17)], [(pn, 0, 320)])
        if (rd, c, 0) in M_V:
            un(m, r(0) if rd else (pn, 0, 64), 1.0, 0.0, (rd, c, 0, "m"))
            if rd == 0:
                un(c_("ra", c, 0, 320), (pn, 0, 320), 1.0, 0.0, (rd, c, 0, "r"))
        else:
            if rd == 0:
                un(r(0), (pn, 0, 64), 1.0, 0.0, (rd, c, 0, "m"))
                un(c_("ra", c, 64, 320), (pn, 64, 320), 1.0, 0.0, (rd, c, 0, "r"))
            m = r(0)
        for st in range(S):
            cur[0] = "%d%d%d" % (rd, c, st)
            byv, umv = (rd, c, st) in M_V, (rd, c, st) in U_V
            sa(pad(fx), m, F.Exp, scale=-17 * LN2, bias=80 * LN2)
            if byv:
                turn((pw, 448, 512), (mp, "ident"))
                cp(c_("ml", c), (pw, 448, 512))
                gather(lambda o, i, x: tt(o, full("thv"), x, A.mult, ind=i), (rd, c, st, "m"), zz, c_("ml", c), q)
            else:
                parts = [r(0)] if st == 0 else [r(1) if st == 1 else n2, xm]
                o = top((pn, 128, 256))
                pe([(128, at(o), at(x), at(full("ident")), k == 0, k == len(parts) - 1) for k, x in enumerate(parts)],
                   parts + [full("ident")], [o])
                sa(top(c_("fts", c)), o, F.Exp, scale=-17 * LN2, bias=80 * LN2)
                for h, bank in ((0, pw), (1, pn)):
                    k, both = None, ["q", "f"][::-1 if rd == 1 and st == 0 else 1]
                    for x in both:
                        calls = []
                        for jl in range(4 * h, 4 * h + 4):
                            o, a, z = (bank, 128 * (jl % 4), 128 * (jl % 4) + 128), k is None and jl % 4 == 0, k is not None and jl % 4 == 3
                            if x == "q":
                                calls.append((128, at(o), at(full("i68")), at(qv(rd, c, None, jl)), a, z))
                            else:
                                calls.append((128, at(o), at(top(("lk", 128 * jl, 128 * jl + 128))), at(top(c_("fts", c))), a, z))
                        k = pe(calls, [q, full("i68")] if x == "q" else [("lk", 512 * h, 512 * h + 512), c_("fts", c)],
                               [(bank, 0, 512)], k, 10 if k is None else 60)
                    if (rd, c, st, h) in Z_V:
                        ts(c_("zz", c, 512 * h, 512 * h + 512), (bank, 0, 512), col("zb"), A.add, 0.0, A.max)
                    else:
                        sa(c_("zz", c, 512 * h, 512 * h + 512), (bank, 0, 512), F.Relu, bias=col("zb"))
            kt = 2 if (rd, c, st, 2) in K_T else 1 if (rd, c, st, 1) in K_T else 0
            if (rd, c, st) in D_S:
                kt = min(kt, 1)
            ky = (pn, 64, 128)
            if not kt:
                un(ky, m, 8192.0, 0.0, (rd, c, st, "y"))
            ums = (rd, c, st) in U_S and not umv
            u, u12, ta = (pw, 0, 320 if ums else 192), (pw, 0, 128), (pw, 128, 192)
            wu = full("wu3") if umv else ("wu1", 0, 40 if ums else 24)
            big = lambda l: (128, at(u12), at(full(l)), at(("cc", 192, 320)), False, False)
            m97 = lambda first, last: (64, at(ta), at(full("i97")), at(m), first, last)
            cst = lambda lo, first: (192 - lo, at((pw, lo, 192)), at(full("two")), at(("cc", lo, 192)), first, False)
            R = [full(x) for x in ("i97", "n97", "two", "cc", "wu2")] + [wu, m]
            step, late = 8 if byv else 1, umv or ums
            head = [] if late else [cst(0, True), m97(False, False)] if byv else [m97(True, False), big("i97")]
            if not byv:
                head += feats(pw, 0, wu, zz, late, False, range(4), 1)
            k = pe(head, R + ([] if byv else [c_("zz", c, 0, 512)]), [u]) if head else None
            rest = feats(pw, 0, wu, zz, not head, False, range(8) if byv else range(4, 8), step)
            if late:
                rest += ([cst(128 if umv else 0, False)] if byv else []) + [m97(False, True)]
            else:
                rest += ([big("i97")] if byv else []) + [big("n97")] + feats(pw, 0, full("wu2"), zz, False, True, range(8), step)
            pe(rest, R + [zz], [u], cont=k)
            if umv:
                cp(c_("ui", c), u12)
                ts(c_("ac", c), c_("ui", c), 4095, A.bitwise_and)
                tt(c_("pp", c), c_("ac", c, 0, 64), c_("ac", c, 64, 128), A.mult)
            elif ums:
                sa(c_("ta", c), u12, F.Identity, bias=M12)
                sa(c_("tb", c), c_("ta", c), F.Identity, bias=-M12)
                tt(c_("cs", c), (pw, 256, 320), c_("tb", c, 64, 128), A.subtract)
                tt(ss, (pw, 192, 256), c_("tb", c, 0, 64), A.subtract)
                tt(c_("pp", c), ss, c_("cs", c), A.mult)
            else:
                un(c_("cs", c), (pw, 64, 128), 1.0, 0.0, (rd, c, st, "c"))
                tt(c_("pp", c), (pw, 0, 64), c_("cs", c), A.mult)
            ts(c_("kk", c), c_("pp", c), 5, A.arith_shift_right)
            tt(pad(xf), ta, c_("kk", c), A.add)
            tag = float((st + 1) << 18)
            ts(pad(tp), pad(xf), M13, A.add, M13 + tag, A.subtract)
            turn((pw, 384, 448), (fx, "ik"), (xf, "identf"), (tp, "nident"), cut=True)
            ts(c_("hl", c), (pw, 384, 448), HALF - tag, A.add, float(W), A.min)
            key = ("vp", c * 128 + 64, c * 128 + 128)
            if kt:
                parts = [(full("i8k"), m), (full("nident"), pad(tp))]
                calls = [(64, at(ky), at(l), at(x), k == 0, k == 1 and kt == 1) for k, (l, x) in enumerate(parts)]
                if kt == 2:
                    calls.append((256, at(ky), at(full("identf")), at(pad(xf)), False, True))
                pe(calls, [x for p in parts for x in p] + [pad(xf), full("identf")], [ky])
                if kt == 2:
                    key = ky
                else:
                    tt(key, ky, pad(xf), A.add)
            else:
                tt(ss, ky, pad(tp), A.subtract)
                tt(key, ss, pad(xf), A.add)
            if rd == 0 and c == 0:
                sa(full("act"), m, F.Sign)
                if st == 0:
                    tt(pad("xa"), key, full("act"), A.mult)
                else:
                    tt(("vp", 384, 448), key, full("act"), A.mult)
                    tt(pad("xa"), ("vp", 384, 448), pad("xa"), A.max)
            nf, d0, d1 = 64 - 8 * st, (pn, 384, 448), (pn, 448, 512)
            if (rd, c, st) in D_S:
                gather(lambda o, i: sa(o, mk, F.Copy, ind=i), (rd, c, st, "d"), dd, c_("hl", c))
                o, wq = (pn, 0, 8 * nf), (("wg", 64, 128), ("wg", 128, 184), ("wg", 64, 112))[st]
                k = pe(feats(pn, 0, wq, (rd, c), True, False) + ([(64, at(d0), at(full("nident")), at(n2), False, False)] if st == 1 else []),
                       [q, wq, full("nident"), n2], [o])
                pe(feats(pn, 0, ("wg", 0, nf), dd, False, True), [("wg", 0, nf), dd], [o], cont=k)
                sa(c_("da", c), (pn, 0, 384), F.Abs)
                ea = (pn, 0, 64)
                mm(ea, *[(full("ident"), c_("da", c, 64 * i, 64 * i + 64)) for i in range(6)])
            else:
                gather(lambda o, i, x: tt(o, mk, x, A.subtract, ind=i), (rd, c, st, "d"), dd, c_("hl", c), q)
                o, ea = (pn, 320, 512 - 64 * st), (pn, 256, 320)
                calls = feats(pn, 320, ("wd0", 0, 24 - 8 * st), dd, True, st == 2)
                if st == 0:
                    calls.append((128, at((pn, 384, 512)), at(full("ident")), at(c_(ra, c, 192, 320)), False, True))
                if st == 1:
                    calls += [(64, at(d0), at(full("nident")), at(n2), False, False), (64, at(d0), at(full("ident")), at(r(0)), False, True)]
                pe(calls, [full("ident"), full("nident"), c_(ra, c), full("wd0"), dd] + ([n2] if st == 1 else []), [o])
                sa(ea, (pn, 320, 384), F.Abs)
            tt(hit, ea, pad(fx), A.is_lt)
            if st < 2:
                tt(xm, d0, hit, A.mult)
                m = pad(mp)
                if (rd, c, st, "a") in A_V:
                    tt(m, xm, r(1) if st == 0 else n2, A.add)
                else:
                    x = (pn, 0, 64)
                    mm(x, (full("ident"), r(1) if st == 0 else n2), (full("ident"), xm))
                    sa(m, x, F.Copy)
            if st == 0:
                tt(d1, d1, hit, A.mult)
                tt(n2, d1, r(2), A.add)
                tt(kb, key, hit, A.mult)
            else:
                tt(ss, key, hit, A.mult)
                tt(kb, ss, kb, A.max)

    def learn(rd, c):
        nw = "nwa" if rd == 0 else "nwb"
        mk = ("mk0" if rd == 0 else "mk1", 0, W + 16)
        pn, pw, fx, xf = "pn%d" % c, "pw%d" % c, "fx%d" % c, "xf%d" % c
        xk, tp, mp = "xk%d" % c, "tp%d" % c, "mp%d" % c
        kb = pad(xk)
        cur[0] = "%d%d3" % (rd, c)
        ts(pad(tp), kb, M13, A.add, M13, A.subtract)
        turn((pn, 192, 256), (xk, "identf"), (tp, "nident"), cut=True)
        ts(c_("bl", c), (pn, 192, 256), HALF, A.add, float(W), A.min)

        def hv(n, h, w):
            x = c_(n, c)
            return (n, x[1] + w * h, x[1] + w * h + w, lambda T: T[n][:, x[1] + w * half(h):x[1] + w * half(h) + w], w)

        def qh_(h):
            return qv(rd, c)[:3] + (lambda T: ap(T, qv(rd, c, half(h))), 512)
        for h in (0, 1):
            if (rd, c, h) in L_V:
                tt(hv("ld", h, 512), mk, qh_(h), A.subtract, ind=c_("bl", c)[:3] + hv("bl", h, 32)[3:])
            else:
                sa(hv("ld", h, 512), mk, F.Copy, ind=c_("bl", c)[:3] + hv("bl", h, 32)[3:])
        ts(pad(mp), kb, M18, A.add, M18, A.subtract)
        bym = [(rd, c, h) in L_M and (rd, c, h) in L_V for h in (0, 1)]
        if any(bym):
            turn((pw, 128, 192), (tp, "ident"), (mp, "nident"))
            ts(c_("ml", c), (pw, 128, 192), 2.0 ** -13, A.mult)
        if not all(bym):
            o = (pw, 0, 128)
            pe([(128, at(o), win(tp, 0), at(full("ident")), True, False), (128, at(o), win(mp, 0), at(full("nident")), False, True)],
               [pad(tp), pad(mp), full("ident"), full("nident")], [o])
            sa(c_("fts", c), o, F.Exp, scale=-21 * LN2 / 8192, bias=60 * LN2)
        if rd == 1:
            blocks(c)
        for h, bank in ((0, pn), (1, pw)):
            o, qh, lh = (bank, 0, 512), qh_(h), hv("ld", h, 512)
            if bym[h]:
                tt(hv("zz", h, 512), full("th3"), lh, A.mult, ind=c_("ml", c)[:3] + hv("ml", h, 32)[3:])
                mm(o, (full("ident"), qh), (full("ident"), hv("zz", h, 512)))
                un(hv(nw, h, 512), o, 1.0, 0.0, (rd, c, h, "e"))
                continue
            calls = [(512, at(o), at(full("i75")), at(lh), True, False)]
            if (rd, c, h) not in L_V:
                calls.append((512, at(o), at(full("n75")), at(qh), False, False))
            for l in ("lp", "ln"):
                for jl in range(8):
                    calls.append((64, sl(bank, jl, 512, 8), at((l, 128 * jl, 128 * jl + 128)),
                                  at(hv("fts", h, 64)), False, False))
            calls.append((512, at(o), at(full("f75")), at(qh), False, True))
            pes(calls, [qh, lh, full("i75"), full("n75"), full("f75"), full("lp"), full("ln"), c_("fts", c)], [o])
            sa(hv(nw, h, 512), o, F.Relu, scale=2.0 ** 75, bias=-2.0 ** -10)

    def ropes():
        add("Y", 60, lambda g, T, e: g.sync.dma_start(T.ro1[:, :, :], T.ra[:, :]), [full("ra")], [("ro1", 0, 8)], sem="r1", inc=16,
            lat=2500)

        def f(g, T, e):
            core, rank, topo = e
            moves = []
            for s, en in single(T, topo, rank).items():
                ad = topo.addr(T.cores[s])
                moves.append(RemoteDMATransfer(dst_ids=[DstId(rid=ad[0], pnc=ad[1])], dma_engine_mask=1 << en,
                                               remote_sem=T.sem["arrr"], src=T.ro1[s], dst=T.ro2[rank]))
            return g.remote_dma_fused(moves, local_sem=T.sem["sntr"])
        i = add("G", 4000, f, [("ro1", 0, 8)], [], sem="noner", inc=0)
        first.append(i)
        j = add("arrr", 0, None, [], [], sem="arrr", inc=7, lat=12000, deps=(i,))
        k = add("Y", 60, lambda g, T, e: g.sync.dma_start(T.ro2[e[1]], T.ro1[e[1]]), [("ro1", 0, 8)], [], sem="r2", inc=16, lat=2500)
        add("Y", 60, lambda g, T, e: g.sync.dma_start(T.ra2[:, :], T.ro2[:, :, :]), [], [full("ra2")], sem="r3", inc=16, lat=2500,
            deps=(j, k))

    first = []

    def move(c):
        def f(g, T, e, h):
            core, rank, topo = e
            moves = []
            for s, en in lanes(T, topo, rank, half(h)).items():
                ad = topo.addr(T.cores[s])
                moves.append(RemoteDMATransfer(
                    dst_ids=[DstId(rid=ad[0], pnc=ad[1])], dma_engine_mask=sum(1 << x for x in en), remote_sem=T.sem["arr%d" % c],
                    src=T.nwa[:, c * CH + 128 * s:c * CH + 128 * s + 128],
                    dst=T.qb[:, c * CH + 128 * rank:c * CH + 128 * rank + 128]))
            return g.remote_dma_fused(moves, local_sem=T.sem["snt%d" % c])
        i = [add("G", 1000 if c or h else 1500, lambda g, T, e, h=h: f(g, T, e, h), [c_("nwa", c, 512 * h, 512 * h + 512)], [], sem="none%d%d" % (c, h), inc=0,
                 cont=first[0])
             for h in (0, 1)]
        add("arr%d" % c, 0, None, [], [c_("qb", c)], sem="arr%d" % c, inc=1, lat=5500, deps=i)

        def f2(g, T, e):
            a = c * CH + 128 * e[1]
            return g.sync.dma_start(T.qb[:, a:a + 128], T.nwa[:, a:a + 128])
        k = add("Y", 60, f2, [c_("nwa", c, 512, CH)], [], sem="slf%d" % c, inc=16, lat=2500)
        acc["qb"].append((k, "Y", c * CH, c * CH + CH, True))

    def edits():
        a8 = lambda n, k: (n, 8 * k, 8 * k + 8)
        bl = ("bl", 0, 8)
        turn(("pe", 256, 264), ("xa", "identf"))
        turn(("pe", 264, 272), ("xk0", "identf"))
        ts(full("k2"), ("pe", 256, 272), HALF, A.add)
        ts(full("fb"), full("k2"), W - 1, A.bitwise_and)
        ts(a8("mfi", 0), a8("k2", 0), 13, A.arith_shift_right, 15, A.bitwise_and)
        ts(a8("mfi", 1), a8("k2", 1), 18, A.arith_shift_right)
        cp(full("mfl"), full("mfi"))
        tt(full("ed1"), a8("k2", 0), a8("k2", 1), A.is_gt)
        ts(full("ed0"), a8("k2", 1), 8192.0, A.is_gt)
        for k in (0, 1):
            tt(a8("ed", k), full("ed1"), full("ed0"), A.mult)
        ts(full("fbm"), full("fb"), -8193.0, A.add)
        tt(full("fbe"), full("fbm"), full("ed"), A.mult)
        ts(full("flu"), full("fbe"), 8193.0, A.add)
        sa(full("nb"), full("fbe"), F.Identity, scale=-256.0, bias=-256.0 * 8193)
        tt(full("krow"), full("iot"), full("trow"), A.add, ind=full("flu"))
        for k in range(16):
            h, n = 128 * (k // 8), 16 * (k % 8 + 1)
            sa(("dk", 128 * k, 128 * k + n), ("krow", h, h + n), F.Identity, bias=("nb", k, k + 1))
            add("V", vdur(n), lambda g, T, e, k=k, n=n: g.vector.tensor_reduce(
                T.first[:, k:k + 1], T.dk[:, 128 * k:128 * k + n], AxisListType.X, A.min, apply_absolute_value=True),
                [("dk", 128 * k, 128 * k + n)], [("first", k, k + 1)])
        tt(full("gg"), full("fbe"), full("t16b"), A.subtract)
        tt(full("win"), full("first"), full("t16"), A.is_equal)
        tt(full("gg"), full("gg"), full("win"), A.mult)
        tt(full("tgt"), full("gg"), full("dump16"), A.add)
        cp(full("tgu"), full("tgt"))
        sa(full("g0"), ("mk0", 0, W + 16), F.Copy, ind=bl)
        tt(full("ga1"), full("sel1"), full("g0"), A.mult, ind=a8("mfl", 1))
        tt(full("ga2"), full("sel2"), full("g0"), A.mult, ind=a8("mfl", 1))
        mm(("pe", 0, 128), (full("sh1"), full("ga1")), (full("sh2"), full("ga2")), (full("isym"), ("qa", 0, 128)))
        sa(full("wnew"), ("pe", 0, 128), F.Copy)
        scat(full("mk1"), ("tgu", 0, 8), full("wnew"))
        sa(full("g1"), ("mk1", 0, W + 16), F.Copy, ind=bl)
        sa(full("mfw"), full("mt"), F.Copy, ind=a8("mfl", 0))
        mm(("pe", 0, 128), (full("spl"), full("g1")), (full("ident"), full("mfw")))
        sa(full("snew"), ("pe", 0, 128), F.Copy)
        scat(full("mk1"), ("tgu", 8, 16), full("snew"))

    def blocks(c):
        v, x = ("pn%d" % c, 192, 256), ("vp", c * 128 + 64, c * 128 + 128)
        ts(c_("ybx", c), v, 0.0, A.is_equal, -HALF - 1.0, A.mult)
        tt(c_("cs", c), v, c_("ybx", c), A.add)
        un(("yby", 64 * c, 64 * c + 64, lambda T: T.yby[:, :, 8 * c:8 * c + 8], 64), c_("cs", c), 1.0, HALF, (1, c, 0, "b"))
        if c == NC - 1:
            add("Y", 60, lambda g, T, e: g.sync.dma_start(T.yb[:, :], T.yby[:, :, :]),
                [("yby", 0, 192)], [], sem="lyb", inc=16, lat=2500)

    def store(c):
        for s in range(8):
            q = "S" if c == NC - 1 and s >= 6 else "Y"
            a = c * CH + 128 * s

            def f(g, T, e, s=s, q=q):
                x = 4 * half(s // 4) + s % 4
                return (g.sync if q == "Y" else g.scalar).dma_start(
                    T.yq[:, 384 * x + 128 * c:384 * x + 128 * c + 128], T.nwb[:, c * CH + 128 * x:c * CH + 128 * x + 128])
            add(q, 60, f, [("nwb", a, a + 128)], [], sem="out%d" % c, inc=16, lat=2500)

    cur[0] = "l"
    learn_constants()
    for c in range(NC):
        search(0, c)
    cur[0] = "r"
    ropes()
    for c in range(NC):
        learn(0, c)
        move(c)
    cur[0] = "k"
    edit_constants()
    cur[0] = "e"
    edits()
    for c in range(NC):
        search(1, c)
        learn(1, c)
        store(c)
    return ops


QSEM = {"T": "sT", "V": "sV", "S": "sS", "G": "sG"}


def schedule(ops):
    n = len(ops)
    kids = [[] for _ in range(n)]
    need = [len(o["deps"]) for o in ops]
    for i, o in enumerate(ops):
        for d in o["deps"]:
            kids[d].append(i)
    tail = [0.0] * n
    for i in range(n - 1, -1, -1):
        tail[i] = ops[i]["dur"] + ops[i]["lat"] + max([tail[k] + WAKE for k in kids[i]] or [0.0])
    prio = [tail[i] + ops[i]["pr"] + BIAS.get(ops[i]["tag"], 0.0) for i in range(n)]
    free, ready, est, done = {}, {}, [0.0] * n, [0.0] * n
    for i in range(n):
        ready.setdefault(ops[i]["q"], [])
        free[ops[i]["q"]] = 0.0
        if need[i] == 0:
            ready[ops[i]["q"]].append(i)
    order = []
    for _ in range(n):
        best = None
        for q, lst in ready.items():
            if lst:
                t = max(free[q], min(est[i] for i in lst))
                if best is None or t < best[0]:
                    best = (t, q)
        t, q = best
        i = max((i for i in ready[q] if est[i] <= t), key=lambda i: (prio[i], -i))
        ready[q].remove(i)
        free[q] = t + ops[i]["dur"]
        done[i] = free[q] + ops[i]["lat"]
        order.append(i)
        for k in kids[i]:
            est[k] = max(est[k], done[i] + (0.0 if i in ops[k]["soft"] else WAKE))
            need[k] -= 1
            if need[k] == 0:
                ready[ops[k]["q"]].append(k)
    return order, max(done), done


def plan(ops):
    order = [(ord(ORDER[k]) - 48) * 40 + ord(ORDER[k + 1]) - 48 for k in range(0, len(ORDER), 2)]
    seen = set()
    for i in order:
        if i >= len(ops) or not ops[i]["deps"] <= seen:
            break
        seen.add(i)
    return order if len(seen) == len(ops) == len(order) else schedule(ops)[0]


PLAN = {}


def rank_program(g, core, T, topo):
    rank = T.rank_of(core)
    if rank is None:
        return
    if not PLAN:
        PLAN["ops"] = graph()
        PLAN["order"] = plan(PLAN["ops"])
    ops, order = PLAN["ops"], PLAN["order"]
    env = (core, rank, topo)
    eng = {"T": g.tensor, "V": g.vector, "S": g.scalar, "G": g, "Y": g.sync}
    total = {}
    for o in ops:
        if o["sem"] and o["inc"]:
            total[o["sem"]] = total.get(o["sem"], 0) + o["inc"]
    for c in range(NC):
        total["arr%d" % c] = sum(len(lanes(T, topo, s, rank // 4)[rank]) for s in range(8) if s != rank)
        total["snt%d" % c] = sum(len(en) for h in (0, 1) for en in lanes(T, topo, rank, h).values())
    total["sntr"] = 7
    RANK[0] = rank
    count, stamp, clock, known = {}, {}, {}, {}
    for i in order:
        o = ops[i]
        q = o["q"]
        kn = known.setdefault(q, {})
        want = {}
        for d in o["deps"]:
            if d in o["soft"]:
                continue
            s, v = stamp[d]
            if kn.get(s, 0) < v:
                want[s] = max(want.get(s, 0), v)
        for s in sorted(want, key=lambda s: -len(clock[(s, want[s])])):
            v = want[s]
            if kn.get(s, 0) >= v:
                continue
            if o["fn"] is not None and not s.startswith("none"):
                eng[q].wait_ge(T.sem[s], v)
            kn[s] = max(kn.get(s, 0), v)
            for s2, v2 in clock[(s, v)].items():
                kn[s2] = max(kn.get(s2, 0), v2)
        ins = o["fn"](g, T, env) if o["fn"] is not None else None
        if o["sem"] is None:
            s = QSEM[q]
            count[s] = count.get(s, 0) + 1
            ins.then_inc(T.sem[s], 1)
            v = count[s]
            prev = clock.get((s, v - 1), {})
        else:
            s = o["sem"]
            v = total.get(s, 1)
            if ins is not None and o["inc"]:
                ins.then_inc(T.sem[s], o["inc"])
            prev = clock.get((s, v), {})
        stamp[i] = (s, v)
        ck = {}
        if not s.startswith("arr"):
            ck = dict(prev)
            for s2, v2 in kn.items():
                ck[s2] = max(ck.get(s2, 0), v2)
        clock[(s, v)] = ck
    for s in SEMAPHORES:
        if s in count:
            g.wait_ge(T.sem[s], count[s])
        else:
            g.wait_ge(T.sem[s], total[s])
